import numpy as np
import ml_dtypes


def mxq(x, axis, fmt="e4m3"):
    dtype, down = {"e4m3": (ml_dtypes.float8_e4m3fn, 7), "e5m2": (ml_dtypes.float8_e5m2, 14)}[fmt]
    v = np.moveaxis(np.asarray(x, np.float32).astype(ml_dtypes.bfloat16).astype(np.float64), axis, -1)
    blocks = v.reshape(v.shape[:-1] + (-1, 32))
    amax = np.abs(blocks).max(-1, keepdims=True)
    byte = np.maximum(np.where(amax > 0, np.frexp(amax)[1] - 1 + 127, 0) - down, 1)
    scale = np.exp2(byte - 127.0)
    codes = (blocks / scale).astype(np.float32).astype(dtype).astype(np.float64)
    return np.moveaxis((codes * scale).reshape(v.shape), -1, axis)


WIDE = False


def mx_kscale(k):
    if not WIDE:
        return np.ones(k)
    levels = np.array([10, -10, 5, -5, 0])
    if k % 512:
        return np.exp2(np.random.permutation(np.resize(levels, k // 32))).repeat(32)
    a = np.empty((k // 512, 16))
    for p in range(k // 512):
        a[p, :8] = np.random.permutation(np.resize(levels, 8))
        for g in range(8):
            far = levels[np.abs(levels - a[p, g]) >= 10]
            a[p, g + 8] = far[np.random.randint(len(far))]
    return np.exp2(a.ravel()).repeat(32)


BF16 = ml_dtypes.bfloat16


def bf(x):
    return np.asarray(x, np.float32).astype(BF16)


def f64(x):
    return np.asarray(x).astype(np.float64)


E2M1 = np.array([0.0, 0.5, 1.0, 1.5, 2.0, 3.0, 4.0, 6.0, -0.0, -0.5, -1.0, -1.5, -2.0, -3.0, -4.0, -6.0])


def pack_weight(w, fmt):
    k, n = w.shape
    w = f64(bf(w)).reshape(k // 32, 32, n)
    amax = np.abs(w).max(1)
    if fmt == "e4m3":
        byte = np.frexp(amax)[1] - 1 + 127 - 7
    else:
        mant, ex = np.frexp(amax / 6.0)
        byte = np.where(mant > 0.5, ex, ex - 1) + 127
    byte = np.clip(np.where(amax > 0, byte, 1), 1, 254)
    scaled = (w * np.exp2(127.0 - byte)[:, None, :]).reshape(k, n).astype(np.float32)
    by_word = np.ascontiguousarray(scaled.reshape(k // 512, 128, 4, n).transpose(0, 1, 3, 2))
    if fmt == "e4m3":
        words = by_word.astype(ml_dtypes.float8_e4m3fn).view(np.uint8)
    else:
        c = by_word.astype(ml_dtypes.float4_e2m1fn).view(np.uint8) & 0xF
        words = c[..., 0::2] | (c[..., 1::2] << 4)
    return np.ascontiguousarray(words), np.ascontiguousarray(byte.astype(np.uint8).reshape(k // 512, 16, n))


def unpack_weight(words, scales, fmt):
    g, p, n, _ = words.shape
    if fmt == "e4m3":
        vals = np.ascontiguousarray(words).view(ml_dtypes.float8_e4m3fn).astype(np.float64)
    else:
        nib = np.empty((g, p, n, 4), np.uint8)
        nib[..., 0::2] = words & 0xF
        nib[..., 1::2] = words >> 4
        vals = E2M1[nib]
    vals = vals * np.repeat(np.exp2(scales.astype(np.float64) - 127.0), 8, axis=1)[..., None]
    return vals.transpose(0, 1, 3, 2).reshape(g * 512, n)
def pack4(w):
    words, scales = pack_weight(w, "e2m1")
    return words.reshape(words.shape[0], 128, -1), scales


def unpack4(words, scales):
    return unpack_weight(words.reshape(words.shape[0], 128, -1, 2), scales, "e2m1")


M, N = 1536, 1024
C_EYE, C_ZY = 1.5, 0.5


def draw0():
    s, t = mx_kscale(N), mx_kscale(N)
    y = np.eye(N) + np.random.standard_normal((N, N)) / np.sqrt(N)
    zt = np.eye(N) + np.random.standard_normal((N, N)) / np.sqrt(N)
    z_words, z_scales = pack4(zt / s[:, None] / t)
    return {"x": bf(np.random.standard_normal((M, N)) / s),
            "y": bf(y * s[:, None] * t),
            "z_words": z_words,
            "z_scales": z_scales,
            "gain": bf((1 + 0.1 * np.random.standard_normal(N)) / t)}


def core(x, y, z_words, z_scales, gain):
    zt = unpack4(z_words, z_scales)
    yq = mxq(f64(y), 0, "e4m3")
    v = mxq(f64(x), 1, "e4m3") @ yq
    zy = zt.T @ yq
    c = C_EYE * np.eye(N) - C_ZY * zy
    return (mxq(v, 1, "e4m3") @ mxq(c, 0, "e4m3")) * f64(gain)


def e4m3fn_bytes(y):
    return np.clip(np.asarray(y, np.float64), -448.0, 448.0).astype(np.float32).astype(ml_dtypes.float8_e4m3fn).view(np.uint8)


def e4m3fn_values(b):
    return np.asarray(b, np.uint8).view(ml_dtypes.float8_e4m3fn).astype(np.float64)


def setup_inputs():
    d = draw0()
    x0 = np.asarray(d['x']).astype(np.float64)
    s = (np.max(np.abs(x0), axis=(0,), keepdims=True) / 448.0).astype(np.float32)
    out = {}
    for k, v in d.items():
        if k == 'x':
            out['x_bytes'] = e4m3fn_bytes(x0 / s.astype(np.float64))
            out['x_scale'] = s
        else:
            out[k] = v
    return out


def reference(x_bytes, x_scale, y, z_words, z_scales, gain):
    return core(e4m3fn_values(x_bytes) * x_scale.astype(np.float64), y, z_words, z_scales, gain)

@@ -1,0 +1,539 @@
+from contextlib import ExitStack
+
+import concourse.mybir as mybir
+from concourse.masks import make_identity
+
+M, N = 1536, 1024
+FLOPS = 2 * N * N * (2 * M + N)
+
+F32 = mybir.dt.float32
+BF16 = mybir.dt.bfloat16
+I32 = mybir.dt.int32
+U32 = mybir.dt.uint32
+U8 = mybir.dt.uint8
+FP8 = mybir.dt.float8_e4m3fn
+FP8X4 = mybir.dt.float8_e4m3fn_x4
+FP4X4 = mybir.dt.float4_e2m1fn_x4
+MULT = mybir.AluOpType.mult
+ADD = mybir.AluOpType.add
+COPY = mybir.ActivationFunctionType.Copy
+
+P = 128
+TILES = M // P
+PAIRS = TILES // 2
+
+
+def tile_coupled_newton_colouring_step_s11_kernel(tc, x_bytes, x_scale, y, z_words, z_scales, gain, out):
+    nc = tc.nc
+    with ExitStack() as ctx:
+        keep = ctx.enter_context(tc.tile_pool(name="keep", bufs=1))
+        work = ctx.enter_context(tc.tile_pool(name="work", bufs=3))
+        psum = ctx.enter_context(tc.psum_pool(name="psum", bufs=2))
+        ctx.enter_context(tc.manual_schedule())
+
+        xs_col = keep.tile([P, 8], F32, name="xs_col")
+        nc.sync.dma_start(out=xs_col[:], in_=x_scale.rearrange("o (p j) -> p (o j)", j=8))
+        zs_raw = keep.tile([P, 2, N], U8, name="zs_raw", align_bytes=64)
+        nc.vector.memset(zs_raw[:].rearrange("p g n -> p (g n)").bitcast(I32), 0)
+        for q in range(4):
+            nc.sync.dma_start(
+                out=zs_raw[32 * q : 32 * q + 4, :, :].bitcast(I32),
+                in_=z_scales[:, 4 * q : 4 * q + 4, :].bitcast(I32).rearrange("g r n -> r g n"),
+            )
+        y_view = y.rearrange("(g p j) n -> g p j n", p=P, j=4)
+        y_raw = {}
+        zw_raw = keep.tile([P, 2, 2 * N], U8, name="zw_raw", align_bytes=64)
+        xb = []
+
+        def load_y(kp, h):
+            t = keep.tile([P, 4, 512], BF16, name=f"y_raw_{kp}{h}", align_bytes=64)
+            nc.sync.dma_start(out=t[:], in_=y_view[kp][:, :, 512 * h : 512 * h + 512])
+            y_raw[kp, h] = t
+
+        x_view = x_bytes.rearrange("(i s p) k -> i p s k", s=2, p=P)
+
+        def load_x(pair):
+            t = keep.tile([P, 2, N], U8, name=f"xb_{pair}", align_bytes=64)
+            nc.sync.dma_start(out=t[:], in_=x_view[pair])
+            xb.append(t)
+
+        def load_z(g):
+            for kp in range(2):
+                nc.sync.dma_start(
+                    out=zw_raw[:, kp, N * g : N * g + N].bitcast(I32), in_=z_words[kp][:, N * g : N * g + N].bitcast(I32)
+                )
+
+        load_x(0)
+        load_z(0)
+        load_y(0, 0)
+        load_y(1, 0)
+        load_z(1)
+        load_x(1)
+        load_y(0, 1)
+        load_y(1, 1)
+        for pair in range(2, PAIRS):
+            load_x(pair)
+        gain_bc = keep.tile([P, N], BF16, name="gain_bc", align_bytes=64)
+        nc.sync.dma_start(out=gain_bc[:], in_=gain.partition_broadcast(P))
+
+        ident = keep.tile([P, P], F32, name="ident", align_bytes=64)
+        make_identity(nc, ident[:])
+        eye15 = keep.tile([P, P], F32, name="eye15", align_bytes=64)
+        nc.gpsimd.tensor_scalar(out=eye15[:], in0=ident[:], scalar1=1.5, scalar2=0.0, op0=MULT, op1=ADD)
+
+        xsb = keep.tile([P, N], F32, name="xsb", align_bytes=64)
+        for half in range(2):
+            ps = psum.tile([P, 4, P], F32, name="xt", tag="xt", bufs=2)
+            for j in range(4):
+                nc.tensor.transpose(ps[:, j, :], xs_col[:, 4 * half + j : 4 * half + j + 1].to_broadcast([P, P]), ident[:])
+            copy = nc.vector.tensor_copy if half else nc.scalar.copy
+            copy(
+                out=xsb[:].rearrange("p (c j) -> p c j", j=8)[:, :, 4 * half : 4 * half + 4],
+                in_=ps[:].rearrange("p j c -> p c j"),
+            )
+
+        yq = keep.tile([P, 2, N], U32, name="yq", align_bytes=64)
+        ys = keep.tile([P, 2, N], U8, name="ys", align_bytes=64)
+        zq = keep.tile([P, 2, 2 * N], U8, name="zq", align_bytes=64)
+        zs = keep.tile([P, 2, N], U8, name="zs", align_bytes=64)
+        cq = keep.tile([P, 2, N], U32, name="cq", align_bytes=64)
+        cs = keep.tile([P, 2, N], U8, name="cs", align_bytes=64)
+        yi = {}
+        ci = {}
+
+        def y_lay(kp, h, t, copy):
+            if (kp, h) not in yi:
+                yi[kp, h] = keep.tile([P, 512, 4], BF16, name=f"yi_{kp}{h}", align_bytes=64)
+            dst = yi[kp, h][:].rearrange("p (t q r) j -> p t q r j", t=4, r=8)
+            raw = y_raw[kp, h][:].rearrange("p j (q t r) -> p t q r j", t=4, r=8)
+            copy(out=dst[:, t], in_=raw[:, t])
+
+        def y_quant(kp, h, t0, nt):
+            lo, hi = 128 * t0, 128 * (t0 + nt)
+            nc.vector.quantize_mx(
+                out=yq[:, kp, 512 * h + lo : 512 * h + hi].bitcast(FP8X4),
+                scales=ys[:, kp, 512 * h + lo : 512 * h + hi],
+                in_=yi[kp, h][:, lo:hi].rearrange("p n j -> p (n j)"),
+            )
+
+        def z_lay(g):
+            for kp in range(2):
+                nc.vector.tensor_copy(
+                    out=zq[:, kp, N * g : N * g + N].bitcast(I32).rearrange("p (t q r) -> p t q r", t=4, r=4),
+                    in_=zw_raw[:, kp, N * g : N * g + N].bitcast(I32).rearrange("p (q t r) -> p t q r", t=4, r=4),
+                )
+                nc.vector.tensor_copy(
+                    out=zs[:, kp, 512 * g : 512 * g + 512].bitcast(I32).rearrange("p (t q r) -> p t q r", t=4, r=2),
+                    in_=zs_raw[:, kp, 512 * g : 512 * g + 512].bitcast(I32).rearrange("p (q t r) -> p t q r", t=4, r=2),
+                )
+
+        xw, xt, xi, xq, xqs = {}, {}, {}, {}, {}
+
+        def widen(i):
+            if i >= TILES:
+                return
+            xw[i] = work.tile([P, N], BF16, name="xw", tag="xw", bufs=6, align_bytes=64)
+            nc.vector.tensor_tensor(out=xw[i][:], in0=xb[i // 2][:, i % 2, :].bitcast(FP8), in1=xsb[:], op=MULT)
+
+        xp = {}
+
+        def x_perm(i):
+            if i >= TILES:
+                return
+            xp[i] = work.tile([P, 2, 2, P], F32, name="xp", tag="xp", bufs=6, align_bytes=64)
+            nc.scalar.copy(out=xp[i][:], in_=xw[i][:].bitcast(F32).rearrange("p (g n u) -> p g u n", g=2, u=2))
+
+        def turn(i):
+            if i >= TILES:
+                return
+            perm = i in xp
+            words = xp[i][:].rearrange("p g u n -> p (g u n)") if perm else xw[i][:].bitcast(F32)
+            xt[i] = psum.tile([P, 2, 2, P], F32, name="xt", tag="xt", bufs=2)
+            for g in range(2):
+                for u in range(2):
+                    nc.tensor.transpose(xt[i][:, g, u, :], words[:, 256 * g + 128 * u : 256 * g + 128 * u + 128] if perm else words[:, 256 * g + u : 256 * (g + 1) : 2], ident[:])
+
+        def x_out(i):
+            if i >= TILES:
+                return
+            xi[i] = work.tile([P, 2, P, 4], BF16, name="xi", tag="xi", bufs=4, align_bytes=64)
+            nc.scalar.copy(
+                out=xi[i][:].rearrange("p g m t -> p (g m t)").bitcast(F32).rearrange("p (g m u) -> p g m u", g=2, u=2),
+                in_=xt[i][:].rearrange("p g u m -> p g m u"),
+            )
+
+        def x_quant(i):
+            if i >= TILES:
+                return
+            xq[i] = work.tile([P, 2 * P], U32, name="xq", tag="xq", bufs=6, align_bytes=64)
+            xqs[i] = work.tile([P, 2 * P], U8, name="xqs", tag="xqs", bufs=6, align_bytes=64)
+            nc.vector.quantize_mx(
+                out=xq[i][:].bitcast(FP8X4), scales=xqs[i][:], in_=xi[i][:].rearrange("p g m t -> p (g m t)")
+            )
+
+        zps = {}
+
+        def zy(h, t1, g):
+            ps = psum.tile([P, 4, P], F32, name="mm", tag="mm", bufs=3)
+            cols = slice(512 * h + 128 * t1, 512 * h + 128 * t1 + 128)
+            for t in range(4):
+                c0 = 512 * g + 128 * t
+                for kp in range(2):
+                    nc.tensor.matmul_mx(
+                        out=ps[:, t, :],
+                        lhsT=zq[:, kp, 2 * c0 : 2 * c0 + 256].bitcast(FP4X4),
+                        lhsT_scale=zs[:, kp, c0 : c0 + 128],
+                        rhs=yq[:, kp, cols].bitcast(FP8X4),
+                        rhs_scale=ys[:, kp, cols],
+                        start=(kp == 0),
+                        stop=(kp == 1),
+                    )
+            zps[h, t1, g] = ps
+
+        dblk = {}
+
+        def d_out(h, t1, g):
+            dblk[h, t1] = work.tile([P, P], F32, name="dblk", tag="dblk", bufs=8, align_bytes=64)
+            nc.scalar.activation(out=dblk[h, t1][:], in_=zps[h, t1, g][:, t1, :], func=COPY, scale=-0.5)
+
+        def d_add(h, t1, g):
+            dst = ci[g, h][:].rearrange("p (q t r) f -> p t q r f", t=4, r=8)[:, t1, :, :, t1]
+            nc.gpsimd.tensor_tensor(
+                out=dst,
+                in0=dblk[h, t1][:].rearrange("p (q r) -> p q r", r=8),
+                in1=eye15[:].rearrange("p (q r) -> p q r", r=8),
+                op=ADD,
+            )
+
+        def c_out(h, t1, g, eng):
+            if (g, h) not in ci:
+                ci[g, h] = keep.tile([P, 512, 4], BF16, name=f"ci_{g}{h}", align_bytes=64)
+            src = zps[h, t1, g][:].rearrange("p f (q r) -> p q r f", r=8)
+            dst = ci[g, h][:].rearrange("p (q t r) f -> p t q r f", t=4, r=8)[:, t1]
+            if eng == "V":
+                nc.vector.tensor_scalar(out=dst, in0=src, scalar1=-0.5, scalar2=None, op0=MULT)
+            else:
+                nc.scalar.activation(out=dst, in_=src, func=COPY, scale=-0.5)
+
+        def c_quant(g, h):
+            nc.vector.quantize_mx(
+                out=cq[:, g, 512 * h : 512 * h + 512].bitcast(FP8X4),
+                scales=cs[:, g, 512 * h : 512 * h + 512],
+                in_=ci[g, h][:].rearrange("p n f -> p (n f)"),
+            )
+
+        vps, vi, vq, vqs = {}, {}, {}, {}
+
+        def v_mm(i, gs=(0, 1)):
+            for g in gs:
+                ps = psum.tile([P, 4, P], F32, name="mm", tag="mm", bufs=3)
+                for t in range(4):
+                    c0 = 512 * g + 128 * t
+                    for kp in range(2):
+                        nc.tensor.matmul_mx(
+                            out=ps[:, t, :],
+                            lhsT=yq[:, kp, c0 : c0 + 128].bitcast(FP8X4),
+                            lhsT_scale=ys[:, kp, c0 : c0 + 128],
+                            rhs=xq[i][:, P * kp : P * kp + P].bitcast(FP8X4),
+                            rhs_scale=xqs[i][:, P * kp : P * kp + P],
+                            start=(kp == 0),
+                            stop=(kp == 1),
+                        )
+                vps[i, g] = ps
+
+        def v_out(i, gs=(0, 1)):
+            if i not in vi:
+                vi[i] = work.tile([P, 2, P, 4], BF16, name="vi", tag="vi", bufs=4, align_bytes=64)
+            for g in gs:
+                nc.scalar.copy(out=vi[i][:, g], in_=vps[i, g][:].rearrange("p t m -> p m t"))
+
+        def v_quant(i):
+            vq[i] = work.tile([P, 2 * P], U32, name="vq", tag="vq", bufs=3, align_bytes=64)
+            vqs[i] = work.tile([P, 2 * P], U8, name="vqs", tag="vqs", bufs=3, align_bytes=64)
+            parts = [(0, 1), (1, 2)] if i == TILES - 1 else [(0, 2)]
+            for g0, g1 in parts:
+                nc.vector.quantize_mx(
+                    out=vq[i][:, P * g0 : P * g1].bitcast(FP8X4),
+                    scales=vqs[i][:, P * g0 : P * g1],
+                    in_=vi[i][:, g0:g1].rearrange("p g m t -> p (g m t)"),
+                )
+
+        ops = {}
+
+        def o_mm(i, hs=(0, 1)):
+            for h in hs:
+                ps = psum.tile([P, 512], F32, name="ops", tag="ops", bufs=3)
+                for g in range(2):
+                    nc.tensor.matmul_mx(
+                        out=ps[:],
+                        lhsT=vq[i][:, P * g : P * g + P].bitcast(FP8X4),
+                        lhsT_scale=vqs[i][:, P * g : P * g + P],
+                        rhs=cq[:, g, 512 * h : 512 * h + 512].bitcast(FP8X4),
+                        rhs_scale=cs[:, g, 512 * h : 512 * h + 512],
+                        start=(g == 0),
+                        stop=(g == 1),
+                    )
+                ops[i, h] = ps
+
+        out_view = out.rearrange("(i p) n -> i p n", p=P)
+
+        ot = {}
+
+        def o_out(i, hs=(0, 1)):
+            if i not in ot:
+                ot[i] = work.tile([P, N], F32, name="ot", tag="ot", bufs=4, align_bytes=64)
+            width = 256 if i == TILES - 1 else 512
+            for h in hs:
+                for c0 in range(0, 512, width):
+                    c = slice(512 * h + c0, 512 * h + c0 + width)
+                    nc.vector.tensor_tensor(out=ot[i][:, c], in0=ops[i, h][:, c0 : c0 + width], in1=gain_bc[:, c], op=MULT)
+                    if i == TILES - 1:
+                        nc.sync.dma_start(out=out_view[i][:, c], in_=ot[i][:, c])
+                if h == 1 and i < TILES - 1:
+                    nc.sync.dma_start(out=out_view[i], in_=ot[i][:])
+
+        V, S = nc.vector.tensor_copy, nc.scalar.copy
+        widen(1)
+        widen(0)
+        y_lay(0, 0, 3, S)
+        y_lay(0, 0, 1, V)
+        z_lay(0)
+        turn(1)
+        y_lay(0, 0, 0, S)
+        turn(0)
+        y_lay(1, 0, 0, V)
+        y_lay(1, 0, 1, V)
+        y_lay(0, 0, 2, V)
+        y_lay(1, 0, 3, S)
+        y_quant(1, 0, 0, 1)
+        y_quant(0, 0, 0, 1)
+        x_out(1)
+        y_quant(1, 0, 1, 1)
+        zy(0, 0, 0)
+        y_lay(1, 0, 2, S)
+        y_quant(0, 0, 1, 1)
+        x_out(0)
+        z_lay(1)
+        y_quant(1, 0, 2, 2)
+        zy(0, 1, 0)
+        y_lay(0, 1, 0, V)
+        d_out(0, 0, 0)
+        zy(0, 1, 1)
+        x_quant(0)
+        c_out(0, 0, 0, "S")
+        d_out(0, 1, 0)
+        c_out(0, 1, 0, "S")
+        zy(0, 0, 1)
+        y_lay(1, 1, 1, V)
+        c_out(0, 1, 1, "S")
+        y_quant(0, 0, 2, 2)
+        y_lay(0, 1, 3, V)
+        x_quant(1)
+        zy(0, 3, 0)
+        y_lay(1, 1, 3, S)
+        c_out(0, 0, 1, "S")
+        zy(0, 2, 1)
+        y_lay(0, 1, 2, V)
+        widen(2)
+        d_out(0, 3, 0)
+        c_out(0, 3, 0, "S")
+        y_lay(0, 1, 1, V)
+        c_out(0, 2, 1, "S")
+        y_lay(1, 1, 0, V)
+        zy(0, 2, 0)
+        y_lay(1, 1, 2, V)
+        d_out(0, 2, 0)
+        v_mm(0, (0,))
+        y_quant(0, 1, 0, 4)
+        c_out(0, 2, 0, "S")
+        v_mm(1, (0,))
+        v_out(0, (0,))
+        v_out(1, (0,))
+        zy(0, 3, 1)
+        y_quant(1, 1, 0, 4)
+        x_perm(2)
+        zy(1, 3, 0)
+        c_out(1, 3, 0, "S")
+        c_out(0, 3, 1, "V")
+        zy(1, 0, 1)
+        d_add(0, 1, 0)
+        d_add(0, 0, 0)
+        d_out(1, 0, 1)
+        widen(3)
+        c_out(1, 0, 1, "S")
+        c_quant(1, 0)
+        v_mm(0, (1,))
+        d_add(0, 2, 0)
+        v_out(0, (1,))
+        zy(1, 1, 0)
+        x_perm(3)
+        zy(1, 0, 0)
+        zy(1, 2, 0)
+        c_out(1, 1, 0, "V")
+        turn(2)
+        d_add(0, 3, 0)
+        c_out(1, 0, 0, "S")
+        turn(3)
+        c_out(1, 2, 0, "S")
+        v_mm(1, (1,))
+        v_quant(0)
+        c_quant(0, 0)
+        widen(4)
+        c_quant(0, 1)
+        x_out(2)
+        zy(1, 2, 1)
+        v_out(1, (1,))
+        zy(1, 1, 1)
+        widen(5)
+        d_out(1, 2, 1)
+        v_quant(1)
+        zy(1, 3, 1)
+        x_quant(2)
+        x_out(3)
+        o_mm(0, (0,))
+        c_out(1, 2, 1, "S")
+        o_mm(1, (0,))
+        d_out(1, 1, 1)
+        d_add(1, 2, 1)
+        c_out(1, 1, 1, "V")
+        d_out(1, 3, 1)
+        v_mm(2, (1,))
+        c_out(1, 3, 1, "S")
+        v_mm(2, (0,))
+        o_out(0, (0,))
+        d_add(1, 0, 1)
+        o_out(1, (0,))
+        d_add(1, 1, 1)
+        d_add(1, 3, 1)
+        x_perm(5)
+        x_perm(4)
+        v_out(2, (0,))
+        x_quant(3)
+        c_quant(1, 1)
+        turn(5)
+        turn(4)
+        widen(6)
+        v_out(2, (1,))
+        x_out(5)
+        x_out(4)
+        o_mm(1, (1,))
+        v_quant(2)
+        o_out(1, (1,))
+        o_mm(0, (1,))
+        x_perm(6)
+        x_quant(5)
+        o_out(0, (1,))
+        x_quant(4)
+        v_mm(3, (0,))
+        v_mm(3, (1,))
+        v_out(3, (0,))
+        v_out(3, (1,))
+        widen(7)
+        o_mm(2, (0,))
+        o_mm(2, (1,))
+        v_quant(3)
+        x_perm(7)
+        o_out(2, (0,))
+        o_out(2, (1,))
+        v_mm(4, (0,))
+        v_mm(4, (1,))
+        v_out(4, (0,))
+        v_out(4, (1,))
+        widen(8)
+        o_mm(3, (0,))
+        o_mm(3, (1,))
+        v_quant(4)
+        o_out(3, (0,))
+        o_out(3, (1,))
+        turn(6)
+        turn(7)
+        x_out(6)
+        x_out(7)
+        x_perm(8)
+        x_quant(6)
+        x_quant(7)
+        v_mm(5, (0,))
+        v_mm(5, (1,))
+        v_out(5, (0,))
+        v_out(5, (1,))
+        widen(9)
+        o_mm(4, (0,))
+        o_mm(4, (1,))
+        v_quant(5)
+        x_perm(9)
+        o_out(4, (0,))
+        o_out(4, (1,))
+        v_mm(6, (0,))
+        v_mm(6, (1,))
+        v_out(6, (0,))
+        v_out(6, (1,))
+        widen(10)
+        o_mm(5, (0,))
+        o_mm(5, (1,))
+        v_quant(6)
+        o_out(5, (0,))
+        o_out(5, (1,))
+        turn(8)
+        turn(9)
+        x_out(8)
+        x_out(9)
+        x_perm(10)
+        x_quant(8)
+        x_quant(9)
+        v_mm(7, (0,))
+        v_mm(7, (1,))
+        v_out(7, (0,))
+        v_out(7, (1,))
+        widen(11)
+        o_mm(6, (0,))
+        o_mm(6, (1,))
+        v_quant(7)
+        x_perm(11)
+        o_out(6, (0,))
+        o_out(6, (1,))
+        v_mm(8, (0,))
+        v_mm(8, (1,))
+        v_out(8, (0,))
+        v_out(8, (1,))
+        o_mm(7, (0,))
+        o_mm(7, (1,))
+        v_quant(8)
+        o_out(7, (0,))
+        o_out(7, (1,))
+        turn(10)
+        turn(11)
+        x_out(10)
+        x_out(11)
+        x_quant(10)
+        x_quant(11)
+        v_mm(9, (0,))
+        v_mm(9, (1,))
+        v_out(9, (0,))
+        v_out(9, (1,))
+        o_mm(8, (0,))
+        o_mm(8, (1,))
+        v_quant(9)
+        o_out(8, (0,))
+        o_out(8, (1,))
+        v_mm(10, (0,))
+        v_mm(10, (1,))
+        v_out(10, (0,))
+        v_out(10, (1,))
+        o_mm(9, (0,))
+        o_mm(9, (1,))
+        v_quant(10)
+        o_out(9, (0,))
+        o_out(9, (1,))
+        v_mm(11, (0,))
+        v_mm(11, (1,))
+        v_out(11, (0,))
+        v_out(11, (1,))
+        o_mm(10, (0,))
+        o_mm(10, (1,))
+        v_quant(11)
+        o_out(10, (0,))
+        o_out(10, (1,))
+        o_mm(11, (0,))
+        o_mm(11, (1,))
+        o_out(11, (0,))
+        o_out(11, (1,))

@@ -28,68 +28,71 @@ def tile_coupled_newton_colouring_step_s11_kernel(tc, x_bytes, x_scale, y, z_wor
     with ExitStack() as ctx:
         keep = ctx.enter_context(tc.tile_pool(name="keep", bufs=1))
         work = ctx.enter_context(tc.tile_pool(name="work", bufs=3))
-        psum = ctx.enter_context(tc.psum_pool(name="psum", bufs=2))
+        psum = ctx.enter_context(tc.psum_pool(name="psum", bufs=8))
         ctx.enter_context(tc.manual_schedule())
+        on_vector, on_scalar = nc.vector.tensor_copy, nc.scalar.copy
+
+        def bank():
+            return psum.tile([P, 4, P], F32, name="bank", tag="bank", bufs=8)
 
         xs_col = keep.tile([P, 8], F32, name="xs_col")
-        nc.sync.dma_start(out=xs_col[:], in_=x_scale.rearrange("o (p j) -> p (o j)", j=8))
         zs_raw = keep.tile([P, 2, N], U8, name="zs_raw", align_bytes=64)
-        nc.vector.memset(zs_raw[:].rearrange("p g n -> p (g n)").bitcast(I32), 0)
-        for q in range(4):
-            nc.sync.dma_start(
-                out=zs_raw[32 * q : 32 * q + 4, :, :].bitcast(I32),
-                in_=z_scales[:, 4 * q : 4 * q + 4, :].bitcast(I32).rearrange("g r n -> r g n"),
-            )
+        gain_bc = keep.tile([P, N], BF16, name="gain_bc", align_bytes=64)
         y_view = y.rearrange("(g p j) n -> g p j n", p=P, j=4)
-        y_raw = {}
-        zw_raw = keep.tile([P, 2, 2 * N], U8, name="zw_raw", align_bytes=64)
-        xb = []
+        x_view = x_bytes.rearrange("(i p) k -> i p k", p=P)
+        x_view2 = x_bytes.rearrange("(i s p) k -> i p s k", s=2, p=P)
+        y_raw, zw_raw, xb = {}, {}, {}
 
-        def load_y(kp, h):
-            t = keep.tile([P, 4, 512], BF16, name=f"y_raw_{kp}{h}", align_bytes=64)
-            nc.sync.dma_start(out=t[:], in_=y_view[kp][:, :, 512 * h : 512 * h + 512])
-            y_raw[kp, h] = t
+        def load_xs():
+            nc.sync.dma_start(out=xs_col[:], in_=x_scale.rearrange("o (p j) -> p (o j)", j=8))
 
-        x_view = x_bytes.rearrange("(i s p) k -> i p s k", s=2, p=P)
-
-        def load_x(pair):
-            t = keep.tile([P, 2, N], U8, name=f"xb_{pair}", align_bytes=64)
-            nc.sync.dma_start(out=t[:], in_=x_view[pair])
-            xb.append(t)
-
-        def load_z(g):
-            for kp in range(2):
+        def load_zs():
+            for q in range(4):
                 nc.sync.dma_start(
-                    out=zw_raw[:, kp, N * g : N * g + N].bitcast(I32), in_=z_words[kp][:, N * g : N * g + N].bitcast(I32)
+                    out=zs_raw[32 * q : 32 * q + 4, :, :].bitcast(I32),
+                    in_=z_scales[:, 4 * q : 4 * q + 4, :].bitcast(I32).rearrange("g r n -> r g n"),
                 )
 
-        load_x(0)
-        load_z(0)
-        load_y(0, 0)
-        load_y(1, 0)
-        load_z(1)
-        load_x(1)
-        load_y(0, 1)
-        load_y(1, 1)
-        for pair in range(2, PAIRS):
-            load_x(pair)
-        gain_bc = keep.tile([P, N], BF16, name="gain_bc", align_bytes=64)
-        nc.sync.dma_start(out=gain_bc[:], in_=gain.partition_broadcast(P))
+        def load_y(kp, h):
+            y_raw[kp, h] = keep.tile([P, 4, 512], BF16, name=f"y_raw_{kp}{h}", align_bytes=64)
+            nc.sync.dma_start(out=y_raw[kp, h][:], in_=y_view[kp][:, :, 512 * h : 512 * h + 512])
+
+        def load_z(kp):
+            zw_raw[kp] = keep.tile([P, 2 * N], U8, name=f"zw_raw_{kp}", align_bytes=64)
+            nc.sync.dma_start(out=zw_raw[kp][:].bitcast(I32), in_=z_words[kp].bitcast(I32))
+
+        def load_x(i):
+            t = keep.tile([P, N], U8, name=f"xb_{i}", align_bytes=64)
+            nc.sync.dma_start(out=t[:], in_=x_view[i])
+            xb[i] = t[:]
+
+        def load_x_pair(pair):
+            t = keep.tile([P, 2, N], U8, name=f"xb2_{pair}", align_bytes=64)
+            nc.sync.dma_start(out=t[:], in_=x_view2[pair])
+            xb[2 * pair], xb[2 * pair + 1] = t[:, 0, :], t[:, 1, :]
+
+        def load_gain():
+            nc.sync.dma_start(out=gain_bc[:], in_=gain.partition_broadcast(P))
 
         ident = keep.tile([P, P], F32, name="ident", align_bytes=64)
-        make_identity(nc, ident[:])
-        eye15 = keep.tile([P, P], F32, name="eye15", align_bytes=64)
-        nc.gpsimd.tensor_scalar(out=eye15[:], in0=ident[:], scalar1=1.5, scalar2=0.0, op0=MULT, op1=ADD)
-
+        eye15 = keep.tile([P, P, 8], BF16, name="eye15", align_bytes=64)
         xsb = keep.tile([P, N], F32, name="xsb", align_bytes=64)
-        for half in range(2):
-            ps = psum.tile([P, 4, P], F32, name="xt", tag="xt", bufs=2)
+        xs_ps = {}
+
+        def constants():
+            nc.vector.memset(eye15[:].rearrange("p n c -> p (n c)").bitcast(I32), 0)
+            make_identity(nc, ident[:])
+            nc.gpsimd.tensor_scalar(out=eye15[:, :, 3], in0=ident[:], scalar1=1.5, scalar2=0.0, op0=MULT, op1=ADD)
+
+        def xs_turn(half):
+            xs_ps[half] = bank()
             for j in range(4):
-                nc.tensor.transpose(ps[:, j, :], xs_col[:, 4 * half + j : 4 * half + j + 1].to_broadcast([P, P]), ident[:])
-            copy = nc.vector.tensor_copy if half else nc.scalar.copy
+                nc.tensor.transpose(xs_ps[half][:, j, :], xs_col[:, 4 * half + j : 4 * half + j + 1].to_broadcast([P, P]), ident[:])
+
+        def xs_out(half, copy):
             copy(
                 out=xsb[:].rearrange("p (c j) -> p c j", j=8)[:, :, 4 * half : 4 * half + 4],
-                in_=ps[:].rearrange("p j c -> p c j"),
+                in_=xs_ps[half][:].rearrange("p j c -> p c j"),
             )
 
         yq = keep.tile([P, 2, N], U32, name="yq", align_bytes=64)
@@ -116,424 +119,270 @@ def tile_coupled_newton_colouring_step_s11_kernel(tc, x_bytes, x_scale, y, z_wor
                 in_=yi[kp, h][:, lo:hi].rearrange("p n j -> p (n j)"),
             )
 
-        def z_lay(g):
-            for kp in range(2):
-                nc.vector.tensor_copy(
-                    out=zq[:, kp, N * g : N * g + N].bitcast(I32).rearrange("p (t q r) -> p t q r", t=4, r=4),
-                    in_=zw_raw[:, kp, N * g : N * g + N].bitcast(I32).rearrange("p (q t r) -> p t q r", t=4, r=4),
-                )
-                nc.vector.tensor_copy(
-                    out=zs[:, kp, 512 * g : 512 * g + 512].bitcast(I32).rearrange("p (t q r) -> p t q r", t=4, r=2),
-                    in_=zs_raw[:, kp, 512 * g : 512 * g + 512].bitcast(I32).rearrange("p (q t r) -> p t q r", t=4, r=2),
-                )
+        def z_lay(kp, g):
+            nc.vector.tensor_copy(
+                out=zq[:, kp, N * g : N * g + N].bitcast(I32).rearrange("p (t q r) -> p t q r", t=4, r=4),
+                in_=zw_raw[kp][:, N * g : N * g + N].bitcast(I32).rearrange("p (q t r) -> p t q r", t=4, r=4),
+            )
+            nc.vector.tensor_copy(
+                out=zs[:, kp, 512 * g : 512 * g + 512].bitcast(I32).rearrange("p (t q r) -> p t q r", t=4, r=2),
+                in_=zs_raw[:, kp, 512 * g : 512 * g + 512].bitcast(I32).rearrange("p (q t r) -> p t q r", t=4, r=2),
+            )
 
-        xw, xt, xi, xq, xqs = {}, {}, {}, {}, {}
+        xw, xp, xt, xi, xq, xqs = {}, {}, {}, {}, {}, {}
 
         def widen(i):
-            if i >= TILES:
-                return
-            xw[i] = work.tile([P, N], BF16, name="xw", tag="xw", bufs=6, align_bytes=64)
-            nc.vector.tensor_tensor(out=xw[i][:], in0=xb[i // 2][:, i % 2, :].bitcast(FP8), in1=xsb[:], op=MULT)
-
-        xp = {}
+            if i < TILES:
+                xw[i] = work.tile([P, N], BF16, name="xw", tag="xw", bufs=6, align_bytes=64)
+                nc.vector.tensor_tensor(out=xw[i][:], in0=xb[i].bitcast(FP8), in1=xsb[:], op=MULT)
 
         def x_perm(i):
-            if i >= TILES:
-                return
-            xp[i] = work.tile([P, 2, 2, P], F32, name="xp", tag="xp", bufs=6, align_bytes=64)
-            nc.scalar.copy(out=xp[i][:], in_=xw[i][:].bitcast(F32).rearrange("p (g n u) -> p g u n", g=2, u=2))
+            if i < TILES:
+                xp[i] = work.tile([P, 2, 2, P], F32, name="xp", tag="xp", bufs=4, align_bytes=64)
+                nc.scalar.copy(out=xp[i][:], in_=xw[i][:].bitcast(F32).rearrange("p (g n u) -> p g u n", g=2, u=2))
 
         def turn(i):
-            if i >= TILES:
-                return
-            perm = i in xp
-            words = xp[i][:].rearrange("p g u n -> p (g u n)") if perm else xw[i][:].bitcast(F32)
-            xt[i] = psum.tile([P, 2, 2, P], F32, name="xt", tag="xt", bufs=2)
-            for g in range(2):
-                for u in range(2):
-                    nc.tensor.transpose(xt[i][:, g, u, :], words[:, 256 * g + 128 * u : 256 * g + 128 * u + 128] if perm else words[:, 256 * g + u : 256 * (g + 1) : 2], ident[:])
+            if i < TILES:
+                xt[i] = bank()
+                for g in range(2):
+                    for u in range(2):
+                        if i in xp:
+                            words = xp[i][:, g, u, :]
+                        else:
+                            words = xw[i][:].bitcast(F32)[:, 256 * g + u : 256 * (g + 1) : 2]
+                        nc.tensor.transpose(xt[i][:, 2 * g + u, :], words, ident[:])
 
         def x_out(i):
-            if i >= TILES:
-                return
-            xi[i] = work.tile([P, 2, P, 4], BF16, name="xi", tag="xi", bufs=4, align_bytes=64)
-            nc.scalar.copy(
-                out=xi[i][:].rearrange("p g m t -> p (g m t)").bitcast(F32).rearrange("p (g m u) -> p g m u", g=2, u=2),
-                in_=xt[i][:].rearrange("p g u m -> p g m u"),
-            )
+            if i < TILES:
+                if i // 2 not in xi:
+                    xi[i // 2] = work.tile([P, 2, 2, P, 4], BF16, name="xi", tag="xi", bufs=2, align_bytes=64)
+                nc.scalar.copy(
+                    out=xi[i // 2][:, i % 2].rearrange("p g m t -> p (g m t)").bitcast(F32).rearrange("p (g m u) -> p g m u", g=2, u=2),
+                    in_=xt[i][:].rearrange("p (g u) m -> p g m u", u=2),
+                )
 
-        def x_quant(i):
-            if i >= TILES:
-                return
-            xq[i] = work.tile([P, 2 * P], U32, name="xq", tag="xq", bufs=6, align_bytes=64)
-            xqs[i] = work.tile([P, 2 * P], U8, name="xqs", tag="xqs", bufs=6, align_bytes=64)
-            nc.vector.quantize_mx(
-                out=xq[i][:].bitcast(FP8X4), scales=xqs[i][:], in_=xi[i][:].rearrange("p g m t -> p (g m t)")
-            )
+        def x_quant(pair, s0=0, ns=2):
+            if pair < PAIRS:
+                if pair not in xq:
+                    xq[pair] = work.tile([P, 4 * P], U32, name="xq", tag="xq", bufs=3, align_bytes=64)
+                    xqs[pair] = work.tile([P, 4 * P], U8, name="xqs", tag="xqs", bufs=3, align_bytes=64)
+                c = slice(2 * P * s0, 2 * P * (s0 + ns))
+                nc.vector.quantize_mx(
+                    out=xq[pair][:, c].bitcast(FP8X4), scales=xqs[pair][:, c], in_=xi[pair][:, s0 : s0 + ns].rearrange("p s g m t -> p (s g m t)")
+                )
 
         zps = {}
 
-        def zy(h, t1, g):
-            ps = psum.tile([P, 4, P], F32, name="mm", tag="mm", bufs=3)
+        def zy_pass(h, t1, g, t, kp, start, stop):
             cols = slice(512 * h + 128 * t1, 512 * h + 128 * t1 + 128)
-            for t in range(4):
-                c0 = 512 * g + 128 * t
-                for kp in range(2):
-                    nc.tensor.matmul_mx(
-                        out=ps[:, t, :],
-                        lhsT=zq[:, kp, 2 * c0 : 2 * c0 + 256].bitcast(FP4X4),
-                        lhsT_scale=zs[:, kp, c0 : c0 + 128],
-                        rhs=yq[:, kp, cols].bitcast(FP8X4),
-                        rhs_scale=ys[:, kp, cols],
-                        start=(kp == 0),
-                        stop=(kp == 1),
-                    )
-            zps[h, t1, g] = ps
-
-        dblk = {}
-
-        def d_out(h, t1, g):
-            dblk[h, t1] = work.tile([P, P], F32, name="dblk", tag="dblk", bufs=8, align_bytes=64)
-            nc.scalar.activation(out=dblk[h, t1][:], in_=zps[h, t1, g][:, t1, :], func=COPY, scale=-0.5)
-
-        def d_add(h, t1, g):
-            dst = ci[g, h][:].rearrange("p (q t r) f -> p t q r f", t=4, r=8)[:, t1, :, :, t1]
-            nc.gpsimd.tensor_tensor(
-                out=dst,
-                in0=dblk[h, t1][:].rearrange("p (q r) -> p q r", r=8),
-                in1=eye15[:].rearrange("p (q r) -> p q r", r=8),
-                op=ADD,
+            c0 = 512 * g + 128 * t
+            nc.tensor.matmul_mx(
+                out=zps[h, t1, g][:, t, :],
+                lhsT=zq[:, kp, 2 * c0 : 2 * c0 + 256].bitcast(FP4X4),
+                lhsT_scale=zs[:, kp, c0 : c0 + 128],
+                rhs=yq[:, kp, cols].bitcast(FP8X4),
+                rhs_scale=ys[:, kp, cols],
+                start=start,
+                stop=stop,
             )
 
-        def c_out(h, t1, g, eng):
-            if (g, h) not in ci:
-                ci[g, h] = keep.tile([P, 512, 4], BF16, name=f"ci_{g}{h}", align_bytes=64)
-            src = zps[h, t1, g][:].rearrange("p f (q r) -> p q r f", r=8)
-            dst = ci[g, h][:].rearrange("p (q t r) f -> p t q r f", t=4, r=8)[:, t1]
-            if eng == "V":
-                nc.vector.tensor_scalar(out=dst, in0=src, scalar1=-0.5, scalar2=None, op0=MULT)
-            else:
-                nc.scalar.activation(out=dst, in_=src, func=COPY, scale=-0.5)
+        def zy(h, g, t1s):
+            for t1 in t1s:
+                zps[h, t1, g] = bank()
+            for t in range(4):
+                for kp in range(2):
+                    for t1 in t1s:
+                        zy_pass(h, t1, g, t, kp, kp == 0, kp == 1)
 
-        def c_quant(g, h):
+        def zy_half(h, g, t1s, kp):
+            for t1 in t1s:
+                if kp == 0:
+                    zps[h, t1, g] = bank()
+            for t in range(4):
+                for t1 in t1s:
+                    zy_pass(h, t1, g, t, kp, kp == 0 and t == 0, kp == 1 and t == 3)
+
+        def c_out(h, g, t1):
+            if (g, h) not in ci:
+                ci[g, h] = keep.tile([P, 4, P, 4], BF16, name=f"ci_{g}{h}", align_bytes=64)
+            src = zps[h, t1, g][:].rearrange("p f n -> p n f")
+            if g == h:
+                nc.vector.scalar_tensor_tensor(out=ci[g, h][:, t1], in0=src, scalar=-0.5, in1=eye15[:, :, 3 - t1 : 7 - t1], op0=MULT, op1=ADD)
+            else:
+                nc.scalar.activation(out=ci[g, h][:, t1], in_=src, func=COPY, scale=-0.5)
+
+        def c_quant(h, g):
             nc.vector.quantize_mx(
                 out=cq[:, g, 512 * h : 512 * h + 512].bitcast(FP8X4),
                 scales=cs[:, g, 512 * h : 512 * h + 512],
-                in_=ci[g, h][:].rearrange("p n f -> p (n f)"),
+                in_=ci[g, h][:].rearrange("p t n f -> p (t n f)"),
             )
 
         vps, vi, vq, vqs = {}, {}, {}, {}
 
-        def v_mm(i, gs=(0, 1)):
-            for g in gs:
-                ps = psum.tile([P, 4, P], F32, name="mm", tag="mm", bufs=3)
-                for t in range(4):
-                    c0 = 512 * g + 128 * t
-                    for kp in range(2):
+        def v_mm(pair, g):
+            for s in range(2):
+                vps[pair, g, s] = bank()
+            for t in range(4):
+                c0 = 512 * g + 128 * t
+                for kp in range(2):
+                    for s in range(2):
+                        c = slice(P * (2 * s + kp), P * (2 * s + kp + 1))
                         nc.tensor.matmul_mx(
-                            out=ps[:, t, :],
+                            out=vps[pair, g, s][:, t, :],
                             lhsT=yq[:, kp, c0 : c0 + 128].bitcast(FP8X4),
                             lhsT_scale=ys[:, kp, c0 : c0 + 128],
-                            rhs=xq[i][:, P * kp : P * kp + P].bitcast(FP8X4),
-                            rhs_scale=xqs[i][:, P * kp : P * kp + P],
+                            rhs=xq[pair][:, c].bitcast(FP8X4),
+                            rhs_scale=xqs[pair][:, c],
                             start=(kp == 0),
                             stop=(kp == 1),
                         )
-                vps[i, g] = ps
 
-        def v_out(i, gs=(0, 1)):
-            if i not in vi:
-                vi[i] = work.tile([P, 2, P, 4], BF16, name="vi", tag="vi", bufs=4, align_bytes=64)
-            for g in gs:
-                nc.scalar.copy(out=vi[i][:, g], in_=vps[i, g][:].rearrange("p t m -> p m t"))
+        def v_out(pair, g):
+            vi[pair, g] = work.tile([P, 2, P, 4], BF16, name="vi", tag="vi", bufs=4, align_bytes=64)
+            for s in range(2):
+                nc.scalar.copy(out=vi[pair, g][:, s], in_=vps[pair, g, s][:].rearrange("p t m -> p m t"))
 
-        def v_quant(i):
-            vq[i] = work.tile([P, 2 * P], U32, name="vq", tag="vq", bufs=3, align_bytes=64)
-            vqs[i] = work.tile([P, 2 * P], U8, name="vqs", tag="vqs", bufs=3, align_bytes=64)
-            parts = [(0, 1), (1, 2)] if i == TILES - 1 else [(0, 2)]
-            for g0, g1 in parts:
-                nc.vector.quantize_mx(
-                    out=vq[i][:, P * g0 : P * g1].bitcast(FP8X4),
-                    scales=vqs[i][:, P * g0 : P * g1],
-                    in_=vi[i][:, g0:g1].rearrange("p g m t -> p (g m t)"),
-                )
+        def v_quant(pair, g):
+            vq[pair, g] = work.tile([P, 2 * P], U32, name="vq", tag="vq", bufs=2 * PAIRS, align_bytes=64)
+            vqs[pair, g] = work.tile([P, 2 * P], U8, name="vqs", tag="vqs", bufs=2 * PAIRS, align_bytes=64)
+            nc.vector.quantize_mx(
+                out=vq[pair, g][:].bitcast(FP8X4), scales=vqs[pair, g][:], in_=vi[pair, g][:].rearrange("p s m t -> p (s m t)")
+            )
 
         ops = {}
-
-        def o_mm(i, hs=(0, 1)):
-            for h in hs:
-                ps = psum.tile([P, 512], F32, name="ops", tag="ops", bufs=3)
-                for g in range(2):
-                    nc.tensor.matmul_mx(
-                        out=ps[:],
-                        lhsT=vq[i][:, P * g : P * g + P].bitcast(FP8X4),
-                        lhsT_scale=vqs[i][:, P * g : P * g + P],
-                        rhs=cq[:, g, 512 * h : 512 * h + 512].bitcast(FP8X4),
-                        rhs_scale=cs[:, g, 512 * h : 512 * h + 512],
-                        start=(g == 0),
-                        stop=(g == 1),
-                    )
-                ops[i, h] = ps
-
         out_view = out.rearrange("(i p) n -> i p n", p=P)
 
-        ot = {}
+        def o_mm(i, h):
+            ops[i, h] = bank()
+            c = slice(P * (i % 2), P * (i % 2) + P)
+            for g in range(2):
+                nc.tensor.matmul_mx(
+                    out=ops[i, h][:].rearrange("p a b -> p (a b)"),
+                    lhsT=vq[i // 2, g][:, c].bitcast(FP8X4),
+                    lhsT_scale=vqs[i // 2, g][:, c],
+                    rhs=cq[:, g, 512 * h : 512 * h + 512].bitcast(FP8X4),
+                    rhs_scale=cs[:, g, 512 * h : 512 * h + 512],
+                    start=(g == 0),
+                    stop=(g == 1),
+                )
 
-        def o_out(i, hs=(0, 1)):
-            if i not in ot:
-                ot[i] = work.tile([P, N], F32, name="ot", tag="ot", bufs=4, align_bytes=64)
-            width = 256 if i == TILES - 1 else 512
-            for h in hs:
-                for c0 in range(0, 512, width):
-                    c = slice(512 * h + c0, 512 * h + c0 + width)
-                    nc.vector.tensor_tensor(out=ot[i][:, c], in0=ops[i, h][:, c0 : c0 + width], in1=gain_bc[:, c], op=MULT)
-                    if i == TILES - 1:
-                        nc.sync.dma_start(out=out_view[i][:, c], in_=ot[i][:, c])
-                if h == 1 and i < TILES - 1:
-                    nc.sync.dma_start(out=out_view[i], in_=ot[i][:])
+        def o_out(i, h, parts=1):
+            ot = work.tile([P, 16, 4, 8], F32, name="ot", tag="ot", bufs=6, align_bytes=64)
+            src = ops[i, h][:].rearrange("p t (q r) -> p q t r", r=8)
+            gains = gain_bc[:, 512 * h : 512 * h + 512].rearrange("p (q t r) -> p q t r", t=4, r=8)
+            nq = 16 // parts
+            for q0 in range(0, 16, nq):
+                q = slice(q0, q0 + nq)
+                nc.vector.tensor_tensor(out=ot[:, q], in0=src[:, q], in1=gains[:, q], op=MULT)
+                nc.sync.dma_start(
+                    out=out_view[i][:, 512 * h + 32 * q0 : 512 * h + 32 * (q0 + nq)], in_=ot[:, q].rearrange("p q t r -> p (q t r)")
+                )
 
-        V, S = nc.vector.tensor_copy, nc.scalar.copy
-        widen(1)
+        nc.vector.memset(zs_raw[:].rearrange("p g n -> p (g n)").bitcast(I32), 0)
+        load_xs()
+        load_y(0, 0)
+        load_zs()
+        load_z(0)
+        load_y(1, 0)
+        load_z(1)
+        load_x_pair(0)
+        load_y(0, 1)
+        load_y(1, 1)
+        load_x_pair(1)
+        load_x_pair(2)
+        load_gain()
+        for pair in range(3, PAIRS):
+            load_x_pair(pair)
+        constants()
+        xs_turn(0)
+        xs_turn(1)
+        xs_out(0, on_scalar)
+        xs_out(1, on_scalar)
+
+        for kp in range(2):
+            for t in range(4):
+                y_lay(kp, 0, t, on_scalar if t == 3 else on_vector)
+            y_quant(kp, 0, 0, 2)
+            z_lay(kp, 1)
+            zy_half(0, 1, (0, 1), kp)
+            y_quant(kp, 0, 2, 2)
+            zy_half(0, 1, (2, 3), kp)
+            z_lay(kp, 0)
         widen(0)
-        y_lay(0, 0, 3, S)
-        y_lay(0, 0, 1, V)
-        z_lay(0)
-        turn(1)
-        y_lay(0, 0, 0, S)
+        widen(1)
+        zy(0, 0, (0, 1))
+        zy(0, 0, (2, 3))
+        for t in range(4):
+            y_lay(0, 1, t, on_scalar)
+            if t == 1:
+                c_out(0, 1, 0)
+                c_out(0, 1, 1)
+        for t in range(4):
+            y_lay(1, 1, t, on_vector)
         turn(0)
-        y_lay(1, 0, 0, V)
-        y_lay(1, 0, 1, V)
-        y_lay(0, 0, 2, V)
-        y_lay(1, 0, 3, S)
-        y_quant(1, 0, 0, 1)
-        y_quant(0, 0, 0, 1)
-        x_out(1)
-        y_quant(1, 0, 1, 1)
-        zy(0, 0, 0)
-        y_lay(1, 0, 2, S)
-        y_quant(0, 0, 1, 1)
-        x_out(0)
-        z_lay(1)
-        y_quant(1, 0, 2, 2)
-        zy(0, 1, 0)
-        y_lay(0, 1, 0, V)
-        d_out(0, 0, 0)
-        zy(0, 1, 1)
-        x_quant(0)
-        c_out(0, 0, 0, "S")
-        d_out(0, 1, 0)
-        c_out(0, 1, 0, "S")
-        zy(0, 0, 1)
-        y_lay(1, 1, 1, V)
-        c_out(0, 1, 1, "S")
-        y_quant(0, 0, 2, 2)
-        y_lay(0, 1, 3, V)
-        x_quant(1)
-        zy(0, 3, 0)
-        y_lay(1, 1, 3, S)
-        c_out(0, 0, 1, "S")
-        zy(0, 2, 1)
-        y_lay(0, 1, 2, V)
-        widen(2)
-        d_out(0, 3, 0)
-        c_out(0, 3, 0, "S")
-        y_lay(0, 1, 1, V)
-        c_out(0, 2, 1, "S")
-        y_lay(1, 1, 0, V)
-        zy(0, 2, 0)
-        y_lay(1, 1, 2, V)
-        d_out(0, 2, 0)
-        v_mm(0, (0,))
-        y_quant(0, 1, 0, 4)
-        c_out(0, 2, 0, "S")
-        v_mm(1, (0,))
-        v_out(0, (0,))
-        v_out(1, (0,))
-        zy(0, 3, 1)
+        turn(1)
+        y_quant(0, 1, 0, 2)
         y_quant(1, 1, 0, 4)
-        x_perm(2)
-        zy(1, 3, 0)
-        c_out(1, 3, 0, "S")
-        c_out(0, 3, 1, "V")
-        zy(1, 0, 1)
-        d_add(0, 1, 0)
-        d_add(0, 0, 0)
-        d_out(1, 0, 1)
+        y_quant(0, 1, 2, 2)
+        c_out(0, 1, 2)
+        c_out(0, 1, 3)
+        x_out(0)
+        x_out(1)
+        zy(1, 0, (0, 1))
+        for t1 in range(4):
+            c_out(0, 0, t1)
+        zy(1, 0, (2, 3))
+        x_quant(0)
+        for t1 in range(4):
+            c_out(1, 0, t1)
+        widen(2)
         widen(3)
-        c_out(1, 0, 1, "S")
-        c_quant(1, 0)
-        v_mm(0, (1,))
-        d_add(0, 2, 0)
-        v_out(0, (1,))
-        zy(1, 1, 0)
-        x_perm(3)
-        zy(1, 0, 0)
-        zy(1, 2, 0)
-        c_out(1, 1, 0, "V")
-        turn(2)
-        d_add(0, 3, 0)
-        c_out(1, 0, 0, "S")
-        turn(3)
-        c_out(1, 2, 0, "S")
-        v_mm(1, (1,))
-        v_quant(0)
         c_quant(0, 0)
-        widen(4)
         c_quant(0, 1)
+        widen(4)
+        v_mm(0, 0)
+        v_out(0, 0)
+        zy(1, 1, (0, 1))
+        c_out(1, 1, 0)
+        c_out(1, 1, 1)
+        turn(2)
+        turn(3)
         x_out(2)
-        zy(1, 2, 1)
-        v_out(1, (1,))
-        zy(1, 1, 1)
-        widen(5)
-        d_out(1, 2, 1)
-        v_quant(1)
-        zy(1, 3, 1)
-        x_quant(2)
         x_out(3)
-        o_mm(0, (0,))
-        c_out(1, 2, 1, "S")
-        o_mm(1, (0,))
-        d_out(1, 1, 1)
-        d_add(1, 2, 1)
-        c_out(1, 1, 1, "V")
-        d_out(1, 3, 1)
-        v_mm(2, (1,))
-        c_out(1, 3, 1, "S")
-        v_mm(2, (0,))
-        o_out(0, (0,))
-        d_add(1, 0, 1)
-        o_out(1, (0,))
-        d_add(1, 1, 1)
-        d_add(1, 3, 1)
-        x_perm(5)
+        widen(5)
+        v_quant(0, 0)
+        v_mm(0, 1)
+        v_out(0, 1)
+        x_quant(1)
         x_perm(4)
-        v_out(2, (0,))
-        x_quant(3)
+        x_perm(5)
+        zy(1, 1, (2, 3))
+        c_quant(1, 0)
+        c_out(1, 1, 2)
+        c_out(1, 1, 3)
+        v_quant(0, 1)
         c_quant(1, 1)
-        turn(5)
-        turn(4)
-        widen(6)
-        v_out(2, (1,))
-        x_out(5)
-        x_out(4)
-        o_mm(1, (1,))
-        v_quant(2)
-        o_out(1, (1,))
-        o_mm(0, (1,))
-        x_perm(6)
-        x_quant(5)
-        o_out(0, (1,))
-        x_quant(4)
-        v_mm(3, (0,))
-        v_mm(3, (1,))
-        v_out(3, (0,))
-        v_out(3, (1,))
-        widen(7)
-        o_mm(2, (0,))
-        o_mm(2, (1,))
-        v_quant(3)
-        x_perm(7)
-        o_out(2, (0,))
-        o_out(2, (1,))
-        v_mm(4, (0,))
-        v_mm(4, (1,))
-        v_out(4, (0,))
-        v_out(4, (1,))
-        widen(8)
-        o_mm(3, (0,))
-        o_mm(3, (1,))
-        v_quant(4)
-        o_out(3, (0,))
-        o_out(3, (1,))
-        turn(6)
-        turn(7)
-        x_out(6)
-        x_out(7)
-        x_perm(8)
-        x_quant(6)
-        x_quant(7)
-        v_mm(5, (0,))
-        v_mm(5, (1,))
-        v_out(5, (0,))
-        v_out(5, (1,))
-        widen(9)
-        o_mm(4, (0,))
-        o_mm(4, (1,))
-        v_quant(5)
-        x_perm(9)
-        o_out(4, (0,))
-        o_out(4, (1,))
-        v_mm(6, (0,))
-        v_mm(6, (1,))
-        v_out(6, (0,))
-        v_out(6, (1,))
-        widen(10)
-        o_mm(5, (0,))
-        o_mm(5, (1,))
-        v_quant(6)
-        o_out(5, (0,))
-        o_out(5, (1,))
-        turn(8)
-        turn(9)
-        x_out(8)
-        x_out(9)
-        x_perm(10)
-        x_quant(8)
-        x_quant(9)
-        v_mm(7, (0,))
-        v_mm(7, (1,))
-        v_out(7, (0,))
-        v_out(7, (1,))
-        widen(11)
-        o_mm(6, (0,))
-        o_mm(6, (1,))
-        v_quant(7)
-        x_perm(11)
-        o_out(6, (0,))
-        o_out(6, (1,))
-        v_mm(8, (0,))
-        v_mm(8, (1,))
-        v_out(8, (0,))
-        v_out(8, (1,))
-        o_mm(7, (0,))
-        o_mm(7, (1,))
-        v_quant(8)
-        o_out(7, (0,))
-        o_out(7, (1,))
-        turn(10)
-        turn(11)
-        x_out(10)
-        x_out(11)
-        x_quant(10)
-        x_quant(11)
-        v_mm(9, (0,))
-        v_mm(9, (1,))
-        v_out(9, (0,))
-        v_out(9, (1,))
-        o_mm(8, (0,))
-        o_mm(8, (1,))
-        v_quant(9)
-        o_out(8, (0,))
-        o_out(8, (1,))
-        v_mm(10, (0,))
-        v_mm(10, (1,))
-        v_out(10, (0,))
-        v_out(10, (1,))
-        o_mm(9, (0,))
-        o_mm(9, (1,))
-        v_quant(10)
-        o_out(9, (0,))
-        o_out(9, (1,))
-        v_mm(11, (0,))
-        v_mm(11, (1,))
-        v_out(11, (0,))
-        v_out(11, (1,))
-        o_mm(10, (0,))
-        o_mm(10, (1,))
-        v_quant(11)
-        o_out(10, (0,))
-        o_out(10, (1,))
-        o_mm(11, (0,))
-        o_mm(11, (1,))
-        o_out(11, (0,))
-        o_out(11, (1,))
+
+        for pair in range(1, PAIRS + 1):
+            if pair < PAIRS:
+                v_mm(pair, 0)
+                v_out(pair, 0)
+                turn(2 * pair + 2)
+                turn(2 * pair + 3)
+                x_out(2 * pair + 2)
+                x_out(2 * pair + 3)
+                widen(2 * pair + 4)
+                x_quant(pair + 1)
+                widen(2 * pair + 5)
+                v_quant(pair, 0)
+                v_mm(pair, 1)
+                v_out(pair, 1)
+                x_perm(2 * pair + 4)
+                x_perm(2 * pair + 5)
+            for s in range(2):
+                for h in range(2):
+                    o_mm(2 * pair - 2 + s, h)
+                    o_out(2 * pair - 2 + s, h, 2 if pair == PAIRS and s and h else 1)
+                if s == 0 and pair < PAIRS:
+                    v_quant(pair, 1)

@@ -75,14 +75,13 @@ def tile_coupled_newton_colouring_step_s11_kernel(tc, x_bytes, x_scale, y, z_wor
             nc.sync.dma_start(out=gain_bc[:], in_=gain.partition_broadcast(P))
 
         ident = keep.tile([P, P], F32, name="ident", align_bytes=64)
-        eye15 = keep.tile([P, P, 8], BF16, name="eye15", align_bytes=64)
+        eye15 = keep.tile([P, P], F32, name="eye15", align_bytes=64)
         xsb = keep.tile([P, N], F32, name="xsb", align_bytes=64)
         xs_ps = {}
 
         def constants():
-            nc.vector.memset(eye15[:].rearrange("p n c -> p (n c)").bitcast(I32), 0)
             make_identity(nc, ident[:])
-            nc.gpsimd.tensor_scalar(out=eye15[:, :, 3], in0=ident[:], scalar1=1.5, scalar2=0.0, op0=MULT, op1=ADD)
+            nc.gpsimd.tensor_scalar(out=eye15[:], in0=ident[:], scalar1=1.5, scalar2=0.0, op0=MULT, op1=ADD)
 
         def xs_turn(half):
             xs_ps[half] = bank()
@@ -133,7 +132,7 @@ def tile_coupled_newton_colouring_step_s11_kernel(tc, x_bytes, x_scale, y, z_wor
 
         def widen(i):
             if i < TILES:
-                xw[i] = work.tile([P, N], BF16, name="xw", tag="xw", bufs=6, align_bytes=64)
+                xw[i] = work.tile([P, N], BF16, name="xw", tag="xw", bufs=8, align_bytes=64)
                 nc.vector.tensor_tensor(out=xw[i][:], in0=xb[i].bitcast(FP8), in1=xsb[:], op=MULT)
 
         def x_perm(i):
@@ -204,18 +203,27 @@ def tile_coupled_newton_colouring_step_s11_kernel(tc, x_bytes, x_scale, y, z_wor
 
         def c_out(h, g, t1):
             if (g, h) not in ci:
-                ci[g, h] = keep.tile([P, 4, P, 4], BF16, name=f"ci_{g}{h}", align_bytes=64)
-            src = zps[h, t1, g][:].rearrange("p f n -> p n f")
-            if g == h:
-                nc.vector.scalar_tensor_tensor(out=ci[g, h][:, t1], in0=src, scalar=-0.5, in1=eye15[:, :, 3 - t1 : 7 - t1], op0=MULT, op1=ADD)
-            else:
-                nc.scalar.activation(out=ci[g, h][:, t1], in_=src, func=COPY, scale=-0.5)
+                ci[g, h] = keep.tile([P, 512, 4], BF16, name=f"ci_{g}{h}", align_bytes=64)
+            src = zps[h, t1, g][:].rearrange("p f (q r) -> p q r f", r=8)
+            dst = ci[g, h][:].rearrange("p (q t r) f -> p t q r f", t=4, r=8)[:, t1]
+            nc.scalar.activation(out=dst, in_=src, func=COPY, scale=-0.5)
+
+        def c_diag(h, t1):
+            dst = ci[h, h][:].rearrange("p (q t r) f -> p t q r f", t=4, r=8)[:, t1, :, :, t1]
+            nc.vector.scalar_tensor_tensor(
+                out=dst,
+                in0=zps[h, t1, h][:, t1, :].rearrange("p (q r) -> p q r", r=8),
+                scalar=-0.5,
+                in1=eye15[:].rearrange("p (q r) -> p q r", r=8),
+                op0=MULT,
+                op1=ADD,
+            )
 
         def c_quant(h, g):
             nc.vector.quantize_mx(
                 out=cq[:, g, 512 * h : 512 * h + 512].bitcast(FP8X4),
                 scales=cs[:, g, 512 * h : 512 * h + 512],
-                in_=ci[g, h][:].rearrange("p t n f -> p (t n f)"),
+                in_=ci[g, h][:].rearrange("p n f -> p (n f)"),
             )
 
         vps, vi, vq, vqs = {}, {}, {}, {}
@@ -243,41 +251,35 @@ def tile_coupled_newton_colouring_step_s11_kernel(tc, x_bytes, x_scale, y, z_wor
             for s in range(2):
                 nc.scalar.copy(out=vi[pair, g][:, s], in_=vps[pair, g, s][:].rearrange("p t m -> p m t"))
 
-        def v_quant(pair, g):
-            vq[pair, g] = work.tile([P, 2 * P], U32, name="vq", tag="vq", bufs=2 * PAIRS, align_bytes=64)
-            vqs[pair, g] = work.tile([P, 2 * P], U8, name="vqs", tag="vqs", bufs=2 * PAIRS, align_bytes=64)
+        def v_quant(pair, g, s0=0, ns=2):
+            if (pair, g) not in vq:
+                vq[pair, g] = work.tile([P, 2 * P], U32, name="vq", tag="vq", bufs=2 * PAIRS, align_bytes=64)
+                vqs[pair, g] = work.tile([P, 2 * P], U8, name="vqs", tag="vqs", bufs=2 * PAIRS, align_bytes=64)
+            c = slice(P * s0, P * (s0 + ns))
             nc.vector.quantize_mx(
-                out=vq[pair, g][:].bitcast(FP8X4), scales=vqs[pair, g][:], in_=vi[pair, g][:].rearrange("p s m t -> p (s m t)")
+                out=vq[pair, g][:, c].bitcast(FP8X4), scales=vqs[pair, g][:, c], in_=vi[pair, g][:, s0 : s0 + ns].rearrange("p s m t -> p (s m t)")
             )
 
-        ops = {}
         out_view = out.rearrange("(i p) n -> i p n", p=P)
 
-        def o_mm(i, h):
-            ops[i, h] = bank()
-            c = slice(P * (i % 2), P * (i % 2) + P)
+        def o_part(i, c0, width):
+            ps = bank()
+            acc = ps[:].rearrange("p a b -> p (a b)")[:, 0:width]
+            m = slice(P * (i % 2), P * (i % 2) + P)
+            c = slice(c0, c0 + width)
             for g in range(2):
                 nc.tensor.matmul_mx(
-                    out=ops[i, h][:].rearrange("p a b -> p (a b)"),
-                    lhsT=vq[i // 2, g][:, c].bitcast(FP8X4),
-                    lhsT_scale=vqs[i // 2, g][:, c],
-                    rhs=cq[:, g, 512 * h : 512 * h + 512].bitcast(FP8X4),
-                    rhs_scale=cs[:, g, 512 * h : 512 * h + 512],
+                    out=acc,
+                    lhsT=vq[i // 2, g][:, m].bitcast(FP8X4),
+                    lhsT_scale=vqs[i // 2, g][:, m],
+                    rhs=cq[:, g, c].bitcast(FP8X4),
+                    rhs_scale=cs[:, g, c],
                     start=(g == 0),
                     stop=(g == 1),
                 )
-
-        def o_out(i, h, parts=1):
-            ot = work.tile([P, 16, 4, 8], F32, name="ot", tag="ot", bufs=6, align_bytes=64)
-            src = ops[i, h][:].rearrange("p t (q r) -> p q t r", r=8)
-            gains = gain_bc[:, 512 * h : 512 * h + 512].rearrange("p (q t r) -> p q t r", t=4, r=8)
-            nq = 16 // parts
-            for q0 in range(0, 16, nq):
-                q = slice(q0, q0 + nq)
-                nc.vector.tensor_tensor(out=ot[:, q], in0=src[:, q], in1=gains[:, q], op=MULT)
-                nc.sync.dma_start(
-                    out=out_view[i][:, 512 * h + 32 * q0 : 512 * h + 32 * (q0 + nq)], in_=ot[:, q].rearrange("p q t r -> p (q t r)")
-                )
+            ot = work.tile([P, 512], F32, name="ot", tag="ot", bufs=6, align_bytes=64)
+            nc.vector.tensor_tensor(out=ot[:, 0:width], in0=acc, in1=gain_bc[:, c], op=MULT)
+            nc.sync.dma_start(out=out_view[i][:, c], in_=ot[:, 0:width])
 
         nc.vector.memset(zs_raw[:].rearrange("p g n -> p (g n)").bitcast(I32), 0)
         load_xs()
@@ -312,77 +314,103 @@ def tile_coupled_newton_colouring_step_s11_kernel(tc, x_bytes, x_scale, y, z_wor
         widen(0)
         widen(1)
         zy(0, 0, (0, 1))
-        zy(0, 0, (2, 3))
+        turn(0)
+        turn(1)
         for t in range(4):
-            y_lay(0, 1, t, on_scalar)
+            y_lay(0, 1, t, on_scalar if t < 3 else on_vector)
             if t == 1:
                 c_out(0, 1, 0)
                 c_out(0, 1, 1)
+        zy(0, 0, (2, 3))
         for t in range(4):
             y_lay(1, 1, t, on_vector)
-        turn(0)
-        turn(1)
-        y_quant(0, 1, 0, 2)
-        y_quant(1, 1, 0, 4)
-        y_quant(0, 1, 2, 2)
         c_out(0, 1, 2)
         c_out(0, 1, 3)
+        for t0 in (0, 2):
+            y_quant(0, 1, t0, 2)
+            y_quant(1, 1, t0, 2)
+        c_out(0, 0, 0)
+        c_out(0, 0, 1)
         x_out(0)
         x_out(1)
         zy(1, 0, (0, 1))
-        for t1 in range(4):
-            c_out(0, 0, t1)
+        c_diag(0, 0)
+        c_diag(0, 1)
         zy(1, 0, (2, 3))
-        x_quant(0)
-        for t1 in range(4):
-            c_out(1, 0, t1)
+        c_out(0, 0, 2)
+        c_out(0, 0, 3)
         widen(2)
+        x_quant(0)
+        c_diag(0, 2)
+        c_diag(0, 3)
         widen(3)
-        c_quant(0, 0)
         c_quant(0, 1)
         widen(4)
+        for t1 in range(4):
+            c_out(1, 0, t1)
         v_mm(0, 0)
         v_out(0, 0)
         zy(1, 1, (0, 1))
-        c_out(1, 1, 0)
-        c_out(1, 1, 1)
         turn(2)
         turn(3)
+        c_out(1, 1, 0)
         x_out(2)
         x_out(3)
+        c_out(1, 1, 1)
         widen(5)
-        v_quant(0, 0)
-        v_mm(0, 1)
-        v_out(0, 1)
+        c_diag(1, 0)
         x_quant(1)
+        c_diag(1, 1)
+        v_mm(0, 1)
         x_perm(4)
         x_perm(5)
         zy(1, 1, (2, 3))
-        c_quant(1, 0)
         c_out(1, 1, 2)
         c_out(1, 1, 3)
+        v_out(0, 1)
+        c_quant(0, 0)
+        v_quant(0, 0)
+        c_quant(1, 0)
+        c_diag(1, 2)
+        c_diag(1, 3)
         v_quant(0, 1)
-        c_quant(1, 1)
 
-        for pair in range(1, PAIRS + 1):
-            if pair < PAIRS:
-                v_mm(pair, 0)
-                v_out(pair, 0)
-                turn(2 * pair + 2)
-                turn(2 * pair + 3)
-                x_out(2 * pair + 2)
-                x_out(2 * pair + 3)
-                widen(2 * pair + 4)
-                x_quant(pair + 1)
-                widen(2 * pair + 5)
-                v_quant(pair, 0)
-                v_mm(pair, 1)
-                v_out(pair, 1)
-                x_perm(2 * pair + 4)
-                x_perm(2 * pair + 5)
+        for pair in range(1, PAIRS - 1):
+            v_mm(pair, 0)
+            v_out(pair, 0)
+            turn(2 * pair + 2)
+            turn(2 * pair + 3)
+            x_out(2 * pair + 2)
+            x_out(2 * pair + 3)
+            if pair == 1:
+                c_quant(1, 1)
+            widen(2 * pair + 4)
+            v_quant(pair, 0)
+            x_quant(pair + 1)
+            v_mm(pair, 1)
+            v_out(pair, 1)
+            widen(2 * pair + 5)
+            x_perm(2 * pair + 4)
+            x_perm(2 * pair + 5)
             for s in range(2):
-                for h in range(2):
-                    o_mm(2 * pair - 2 + s, h)
-                    o_out(2 * pair - 2 + s, h, 2 if pair == PAIRS and s and h else 1)
-                if s == 0 and pair < PAIRS:
+                o_part(2 * pair - 2 + s, 0, 512)
+                o_part(2 * pair - 2 + s, 512, 512)
+                if s == 0:
                     v_quant(pair, 1)
+        last = PAIRS - 1
+        v_mm(last, 0)
+        v_out(last, 0)
+        o_part(TILES - 4, 0, 512)
+        v_mm(last, 1)
+        v_out(last, 1)
+        v_quant(last, 0)
+        o_part(TILES - 4, 512, 512)
+        v_quant(last, 1, 0, 1)
+        o_part(TILES - 3, 0, 512)
+        v_quant(last, 1, 1, 1)
+        o_part(TILES - 3, 512, 512)
+        o_part(TILES - 2, 0, 512)
+        o_part(TILES - 2, 512, 512)
+        o_part(TILES - 1, 0, 512)
+        o_part(TILES - 1, 512, 256)
+        o_part(TILES - 1, 768, 256)

@@ -103,12 +103,12 @@ def tile_coupled_newton_colouring_step_s11_kernel(tc, x_bytes, x_scale, y, z_wor
         yi = {}
         ci = {}
 
-        def y_lay(kp, h, t, copy):
+        def y_lay(kp, h, t0, nt, copy):
             if (kp, h) not in yi:
                 yi[kp, h] = keep.tile([P, 512, 4], BF16, name=f"yi_{kp}{h}", align_bytes=64)
             dst = yi[kp, h][:].rearrange("p (t q r) j -> p t q r j", t=4, r=8)
             raw = y_raw[kp, h][:].rearrange("p j (q t r) -> p t q r j", t=4, r=8)
-            copy(out=dst[:, t], in_=raw[:, t])
+            copy(out=dst[:, t0 : t0 + nt], in_=raw[:, t0 : t0 + nt])
 
         def y_quant(kp, h, t0, nt):
             lo, hi = 128 * t0, 128 * (t0 + nt)
@@ -118,14 +118,16 @@ def tile_coupled_newton_colouring_step_s11_kernel(tc, x_bytes, x_scale, y, z_wor
                 in_=yi[kp, h][:, lo:hi].rearrange("p n j -> p (n j)"),
             )
 
-        def z_lay(kp, g):
+        def z_lay_words(kp):
             nc.vector.tensor_copy(
-                out=zq[:, kp, N * g : N * g + N].bitcast(I32).rearrange("p (t q r) -> p t q r", t=4, r=4),
-                in_=zw_raw[kp][:, N * g : N * g + N].bitcast(I32).rearrange("p (q t r) -> p t q r", t=4, r=4),
+                out=zq[:, kp].bitcast(I32).rearrange("p (g t q r) -> p g t q r", g=2, t=4, r=4),
+                in_=zw_raw[kp][:].bitcast(I32).rearrange("p (g q t r) -> p g t q r", g=2, t=4, r=4),
             )
+
+        def z_lay_scales():
             nc.vector.tensor_copy(
-                out=zs[:, kp, 512 * g : 512 * g + 512].bitcast(I32).rearrange("p (t q r) -> p t q r", t=4, r=2),
-                in_=zs_raw[:, kp, 512 * g : 512 * g + 512].bitcast(I32).rearrange("p (q t r) -> p t q r", t=4, r=2),
+                out=zs[:].rearrange("p k n -> p (k n)").bitcast(I32).rearrange("p (g t q r) -> p g t q r", g=4, t=4, r=2),
+                in_=zs_raw[:].rearrange("p k n -> p (k n)").bitcast(I32).rearrange("p (g q t r) -> p g t q r", g=4, t=4, r=2),
             )
 
         xw, xp, xt, xi, xq, xqs = {}, {}, {}, {}, {}, {}
@@ -201,23 +203,36 @@ def tile_coupled_newton_colouring_step_s11_kernel(tc, x_bytes, x_scale, y, z_wor
                 for t1 in t1s:
                     zy_pass(h, t1, g, t, kp, kp == 0 and t == 0, kp == 1 and t == 3)
 
-        def c_out(h, g, t1):
+        planes = {}
+
+        def c_dst(h, g, t1):
             if (g, h) not in ci:
                 ci[g, h] = keep.tile([P, 512, 4], BF16, name=f"ci_{g}{h}", align_bytes=64)
+            return ci[g, h][:].rearrange("p (q t r) f -> p t q r f", t=4, r=8)[:, t1]
+
+        def c_out(h, g, t1, vector=False):
             src = zps[h, t1, g][:].rearrange("p f (q r) -> p q r f", r=8)
-            dst = ci[g, h][:].rearrange("p (q t r) f -> p t q r f", t=4, r=8)[:, t1]
-            nc.scalar.activation(out=dst, in_=src, func=COPY, scale=-0.5)
+            if vector:
+                nc.vector.tensor_scalar(out=c_dst(h, g, t1), in0=src, scalar1=-0.5, scalar2=None, op0=MULT)
+            else:
+                nc.scalar.activation(out=c_dst(h, g, t1), in_=src, func=COPY, scale=-0.5)
+
+        def c_plane(h, t1):
+            planes[h, t1] = work.tile([P, P], F32, name="plane", tag="plane", bufs=4, align_bytes=64)
+            nc.scalar.activation(out=planes[h, t1][:], in_=zps[h, t1, h][:, t1, :], func=COPY, scale=-0.5)
 
         def c_diag(h, t1):
-            dst = ci[h, h][:].rearrange("p (q t r) f -> p t q r f", t=4, r=8)[:, t1, :, :, t1]
-            nc.vector.scalar_tensor_tensor(
-                out=dst,
-                in0=zps[h, t1, h][:, t1, :].rearrange("p (q r) -> p q r", r=8),
-                scalar=-0.5,
+            nc.gpsimd.tensor_tensor(
+                out=c_dst(h, h, t1)[:, :, :, t1],
+                in0=planes[h, t1][:].rearrange("p (q r) -> p q r", r=8),
                 in1=eye15[:].rearrange("p (q r) -> p q r", r=8),
-                op0=MULT,
-                op1=ADD,
+                op=ADD,
             )
+
+        def c_full(h, t1, vector=False):
+            c_plane(h, t1)
+            c_out(h, h, t1, vector)
+            c_diag(h, t1)
 
         def c_quant(h, g):
             nc.vector.quantize_mx(
@@ -246,44 +261,52 @@ def tile_coupled_newton_colouring_step_s11_kernel(tc, x_bytes, x_scale, y, z_wor
                             stop=(kp == 1),
                         )
 
-        def v_out(pair, g):
-            vi[pair, g] = work.tile([P, 2, P, 4], BF16, name="vi", tag="vi", bufs=4, align_bytes=64)
-            for s in range(2):
-                nc.scalar.copy(out=vi[pair, g][:, s], in_=vps[pair, g, s][:].rearrange("p t m -> p m t"))
+        def v_out(pair, g, tiles=(0, 1)):
+            if pair not in vi:
+                vi[pair] = work.tile([P, 2, 2, P, 4], BF16, name="vi", tag="vi", bufs=2, align_bytes=64)
+            for s in tiles:
+                nc.scalar.copy(out=vi[pair][:, g, s], in_=vps[pair, g, s][:].rearrange("p t m -> p m t"))
 
-        def v_quant(pair, g, s0=0, ns=2):
-            if (pair, g) not in vq:
-                vq[pair, g] = work.tile([P, 2 * P], U32, name="vq", tag="vq", bufs=2 * PAIRS, align_bytes=64)
-                vqs[pair, g] = work.tile([P, 2 * P], U8, name="vqs", tag="vqs", bufs=2 * PAIRS, align_bytes=64)
-            c = slice(P * s0, P * (s0 + ns))
+        def v_quant(pair, j0=0, nj=4):
+            if pair not in vq:
+                vq[pair] = work.tile([P, 4 * P], U32, name="vq", tag="vq", bufs=3, align_bytes=64)
+                vqs[pair] = work.tile([P, 4 * P], U8, name="vqs", tag="vqs", bufs=3, align_bytes=64)
+            c = slice(P * j0, P * (j0 + nj))
             nc.vector.quantize_mx(
-                out=vq[pair, g][:, c].bitcast(FP8X4), scales=vqs[pair, g][:, c], in_=vi[pair, g][:, s0 : s0 + ns].rearrange("p s m t -> p (s m t)")
+                out=vq[pair][:, c].bitcast(FP8X4),
+                scales=vqs[pair][:, c],
+                in_=vi[pair][:].rearrange("p g s m t -> p (g s m t)")[:, 4 * P * j0 : 4 * P * (j0 + nj)],
             )
 
         out_view = out.rearrange("(i p) n -> i p n", p=P)
 
-        def o_part(i, c0, width):
+        def o_part(i, c0, width, pool=False):
             ps = bank()
             acc = ps[:].rearrange("p a b -> p (a b)")[:, 0:width]
-            m = slice(P * (i % 2), P * (i % 2) + P)
             c = slice(c0, c0 + width)
             for g in range(2):
+                m = slice(P * (2 * g + i % 2), P * (2 * g + i % 2 + 1))
                 nc.tensor.matmul_mx(
                     out=acc,
-                    lhsT=vq[i // 2, g][:, m].bitcast(FP8X4),
-                    lhsT_scale=vqs[i // 2, g][:, m],
+                    lhsT=vq[i // 2][:, m].bitcast(FP8X4),
+                    lhsT_scale=vqs[i // 2][:, m],
                     rhs=cq[:, g, c].bitcast(FP8X4),
                     rhs_scale=cs[:, g, c],
                     start=(g == 0),
                     stop=(g == 1),
                 )
             ot = work.tile([P, 512], F32, name="ot", tag="ot", bufs=6, align_bytes=64)
-            nc.vector.tensor_tensor(out=ot[:, 0:width], in0=acc, in1=gain_bc[:, c], op=MULT)
+            if pool:
+                stage = work.tile([P, 512], F32, name="stage", tag="stage", bufs=2, align_bytes=64)
+                nc.scalar.copy(out=stage[:, 0:width], in_=acc)
+                nc.gpsimd.tensor_tensor(out=ot[:, 0:width], in0=stage[:, 0:width], in1=gain_bc[:, c], op=MULT)
+            else:
+                nc.vector.tensor_tensor(out=ot[:, 0:width], in0=acc, in1=gain_bc[:, c], op=MULT)
             nc.sync.dma_start(out=out_view[i][:, c], in_=ot[:, 0:width])
 
         nc.vector.memset(zs_raw[:].rearrange("p g n -> p (g n)").bitcast(I32), 0)
-        load_xs()
         load_y(0, 0)
+        load_xs()
         load_zs()
         load_z(0)
         load_y(1, 0)
@@ -299,81 +322,76 @@ def tile_coupled_newton_colouring_step_s11_kernel(tc, x_bytes, x_scale, y, z_wor
         constants()
         xs_turn(0)
         xs_turn(1)
-        xs_out(0, on_scalar)
-        xs_out(1, on_scalar)
 
         for kp in range(2):
-            for t in range(4):
-                y_lay(kp, 0, t, on_scalar if t == 3 else on_vector)
+            y_lay(kp, 0, 0, 2, on_vector)
+            y_lay(kp, 0, 3, 1, on_scalar)
+            y_lay(kp, 0, 2, 1, on_vector)
             y_quant(kp, 0, 0, 2)
-            z_lay(kp, 1)
+            if kp == 0:
+                z_lay_scales()
+                xs_out(0, on_scalar)
+                xs_out(1, on_scalar)
+            z_lay_words(kp)
             zy_half(0, 1, (0, 1), kp)
             y_quant(kp, 0, 2, 2)
             zy_half(0, 1, (2, 3), kp)
-            z_lay(kp, 0)
         widen(0)
         widen(1)
         zy(0, 0, (0, 1))
         turn(0)
         turn(1)
-        for t in range(4):
-            y_lay(0, 1, t, on_scalar if t < 3 else on_vector)
-            if t == 1:
-                c_out(0, 1, 0)
-                c_out(0, 1, 1)
+        y_lay(0, 1, 0, 2, on_scalar)
+        c_out(0, 1, 0)
+        c_out(0, 1, 1)
+        y_lay(0, 1, 2, 2, on_vector)
         zy(0, 0, (2, 3))
-        for t in range(4):
-            y_lay(1, 1, t, on_vector)
+        y_lay(1, 1, 0, 4, on_vector)
         c_out(0, 1, 2)
         c_out(0, 1, 3)
         for t0 in (0, 2):
             y_quant(0, 1, t0, 2)
             y_quant(1, 1, t0, 2)
-        c_out(0, 0, 0)
-        c_out(0, 0, 1)
+        c_full(0, 0)
+        c_full(0, 1)
         x_out(0)
         x_out(1)
         zy(1, 0, (0, 1))
-        c_diag(0, 0)
-        c_diag(0, 1)
-        zy(1, 0, (2, 3))
-        c_out(0, 0, 2)
-        c_out(0, 0, 3)
         widen(2)
+        zy(1, 0, (2, 3))
+        c_full(0, 2)
+        c_full(0, 3)
         x_quant(0)
-        c_diag(0, 2)
-        c_diag(0, 3)
         widen(3)
+        for t1 in range(4):
+            c_out(1, 0, t1, t1 == 3)
+        x_perm(2)
+        x_perm(3)
         c_quant(0, 1)
         widen(4)
-        for t1 in range(4):
-            c_out(1, 0, t1)
         v_mm(0, 0)
         v_out(0, 0)
         zy(1, 1, (0, 1))
         turn(2)
         turn(3)
-        c_out(1, 1, 0)
         x_out(2)
         x_out(3)
-        c_out(1, 1, 1)
+        c_full(1, 0)
+        c_full(1, 1)
         widen(5)
-        c_diag(1, 0)
-        x_quant(1)
-        c_diag(1, 1)
-        v_mm(0, 1)
-        x_perm(4)
-        x_perm(5)
-        zy(1, 1, (2, 3))
-        c_out(1, 1, 2)
-        c_out(1, 1, 3)
-        v_out(0, 1)
         c_quant(0, 0)
-        v_quant(0, 0)
+        x_quant(1)
+        v_mm(0, 1)
+        zy(1, 1, (2, 3))
         c_quant(1, 0)
-        c_diag(1, 2)
-        c_diag(1, 3)
-        v_quant(0, 1)
+        x_perm(4)
+        c_full(1, 2, True)
+        c_full(1, 3, True)
+        x_perm(5)
+        v_out(0, 1)
+        widen(6)
+        v_quant(0)
+        c_quant(1, 1)
 
         for pair in range(1, PAIRS - 1):
             v_mm(pair, 0)
@@ -382,33 +400,30 @@ def tile_coupled_newton_colouring_step_s11_kernel(tc, x_bytes, x_scale, y, z_wor
             turn(2 * pair + 3)
             x_out(2 * pair + 2)
             x_out(2 * pair + 3)
-            if pair == 1:
-                c_quant(1, 1)
-            widen(2 * pair + 4)
-            v_quant(pair, 0)
+            widen(2 * pair + 5)
             x_quant(pair + 1)
             v_mm(pair, 1)
-            v_out(pair, 1)
-            widen(2 * pair + 5)
+            v_out(pair, 1, (0,))
+            o_part(2 * pair - 2, 0, 512, False)
+            v_out(pair, 1, (1,))
             x_perm(2 * pair + 4)
             x_perm(2 * pair + 5)
-            for s in range(2):
-                o_part(2 * pair - 2 + s, 0, 512)
-                o_part(2 * pair - 2 + s, 512, 512)
-                if s == 0:
-                    v_quant(pair, 1)
+            o_part(2 * pair - 1, 0, 512)
+            o_part(2 * pair - 2, 512, 512)
+            o_part(2 * pair - 1, 512, 512)
+            v_quant(pair)
+            widen(2 * pair + 6)
         last = PAIRS - 1
         v_mm(last, 0)
-        v_out(last, 0)
-        o_part(TILES - 4, 0, 512)
         v_mm(last, 1)
+        v_out(last, 0)
         v_out(last, 1)
-        v_quant(last, 0)
-        o_part(TILES - 4, 512, 512)
-        v_quant(last, 1, 0, 1)
+        v_quant(last, 0, 2)
+        o_part(TILES - 4, 0, 512)
+        v_quant(last, 2, 2)
+        o_part(TILES - 4, 512, 512, False)
         o_part(TILES - 3, 0, 512)
-        v_quant(last, 1, 1, 1)
-        o_part(TILES - 3, 512, 512)
+        o_part(TILES - 3, 512, 512, False)
         o_part(TILES - 2, 0, 512)
         o_part(TILES - 2, 512, 512)
         o_part(TILES - 1, 0, 512)

@@ -280,9 +280,8 @@ def tile_coupled_newton_colouring_step_s11_kernel(tc, x_bytes, x_scale, y, z_wor
 
         out_view = out.rearrange("(i p) n -> i p n", p=P)
 
-        def o_part(i, c0, width, pool=False):
-            ps = bank()
-            acc = ps[:].rearrange("p a b -> p (a b)")[:, 0:width]
+        def o_mm(i, c0, width):
+            acc = bank()[:].rearrange("p a b -> p (a b)")[:, 0:width]
             c = slice(c0, c0 + width)
             for g in range(2):
                 m = slice(P * (2 * g + i % 2), P * (2 * g + i % 2 + 1))
@@ -295,14 +294,25 @@ def tile_coupled_newton_colouring_step_s11_kernel(tc, x_bytes, x_scale, y, z_wor
                     start=(g == 0),
                     stop=(g == 1),
                 )
-            ot = work.tile([P, 512], F32, name="ot", tag="ot", bufs=6, align_bytes=64)
-            if pool:
-                stage = work.tile([P, 512], F32, name="stage", tag="stage", bufs=2, align_bytes=64)
-                nc.scalar.copy(out=stage[:, 0:width], in_=acc)
-                nc.gpsimd.tensor_tensor(out=ot[:, 0:width], in0=stage[:, 0:width], in1=gain_bc[:, c], op=MULT)
-            else:
-                nc.vector.tensor_tensor(out=ot[:, 0:width], in0=acc, in1=gain_bc[:, c], op=MULT)
-            nc.sync.dma_start(out=out_view[i][:, c], in_=ot[:, 0:width])
+            return acc
+
+        def o_part(i, c0, width):
+            acc = o_mm(i, c0, width)
+            ot = work.tile([P, 512], F32, name="ot", tag="ot", bufs=8, align_bytes=64)
+            nc.vector.tensor_tensor(out=ot[:, 0:width], in0=acc, in1=gain_bc[:, c0 : c0 + width], op=MULT)
+            nc.sync.dma_start(out=out_view[i][:, c0 : c0 + width], in_=ot[:, 0:width])
+
+        held = {}
+
+        def o_pool(i, c0):
+            acc = o_mm(i, c0, 512)
+            stage = work.tile([P, 512], F32, name="stage", tag="stage", bufs=2, align_bytes=64)
+            nc.scalar.copy(out=stage[:], in_=acc)
+            held[i] = work.tile([P, 512], F32, name="og", tag="og", bufs=2, align_bytes=64)
+            nc.gpsimd.tensor_tensor(out=held[i][:], in0=stage[:], in1=gain_bc[:, c0 : c0 + 512], op=MULT)
+
+        def o_pool_store(i, c0):
+            nc.sync.dma_start(out=out_view[i][:, c0 : c0 + 512], in_=held[i][:])
 
         nc.vector.memset(zs_raw[:].rearrange("p g n -> p (g n)").bitcast(I32), 0)
         load_y(0, 0)
@@ -404,12 +414,13 @@ def tile_coupled_newton_colouring_step_s11_kernel(tc, x_bytes, x_scale, y, z_wor
             x_quant(pair + 1)
             v_mm(pair, 1)
             v_out(pair, 1, (0,))
-            o_part(2 * pair - 2, 0, 512, False)
+            o_pool(2 * pair - 2, 0)
             v_out(pair, 1, (1,))
             x_perm(2 * pair + 4)
             x_perm(2 * pair + 5)
             o_part(2 * pair - 1, 0, 512)
             o_part(2 * pair - 2, 512, 512)
+            o_pool_store(2 * pair - 2, 0)
             o_part(2 * pair - 1, 512, 512)
             v_quant(pair)
             widen(2 * pair + 6)
@@ -421,11 +432,13 @@ def tile_coupled_newton_colouring_step_s11_kernel(tc, x_bytes, x_scale, y, z_wor
         v_quant(last, 0, 2)
         o_part(TILES - 4, 0, 512)
         v_quant(last, 2, 2)
-        o_part(TILES - 4, 512, 512, False)
+        o_pool(TILES - 4, 512)
         o_part(TILES - 3, 0, 512)
-        o_part(TILES - 3, 512, 512, False)
+        o_pool(TILES - 3, 512)
         o_part(TILES - 2, 0, 512)
+        o_pool_store(TILES - 4, 512)
         o_part(TILES - 2, 512, 512)
         o_part(TILES - 1, 0, 512)
+        o_pool_store(TILES - 3, 512)
         o_part(TILES - 1, 512, 256)
         o_part(TILES - 1, 768, 256)

@@ -190,17 +190,17 @@ def tile_coupled_newton_colouring_step_s11_kernel(tc, x_bytes, x_scale, y, z_wor
         def zy(h, g, t1s):
             for t1 in t1s:
                 zps[h, t1, g] = bank()
-            for t in range(4):
-                for kp in range(2):
-                    for t1 in t1s:
+            for t1 in t1s:
+                for t in range(4):
+                    for kp in range(2):
                         zy_pass(h, t1, g, t, kp, kp == 0, kp == 1)
 
         def zy_half(h, g, t1s, kp):
             for t1 in t1s:
                 if kp == 0:
                     zps[h, t1, g] = bank()
-            for t in range(4):
-                for t1 in t1s:
+            for t1 in t1s:
+                for t in range(4):
                     zy_pass(h, t1, g, t, kp, kp == 0 and t == 0, kp == 1 and t == 3)
 
         planes = {}
@@ -229,6 +229,16 @@ def tile_coupled_newton_colouring_step_s11_kernel(tc, x_bytes, x_scale, y, z_wor
                 op=ADD,
             )
 
+        def c_diag_v(h, t1):
+            nc.vector.scalar_tensor_tensor(
+                out=c_dst(h, h, t1)[:, :, :, t1],
+                in0=zps[h, t1, h][:, t1, :].rearrange("p (q r) -> p q r", r=8),
+                scalar=-0.5,
+                in1=eye15[:].rearrange("p (q r) -> p q r", r=8),
+                op0=MULT,
+                op1=ADD,
+            )
+
         def c_full(h, t1, vector=False):
             c_plane(h, t1)
             c_out(h, h, t1, vector)
@@ -243,13 +253,12 @@ def tile_coupled_newton_colouring_step_s11_kernel(tc, x_bytes, x_scale, y, z_wor
 
         vps, vi, vq, vqs = {}, {}, {}, {}
 
-        def v_mm(pair, g):
-            for s in range(2):
+        def v_mm(pair, g, tiles=(0, 1)):
+            for s in tiles:
                 vps[pair, g, s] = bank()
-            for t in range(4):
-                c0 = 512 * g + 128 * t
-                for kp in range(2):
-                    for s in range(2):
+                for t in range(4):
+                    for kp in range(2):
+                        c0 = 512 * g + 128 * t
                         c = slice(P * (2 * s + kp), P * (2 * s + kp + 1))
                         nc.tensor.matmul_mx(
                             out=vps[pair, g, s][:, t, :],
@@ -265,7 +274,7 @@ def tile_coupled_newton_colouring_step_s11_kernel(tc, x_bytes, x_scale, y, z_wor
             if pair not in vi:
                 vi[pair] = work.tile([P, 2, 2, P, 4], BF16, name="vi", tag="vi", bufs=2, align_bytes=64)
             for s in tiles:
-                nc.scalar.copy(out=vi[pair][:, g, s], in_=vps[pair, g, s][:].rearrange("p t m -> p m t"))
+                nc.scalar.copy(out=vi[pair][:, s, g], in_=vps[pair, g, s][:].rearrange("p t m -> p m t"))
 
         def v_quant(pair, j0=0, nj=4):
             if pair not in vq:
@@ -284,7 +293,7 @@ def tile_coupled_newton_colouring_step_s11_kernel(tc, x_bytes, x_scale, y, z_wor
             acc = bank()[:].rearrange("p a b -> p (a b)")[:, 0:width]
             c = slice(c0, c0 + width)
             for g in range(2):
-                m = slice(P * (2 * g + i % 2), P * (2 * g + i % 2 + 1))
+                m = slice(P * (2 * (i % 2) + g), P * (2 * (i % 2) + g + 1))
                 nc.tensor.matmul_mx(
                     out=acc,
                     lhsT=vq[i // 2][:, m].bitcast(FP8X4),
@@ -315,38 +324,43 @@ def tile_coupled_newton_colouring_step_s11_kernel(tc, x_bytes, x_scale, y, z_wor
             nc.sync.dma_start(out=out_view[i][:, c0 : c0 + 512], in_=held[i][:])
 
         nc.vector.memset(zs_raw[:].rearrange("p g n -> p (g n)").bitcast(I32), 0)
-        load_y(0, 0)
         load_xs()
+        load_y(0, 0)
         load_zs()
         load_z(0)
+        load_x_pair(0)
         load_y(1, 0)
         load_z(1)
-        load_x_pair(0)
         load_y(0, 1)
         load_y(1, 1)
         load_x_pair(1)
         load_x_pair(2)
         load_gain()
-        for pair in range(3, PAIRS):
-            load_x_pair(pair)
+        load_x_pair(3)
+        load_x_pair(4)
+        load_x_pair(5)
         constants()
         xs_turn(0)
         xs_turn(1)
-
-        for kp in range(2):
-            y_lay(kp, 0, 0, 2, on_vector)
-            y_lay(kp, 0, 3, 1, on_scalar)
-            y_lay(kp, 0, 2, 1, on_vector)
-            y_quant(kp, 0, 0, 2)
-            if kp == 0:
-                z_lay_scales()
-                xs_out(0, on_scalar)
-                xs_out(1, on_scalar)
-            z_lay_words(kp)
-            zy_half(0, 1, (0, 1), kp)
-            y_quant(kp, 0, 2, 2)
-            zy_half(0, 1, (2, 3), kp)
+        xs_out(0, on_scalar)
+        xs_out(1, on_scalar)
+        y_lay(0, 0, 0, 2, on_vector)
+        y_lay(0, 0, 3, 1, on_scalar)
+        y_lay(0, 0, 2, 1, on_vector)
+        y_quant(0, 0, 0, 2)
+        z_lay_scales()
+        z_lay_words(0)
+        zy_half(0, 1, (0, 1), 0)
+        y_quant(0, 0, 2, 2)
+        zy_half(0, 1, (2, 3), 0)
         widen(0)
+        y_lay(1, 0, 0, 2, on_vector)
+        y_lay(1, 0, 2, 2, on_scalar)
+        z_lay_words(1)
+        y_quant(1, 0, 0, 2)
+        zy_half(0, 1, (0, 1), 1)
+        y_quant(1, 0, 2, 2)
+        zy_half(0, 1, (2, 3), 1)
         widen(1)
         zy(0, 0, (0, 1))
         turn(0)
@@ -359,24 +373,28 @@ def tile_coupled_newton_colouring_step_s11_kernel(tc, x_bytes, x_scale, y, z_wor
         y_lay(1, 1, 0, 4, on_vector)
         c_out(0, 1, 2)
         c_out(0, 1, 3)
-        for t0 in (0, 2):
-            y_quant(0, 1, t0, 2)
-            y_quant(1, 1, t0, 2)
-        c_full(0, 0)
-        c_full(0, 1)
+        y_quant(0, 1, 0, 4)
+        y_quant(1, 1, 0, 2)
+        y_quant(1, 1, 2, 2)
+        c_out(0, 0, 0)
+        c_out(0, 0, 1)
         x_out(0)
         x_out(1)
         zy(1, 0, (0, 1))
-        widen(2)
+        c_diag_v(0, 0)
+        c_diag_v(0, 1)
         zy(1, 0, (2, 3))
-        c_full(0, 2)
-        c_full(0, 3)
+        c_out(0, 0, 2)
+        c_out(0, 0, 3)
+        widen(2)
         x_quant(0)
+        c_diag_v(0, 2)
+        c_diag_v(0, 3)
         widen(3)
-        for t1 in range(4):
-            c_out(1, 0, t1, t1 == 3)
-        x_perm(2)
-        x_perm(3)
+        c_out(1, 0, 0)
+        c_out(1, 0, 1)
+        c_out(1, 0, 2)
+        c_out(1, 0, 3)
         c_quant(0, 1)
         widen(4)
         v_mm(0, 0)
@@ -384,34 +402,35 @@ def tile_coupled_newton_colouring_step_s11_kernel(tc, x_bytes, x_scale, y, z_wor
         zy(1, 1, (0, 1))
         turn(2)
         turn(3)
+        c_out(1, 1, 0)
         x_out(2)
         x_out(3)
-        c_full(1, 0)
-        c_full(1, 1)
+        c_out(1, 1, 1)
         widen(5)
-        c_quant(0, 0)
+        c_diag_v(1, 0)
         x_quant(1)
+        c_diag_v(1, 1)
         v_mm(0, 1)
         zy(1, 1, (2, 3))
-        c_quant(1, 0)
-        x_perm(4)
-        c_full(1, 2, True)
-        c_full(1, 3, True)
-        x_perm(5)
+        c_out(1, 1, 2)
+        c_out(1, 1, 3)
         v_out(0, 1)
-        widen(6)
+        c_quant(0, 0)
+        c_quant(1, 0)
+        c_diag_v(1, 2)
+        c_diag_v(1, 3)
         v_quant(0)
         c_quant(1, 1)
-
-        for pair in range(1, PAIRS - 1):
+        for pair in range(1, PAIRS - 2):
             v_mm(pair, 0)
             v_out(pair, 0)
             turn(2 * pair + 2)
             turn(2 * pair + 3)
             x_out(2 * pair + 2)
             x_out(2 * pair + 3)
-            widen(2 * pair + 5)
+            widen(2 * pair + 4)
             x_quant(pair + 1)
+            widen(2 * pair + 5)
             v_mm(pair, 1)
             v_out(pair, 1, (0,))
             o_pool(2 * pair - 2, 0)
@@ -423,22 +442,38 @@ def tile_coupled_newton_colouring_step_s11_kernel(tc, x_bytes, x_scale, y, z_wor
             o_pool_store(2 * pair - 2, 0)
             o_part(2 * pair - 1, 512, 512)
             v_quant(pair)
-            widen(2 * pair + 6)
         last = PAIRS - 1
-        v_mm(last, 0)
-        v_mm(last, 1)
-        v_out(last, 0)
-        v_out(last, 1)
+        v_mm(4, 0)
+        v_out(4, 0)
+        turn(10)
+        turn(11)
+        x_out(10)
+        x_out(11)
+        x_quant(5)
+        v_mm(4, 1)
+        v_out(4, 1)
+        o_part(6, 0, 512)
+        o_part(7, 0, 512)
+        v_quant(4)
+        o_part(6, 512, 512)
+        o_part(7, 512, 512)
+        v_mm(last, 0, (0,))
+        v_mm(last, 1, (0,))
+        v_out(last, 0, (0,))
+        v_out(last, 1, (0,))
+        o_part(8, 0, 512)
+        o_part(8, 512, 512)
         v_quant(last, 0, 2)
-        o_part(TILES - 4, 0, 512)
-        v_quant(last, 2, 2)
-        o_pool(TILES - 4, 512)
-        o_part(TILES - 3, 0, 512)
-        o_pool(TILES - 3, 512)
-        o_part(TILES - 2, 0, 512)
-        o_pool_store(TILES - 4, 512)
-        o_part(TILES - 2, 512, 512)
-        o_part(TILES - 1, 0, 512)
-        o_pool_store(TILES - 3, 512)
-        o_part(TILES - 1, 512, 256)
-        o_part(TILES - 1, 768, 256)
+        o_part(9, 0, 512)
+        v_mm(last, 0, (1,))
+        v_mm(last, 1, (1,))
+        v_out(last, 0, (1,))
+        v_out(last, 1, (1,))
+        v_quant(last, 2, 1)
+        o_part(9, 512, 512)
+        v_quant(last, 3, 1)
+        o_part(10, 0, 512)
+        o_part(10, 512, 512)
+        o_part(11, 0, 512)
+        o_part(11, 512, 256)
+        o_part(11, 768, 256)

@@ -75,13 +75,14 @@ def tile_coupled_newton_colouring_step_s11_kernel(tc, x_bytes, x_scale, y, z_wor
             nc.sync.dma_start(out=gain_bc[:], in_=gain.partition_broadcast(P))
 
         ident = keep.tile([P, P], F32, name="ident", align_bytes=64)
-        eye15 = keep.tile([P, P], F32, name="eye15", align_bytes=64)
+        eye15 = keep.tile([P, P, 8], BF16, name="eye15", align_bytes=64)
         xsb = keep.tile([P, N], F32, name="xsb", align_bytes=64)
         xs_ps = {}
 
         def constants():
+            nc.vector.memset(eye15[:].rearrange("p n c -> p (n c)").bitcast(I32), 0)
             make_identity(nc, ident[:])
-            nc.gpsimd.tensor_scalar(out=eye15[:], in0=ident[:], scalar1=1.5, scalar2=0.0, op0=MULT, op1=ADD)
+            nc.vector.tensor_scalar(out=eye15[:, :, 3], in0=ident[:], scalar1=1.5, scalar2=None, op0=MULT)
 
         def xs_turn(half):
             xs_ps[half] = bank()
@@ -136,6 +137,17 @@ def tile_coupled_newton_colouring_step_s11_kernel(tc, x_bytes, x_scale, y, z_wor
             if i < TILES:
                 xw[i] = work.tile([P, N], BF16, name="xw", tag="xw", bufs=8, align_bytes=64)
                 nc.vector.tensor_tensor(out=xw[i][:], in0=xb[i].bitcast(FP8), in1=xsb[:], op=MULT)
+
+        plain = {}
+
+        def cast(i):
+            plain[i] = keep.tile([P, N], BF16, name=f"plain_{i}", align_bytes=64)
+            nc.scalar.copy(out=plain[i][:], in_=xb[i].bitcast(FP8))
+            xw[i] = keep.tile([P, N], BF16, name=f"xw_{i}", align_bytes=64)
+
+        def scale_pool(i, g):
+            c = slice(512 * g, 512 * g + 512)
+            nc.gpsimd.tensor_tensor(out=xw[i][:, c], in0=plain[i][:, c], in1=xsb[:, c], op=MULT)
 
         def x_perm(i):
             if i < TILES:
@@ -229,12 +241,17 @@ def tile_coupled_newton_colouring_step_s11_kernel(tc, x_bytes, x_scale, y, z_wor
                 op=ADD,
             )
 
+        def c_whole(h, t1):
+            src = zps[h, t1, h][:].rearrange("p f (q r) -> p q r f", r=8)
+            eye = eye15[:, :, 3 - t1 : 7 - t1].rearrange("p (q r) f -> p q r f", r=8)
+            nc.vector.scalar_tensor_tensor(out=c_dst(h, h, t1), in0=src, scalar=-0.5, in1=eye, op0=MULT, op1=ADD)
+
         def c_diag_v(h, t1):
             nc.vector.scalar_tensor_tensor(
                 out=c_dst(h, h, t1)[:, :, :, t1],
                 in0=zps[h, t1, h][:, t1, :].rearrange("p (q r) -> p q r", r=8),
                 scalar=-0.5,
-                in1=eye15[:].rearrange("p (q r) -> p q r", r=8),
+                in1=eye15[:, :, 3].rearrange("p (q r) -> p q r", r=8),
                 op0=MULT,
                 op1=ADD,
             )
@@ -345,17 +362,17 @@ def tile_coupled_newton_colouring_step_s11_kernel(tc, x_bytes, x_scale, y, z_wor
         xs_out(0, on_scalar)
         xs_out(1, on_scalar)
         y_lay(0, 0, 0, 2, on_vector)
-        y_lay(0, 0, 3, 1, on_scalar)
-        y_lay(0, 0, 2, 1, on_vector)
-        y_quant(0, 0, 0, 2)
+        y_lay(0, 0, 2, 2, on_scalar)
         z_lay_scales()
+        y_quant(0, 0, 0, 2)
         z_lay_words(0)
         zy_half(0, 1, (0, 1), 0)
+        widen(0)
         y_quant(0, 0, 2, 2)
         zy_half(0, 1, (2, 3), 0)
-        widen(0)
         y_lay(1, 0, 0, 2, on_vector)
         y_lay(1, 0, 2, 2, on_scalar)
+        x_perm(0)
         z_lay_words(1)
         y_quant(1, 0, 0, 2)
         zy_half(0, 1, (0, 1), 1)
@@ -371,54 +388,54 @@ def tile_coupled_newton_colouring_step_s11_kernel(tc, x_bytes, x_scale, y, z_wor
         y_lay(0, 1, 2, 2, on_vector)
         zy(0, 0, (2, 3))
         y_lay(1, 1, 0, 4, on_vector)
+        cast(3)
         c_out(0, 1, 2)
         c_out(0, 1, 3)
         y_quant(0, 1, 0, 4)
         y_quant(1, 1, 0, 2)
         y_quant(1, 1, 2, 2)
-        c_out(0, 0, 0)
-        c_out(0, 0, 1)
         x_out(0)
         x_out(1)
         zy(1, 0, (0, 1))
-        c_diag_v(0, 0)
-        c_diag_v(0, 1)
+        scale_pool(3, 0)
+        scale_pool(3, 1)
+        c_whole(0, 0)
+        c_whole(0, 1)
         zy(1, 0, (2, 3))
-        c_out(0, 0, 2)
-        c_out(0, 0, 3)
         widen(2)
         x_quant(0)
-        c_diag_v(0, 2)
-        c_diag_v(0, 3)
-        widen(3)
+        c_whole(0, 2)
+        c_whole(0, 3)
         c_out(1, 0, 0)
         c_out(1, 0, 1)
+        x_perm(2)
         c_out(1, 0, 2)
         c_out(1, 0, 3)
-        c_quant(0, 1)
         widen(4)
+        c_quant(0, 1)
         v_mm(0, 0)
         v_out(0, 0)
         zy(1, 1, (0, 1))
         turn(2)
         turn(3)
-        c_out(1, 1, 0)
+        cast(6)
         x_out(2)
         x_out(3)
-        c_out(1, 1, 1)
         widen(5)
-        c_diag_v(1, 0)
+        c_quant(0, 0)
+        scale_pool(6, 0)
+        scale_pool(6, 1)
+        c_whole(1, 0)
+        c_whole(1, 1)
         x_quant(1)
-        c_diag_v(1, 1)
         v_mm(0, 1)
         zy(1, 1, (2, 3))
-        c_out(1, 1, 2)
-        c_out(1, 1, 3)
+        x_perm(4)
+        x_perm(5)
         v_out(0, 1)
-        c_quant(0, 0)
         c_quant(1, 0)
-        c_diag_v(1, 2)
-        c_diag_v(1, 3)
+        c_whole(1, 2)
+        c_whole(1, 3)
         v_quant(0)
         c_quant(1, 1)
         for pair in range(1, PAIRS - 2):
@@ -428,7 +445,7 @@ def tile_coupled_newton_colouring_step_s11_kernel(tc, x_bytes, x_scale, y, z_wor
             turn(2 * pair + 3)
             x_out(2 * pair + 2)
             x_out(2 * pair + 3)
-            widen(2 * pair + 4)
+            if pair > 1: widen(2 * pair + 4)
             x_quant(pair + 1)
             widen(2 * pair + 5)
             v_mm(pair, 1)

@@ -21,6 +21,7 @@ COPY = mybir.ActivationFunctionType.Copy
 P = 128
 TILES = M // P
 PAIRS = TILES // 2
+XW = 4
 
 
 def tile_coupled_newton_colouring_step_s11_kernel(tc, x_bytes, x_scale, y, z_words, z_scales, gain, out):
@@ -28,15 +29,25 @@ def tile_coupled_newton_colouring_step_s11_kernel(tc, x_bytes, x_scale, y, z_wor
     with ExitStack() as ctx:
         keep = ctx.enter_context(tc.tile_pool(name="keep", bufs=1))
         work = ctx.enter_context(tc.tile_pool(name="work", bufs=3))
-        psum = ctx.enter_context(tc.psum_pool(name="psum", bufs=8))
+        psum = ctx.enter_context(tc.psum_pool(name="psum", bufs=1))
         ctx.enter_context(tc.manual_schedule())
         on_vector, on_scalar = nc.vector.tensor_copy, nc.scalar.copy
 
-        def bank():
-            return psum.tile([P, 4, P], F32, name="bank", tag="bank", bufs=8)
+        def on_pool(out, in_):
+            nc.gpsimd.tensor_scalar(out=out, in0=in_, scalar1=1.0, scalar2=0.0, op0=MULT, op1=ADD)
+
+        free_banks = list(range(8))
+        taken = {}
+
+        def bank(key):
+            taken[key] = free_banks.pop(0)
+            return psum.tile([P, 4, P], F32, name=f"bank{taken[key]}", tag=f"bank{taken[key]}", bufs=1)
+
+        def give_back(key):
+            free_banks.append(taken[key])
 
         xs_col = keep.tile([P, 8], F32, name="xs_col")
-        zs_raw = keep.tile([P, 2, N], U8, name="zs_raw", align_bytes=64)
+        zs_raw = [keep.tile([P, N], U8, name=f"zs_raw_{kp}", align_bytes=64) for kp in range(2)]
         gain_bc = keep.tile([P, N], BF16, name="gain_bc", align_bytes=64)
         y_view = y.rearrange("(g p j) n -> g p j n", p=P, j=4)
         x_view = x_bytes.rearrange("(i p) k -> i p k", p=P)
@@ -46,20 +57,22 @@ def tile_coupled_newton_colouring_step_s11_kernel(tc, x_bytes, x_scale, y, z_wor
         def load_xs():
             nc.sync.dma_start(out=xs_col[:], in_=x_scale.rearrange("o (p j) -> p (o j)", j=8))
 
-        def load_zs():
+        def load_zs(kp):
             for q in range(4):
-                nc.sync.dma_start(
-                    out=zs_raw[32 * q : 32 * q + 4, :, :].bitcast(I32),
-                    in_=z_scales[:, 4 * q : 4 * q + 4, :].bitcast(I32).rearrange("g r n -> r g n"),
-                )
+                nc.sync.dma_start(out=zs_raw[kp][32 * q : 32 * q + 4, :].bitcast(I32), in_=z_scales[kp, 4 * q : 4 * q + 4, :].bitcast(I32))
 
         def load_y(kp, h):
             y_raw[kp, h] = keep.tile([P, 4, 512], BF16, name=f"y_raw_{kp}{h}", align_bytes=64)
             nc.sync.dma_start(out=y_raw[kp, h][:], in_=y_view[kp][:, :, 512 * h : 512 * h + 512])
 
-        def load_z(kp):
-            zw_raw[kp] = keep.tile([P, 2 * N], U8, name=f"zw_raw_{kp}", align_bytes=64)
-            nc.sync.dma_start(out=zw_raw[kp][:].bitcast(I32), in_=z_words[kp].bitcast(I32))
+        def load_z(kp, g):
+            zw_raw[kp, g] = keep.tile([P, N], U8, name=f"zw_raw_{kp}{g}", align_bytes=64)
+            nc.sync.dma_start(out=zw_raw[kp, g][:].bitcast(I32), in_=z_words[kp][:, N * g : N * (g + 1)].bitcast(I32))
+
+        def load_z_whole(kp):
+            t = keep.tile([P, 2, N], U8, name=f"zw_raw_{kp}", align_bytes=64)
+            nc.sync.dma_start(out=t[:].rearrange("p g n -> p (g n)").bitcast(I32), in_=z_words[kp].bitcast(I32))
+            zw_raw[kp, 0], zw_raw[kp, 1] = t[:, 0], t[:, 1]
 
         def load_x(i):
             t = keep.tile([P, N], U8, name=f"xb_{i}", align_bytes=64)
@@ -80,20 +93,25 @@ def tile_coupled_newton_colouring_step_s11_kernel(tc, x_bytes, x_scale, y, z_wor
         xs_ps = {}
 
         def constants():
-            nc.vector.memset(eye15[:].rearrange("p n c -> p (n c)").bitcast(I32), 0)
             make_identity(nc, ident[:])
+            nc.gpsimd.memset(eye15[:].rearrange("p n c -> p (n c)").bitcast(I32), 0)
             nc.vector.tensor_scalar(out=eye15[:, :, 3], in0=ident[:], scalar1=1.5, scalar2=None, op0=MULT)
 
-        def xs_turn(half):
-            xs_ps[half] = bank()
+        def xs_turn(half, plain=0):
+            xs_ps[half] = bank(("xs", half))
             for j in range(4):
-                nc.tensor.transpose(xs_ps[half][:, j, :], xs_col[:, 4 * half + j : 4 * half + j + 1].to_broadcast([P, P]), ident[:])
+                col = xs_col[:, 4 * half + j : 4 * half + j + 1].to_broadcast([P, P])
+                if j < plain:
+                    nc.tensor.matmul(xs_ps[half][:, j, :], lhsT=col, rhs=ident[:], start=True, stop=True)
+                else:
+                    nc.tensor.transpose(xs_ps[half][:, j, :], col, ident[:])
 
         def xs_out(half, copy):
             copy(
                 out=xsb[:].rearrange("p (c j) -> p c j", j=8)[:, :, 4 * half : 4 * half + 4],
                 in_=xs_ps[half][:].rearrange("p j c -> p c j"),
             )
+            give_back(("xs", half))
 
         yq = keep.tile([P, 2, N], U32, name="yq", align_bytes=64)
         ys = keep.tile([P, 2, N], U8, name="ys", align_bytes=64)
@@ -104,48 +122,56 @@ def tile_coupled_newton_colouring_step_s11_kernel(tc, x_bytes, x_scale, y, z_wor
         yi = {}
         ci = {}
 
-        def y_lay(kp, h, t0, nt, copy):
-            if (kp, h) not in yi:
-                yi[kp, h] = keep.tile([P, 512, 4], BF16, name=f"yi_{kp}{h}", align_bytes=64)
-            dst = yi[kp, h][:].rearrange("p (t q r) j -> p t q r j", t=4, r=8)
-            raw = y_raw[kp, h][:].rearrange("p j (q t r) -> p t q r j", t=4, r=8)
-            copy(out=dst[:, t0 : t0 + nt], in_=raw[:, t0 : t0 + nt])
+        def y_lay(kp, h, t0, nt, copy, tag=None):
+            if (kp, h, t0 // 2) not in yi:
+                name = tag or f"yi_{kp}{h}{t0 // 2}"
+                yi[kp, h, t0 // 2] = keep.tile([P, 256, 4], BF16, name=name, tag=name, align_bytes=64)
+            dst = yi[kp, h, t0 // 2][:].rearrange("p (t q r) j -> p q t r j", t=2, r=8)
+            raw = y_raw[kp, h][:].rearrange("p j (q t r) -> p q t r j", t=4, r=8)
+            copy(out=dst[:, :, t0 % 2 : t0 % 2 + nt], in_=raw[:, :, t0 : t0 + nt])
 
         def y_quant(kp, h, t0, nt):
-            lo, hi = 128 * t0, 128 * (t0 + nt)
+            lo = 128 * (t0 % 2)
+            c = slice(512 * h + 128 * t0, 512 * h + 128 * (t0 + nt))
             nc.vector.quantize_mx(
-                out=yq[:, kp, 512 * h + lo : 512 * h + hi].bitcast(FP8X4),
-                scales=ys[:, kp, 512 * h + lo : 512 * h + hi],
-                in_=yi[kp, h][:, lo:hi].rearrange("p n j -> p (n j)"),
+                out=yq[:, kp, c].bitcast(FP8X4),
+                scales=ys[:, kp, c],
+                in_=yi[kp, h, t0 // 2][:, lo : lo + 128 * nt].rearrange("p n j -> p (n j)"),
             )
 
-        def z_lay_words(kp):
+        def z_lay_words(kp, g):
             nc.vector.tensor_copy(
-                out=zq[:, kp].bitcast(I32).rearrange("p (g t q r) -> p g t q r", g=2, t=4, r=4),
-                in_=zw_raw[kp][:].bitcast(I32).rearrange("p (g q t r) -> p g t q r", g=2, t=4, r=4),
+                out=zq[:, kp, N * g : N * (g + 1)].bitcast(I32).rearrange("p (t q r) -> p t q r", t=4, r=4),
+                in_=zw_raw[kp, g][:].bitcast(I32).rearrange("p (q t r) -> p t q r", t=4, r=4),
             )
 
-        def z_lay_scales():
+        def z_lay_scales(kp):
             nc.vector.tensor_copy(
-                out=zs[:].rearrange("p k n -> p (k n)").bitcast(I32).rearrange("p (g t q r) -> p g t q r", g=4, t=4, r=2),
-                in_=zs_raw[:].rearrange("p k n -> p (k n)").bitcast(I32).rearrange("p (g q t r) -> p g t q r", g=4, t=4, r=2),
+                out=zs[:, kp].bitcast(I32).rearrange("p (g t q r) -> p g t q r", g=2, t=4, r=2),
+                in_=zs_raw[kp][:].bitcast(I32).rearrange("p (g q t r) -> p g t q r", g=2, t=4, r=2),
             )
 
         xw, xp, xt, xi, xq, xqs = {}, {}, {}, {}, {}, {}
 
         def widen(i):
             if i < TILES:
-                xw[i] = work.tile([P, N], BF16, name="xw", tag="xw", bufs=8, align_bytes=64)
+                if i == 1:
+                    xw[i] = keep.tile([P, N], BF16, name="xw_1", tag="xw_1", align_bytes=64)
+                else:
+                    xw[i] = work.tile([P, N], BF16, name="xw", tag="xw", bufs=XW, align_bytes=64)
                 nc.vector.tensor_tensor(out=xw[i][:], in0=xb[i].bitcast(FP8), in1=xsb[:], op=MULT)
 
         plain = {}
 
-        def cast(i):
-            plain[i] = keep.tile([P, N], BF16, name=f"plain_{i}", align_bytes=64)
-            nc.scalar.copy(out=plain[i][:], in_=xb[i].bitcast(FP8))
-            xw[i] = keep.tile([P, N], BF16, name=f"xw_{i}", align_bytes=64)
+        def cast(i, g):
+            if g == 0:
+                plain[i] = keep.tile([P, N], BF16, name=f"plain_{i}", align_bytes=64)
+            c = slice(512 * g, 512 * g + 512)
+            nc.scalar.copy(out=plain[i][:, c], in_=xb[i][:, c].bitcast(FP8))
 
         def scale_pool(i, g):
+            if g == 0:
+                xw[i] = keep.tile([P, N], BF16, name="xw_1", tag="xw_1", align_bytes=64)
             c = slice(512 * g, 512 * g + 512)
             nc.gpsimd.tensor_tensor(out=xw[i][:, c], in0=plain[i][:, c], in1=xsb[:, c], op=MULT)
 
@@ -156,7 +182,7 @@ def tile_coupled_newton_colouring_step_s11_kernel(tc, x_bytes, x_scale, y, z_wor
 
         def turn(i):
             if i < TILES:
-                xt[i] = bank()
+                xt[i] = bank(("x", i))
                 for g in range(2):
                     for u in range(2):
                         if i in xp:
@@ -173,6 +199,7 @@ def tile_coupled_newton_colouring_step_s11_kernel(tc, x_bytes, x_scale, y, z_wor
                     out=xi[i // 2][:, i % 2].rearrange("p g m t -> p (g m t)").bitcast(F32).rearrange("p (g m u) -> p g m u", g=2, u=2),
                     in_=xt[i][:].rearrange("p (g u) m -> p g m u", u=2),
                 )
+                give_back(("x", i))
 
         def x_quant(pair, s0=0, ns=2):
             if pair < PAIRS:
@@ -201,7 +228,7 @@ def tile_coupled_newton_colouring_step_s11_kernel(tc, x_bytes, x_scale, y, z_wor
 
         def zy(h, g, t1s):
             for t1 in t1s:
-                zps[h, t1, g] = bank()
+                zps[h, t1, g] = bank(("c", h, t1, g))
             for t1 in t1s:
                 for t in range(4):
                     for kp in range(2):
@@ -210,12 +237,10 @@ def tile_coupled_newton_colouring_step_s11_kernel(tc, x_bytes, x_scale, y, z_wor
         def zy_half(h, g, t1s, kp):
             for t1 in t1s:
                 if kp == 0:
-                    zps[h, t1, g] = bank()
+                    zps[h, t1, g] = bank(("c", h, t1, g))
             for t1 in t1s:
                 for t in range(4):
                     zy_pass(h, t1, g, t, kp, kp == 0 and t == 0, kp == 1 and t == 3)
-
-        planes = {}
 
         def c_dst(h, g, t1):
             if (g, h) not in ci:
@@ -228,38 +253,13 @@ def tile_coupled_newton_colouring_step_s11_kernel(tc, x_bytes, x_scale, y, z_wor
                 nc.vector.tensor_scalar(out=c_dst(h, g, t1), in0=src, scalar1=-0.5, scalar2=None, op0=MULT)
             else:
                 nc.scalar.activation(out=c_dst(h, g, t1), in_=src, func=COPY, scale=-0.5)
-
-        def c_plane(h, t1):
-            planes[h, t1] = work.tile([P, P], F32, name="plane", tag="plane", bufs=4, align_bytes=64)
-            nc.scalar.activation(out=planes[h, t1][:], in_=zps[h, t1, h][:, t1, :], func=COPY, scale=-0.5)
-
-        def c_diag(h, t1):
-            nc.gpsimd.tensor_tensor(
-                out=c_dst(h, h, t1)[:, :, :, t1],
-                in0=planes[h, t1][:].rearrange("p (q r) -> p q r", r=8),
-                in1=eye15[:].rearrange("p (q r) -> p q r", r=8),
-                op=ADD,
-            )
+            give_back(("c", h, t1, g))
 
         def c_whole(h, t1):
             src = zps[h, t1, h][:].rearrange("p f (q r) -> p q r f", r=8)
             eye = eye15[:, :, 3 - t1 : 7 - t1].rearrange("p (q r) f -> p q r f", r=8)
             nc.vector.scalar_tensor_tensor(out=c_dst(h, h, t1), in0=src, scalar=-0.5, in1=eye, op0=MULT, op1=ADD)
-
-        def c_diag_v(h, t1):
-            nc.vector.scalar_tensor_tensor(
-                out=c_dst(h, h, t1)[:, :, :, t1],
-                in0=zps[h, t1, h][:, t1, :].rearrange("p (q r) -> p q r", r=8),
-                scalar=-0.5,
-                in1=eye15[:, :, 3].rearrange("p (q r) -> p q r", r=8),
-                op0=MULT,
-                op1=ADD,
-            )
-
-        def c_full(h, t1, vector=False):
-            c_plane(h, t1)
-            c_out(h, h, t1, vector)
-            c_diag(h, t1)
+            give_back(("c", h, t1, h))
 
         def c_quant(h, g):
             nc.vector.quantize_mx(
@@ -272,7 +272,7 @@ def tile_coupled_newton_colouring_step_s11_kernel(tc, x_bytes, x_scale, y, z_wor
 
         def v_mm(pair, g, tiles=(0, 1)):
             for s in tiles:
-                vps[pair, g, s] = bank()
+                vps[pair, g, s] = bank(("v", pair, g, s))
                 for t in range(4):
                     for kp in range(2):
                         c0 = 512 * g + 128 * t
@@ -292,6 +292,7 @@ def tile_coupled_newton_colouring_step_s11_kernel(tc, x_bytes, x_scale, y, z_wor
                 vi[pair] = work.tile([P, 2, 2, P, 4], BF16, name="vi", tag="vi", bufs=2, align_bytes=64)
             for s in tiles:
                 nc.scalar.copy(out=vi[pair][:, s, g], in_=vps[pair, g, s][:].rearrange("p t m -> p m t"))
+                give_back(("v", pair, g, s))
 
         def v_quant(pair, j0=0, nj=4):
             if pair not in vq:
@@ -306,13 +307,15 @@ def tile_coupled_newton_colouring_step_s11_kernel(tc, x_bytes, x_scale, y, z_wor
 
         out_view = out.rearrange("(i p) n -> i p n", p=P)
 
-        def o_mm(i, c0, width):
-            acc = bank()[:].rearrange("p a b -> p (a b)")[:, 0:width]
+        accs, held = {}, {}
+
+        def o_mm(i, c0, width=512):
+            accs[i, c0] = bank(("o", i, c0))[:].rearrange("p a b -> p (a b)")[:, 0:width]
             c = slice(c0, c0 + width)
             for g in range(2):
                 m = slice(P * (2 * (i % 2) + g), P * (2 * (i % 2) + g + 1))
                 nc.tensor.matmul_mx(
-                    out=acc,
+                    out=accs[i, c0],
                     lhsT=vq[i // 2][:, m].bitcast(FP8X4),
                     lhsT_scale=vqs[i // 2][:, m],
                     rhs=cq[:, g, c].bitcast(FP8X4),
@@ -320,35 +323,39 @@ def tile_coupled_newton_colouring_step_s11_kernel(tc, x_bytes, x_scale, y, z_wor
                     start=(g == 0),
                     stop=(g == 1),
                 )
-            return acc
 
-        def o_part(i, c0, width):
-            acc = o_mm(i, c0, width)
+        def o_out(i, c0, width=512):
             ot = work.tile([P, 512], F32, name="ot", tag="ot", bufs=8, align_bytes=64)
-            nc.vector.tensor_tensor(out=ot[:, 0:width], in0=acc, in1=gain_bc[:, c0 : c0 + width], op=MULT)
+            nc.vector.tensor_tensor(out=ot[:, 0:width], in0=accs[i, c0], in1=gain_bc[:, c0 : c0 + width], op=MULT)
+            give_back(("o", i, c0))
             nc.sync.dma_start(out=out_view[i][:, c0 : c0 + width], in_=ot[:, 0:width])
 
-        held = {}
+        def o_part(i, c0, width=512):
+            o_mm(i, c0, width)
+            o_out(i, c0, width)
 
         def o_pool(i, c0):
-            acc = o_mm(i, c0, 512)
             stage = work.tile([P, 512], F32, name="stage", tag="stage", bufs=2, align_bytes=64)
-            nc.scalar.copy(out=stage[:], in_=acc)
+            nc.scalar.copy(out=stage[:], in_=accs[i, c0])
+            give_back(("o", i, c0))
             held[i] = work.tile([P, 512], F32, name="og", tag="og", bufs=2, align_bytes=64)
             nc.gpsimd.tensor_tensor(out=held[i][:], in0=stage[:], in1=gain_bc[:, c0 : c0 + 512], op=MULT)
 
         def o_pool_store(i, c0):
             nc.sync.dma_start(out=out_view[i][:, c0 : c0 + 512], in_=held[i][:])
 
-        nc.vector.memset(zs_raw[:].rearrange("p g n -> p (g n)").bitcast(I32), 0)
+        for kp in range(2):
+            nc.vector.memset(zs_raw[kp][:].bitcast(I32), 0)
         load_xs()
         load_y(0, 0)
-        load_zs()
-        load_z(0)
-        load_x_pair(0)
+        load_z(0, 1)
+        load_zs(0)
+        load_z(0, 0)
         load_y(1, 0)
-        load_z(1)
+        load_zs(1)
+        load_z_whole(1)
         load_y(0, 1)
+        load_x_pair(0)
         load_y(1, 1)
         load_x_pair(1)
         load_x_pair(2)
@@ -357,140 +364,158 @@ def tile_coupled_newton_colouring_step_s11_kernel(tc, x_bytes, x_scale, y, z_wor
         load_x_pair(4)
         load_x_pair(5)
         constants()
+
         xs_turn(0)
-        xs_turn(1)
+        xs_turn(1, 3)
         xs_out(0, on_scalar)
-        xs_out(1, on_scalar)
-        y_lay(0, 0, 0, 2, on_vector)
+        y_lay(0, 0, 0, 1, on_vector)
         y_lay(0, 0, 2, 2, on_scalar)
-        z_lay_scales()
-        y_quant(0, 0, 0, 2)
-        z_lay_words(0)
-        zy_half(0, 1, (0, 1), 0)
-        widen(0)
+        z_lay_words(0, 1)
+        y_quant(0, 0, 0, 1)
+        z_lay_scales(0)
+        zy_half(0, 1, (0,), 0)
+        y_lay(0, 0, 1, 1, on_vector)
+        z_lay_words(0, 0)
+        zy_half(0, 0, (0,), 0)
+        y_quant(0, 0, 1, 1)
+        zy_half(0, 1, (1,), 0)
+        zy_half(0, 0, (1,), 0)
         y_quant(0, 0, 2, 2)
-        zy_half(0, 1, (2, 3), 0)
+        zy_half(0, 1, (2,), 0)
+        zy_half(0, 0, (2,), 0)
+        zy_half(0, 1, (3,), 0)
+        xs_out(1, on_scalar)
+        zy_half(0, 0, (3,), 0)
         y_lay(1, 0, 0, 2, on_vector)
         y_lay(1, 0, 2, 2, on_scalar)
-        x_perm(0)
-        z_lay_words(1)
+        z_lay_scales(1)
         y_quant(1, 0, 0, 2)
+        z_lay_words(1, 1)
         zy_half(0, 1, (0, 1), 1)
+        z_lay_words(1, 0)
         y_quant(1, 0, 2, 2)
+        zy_half(0, 0, (0, 1), 1)
         zy_half(0, 1, (2, 3), 1)
-        widen(1)
-        zy(0, 0, (0, 1))
-        turn(0)
-        turn(1)
+        zy_half(0, 0, (2, 3), 1)
         y_lay(0, 1, 0, 2, on_scalar)
+        y_lay(0, 1, 2, 2, on_vector)
+        widen(0)
         c_out(0, 1, 0)
         c_out(0, 1, 1)
-        y_lay(0, 1, 2, 2, on_vector)
-        zy(0, 0, (2, 3))
-        y_lay(1, 1, 0, 4, on_vector)
-        cast(3)
+        y_quant(0, 1, 2, 2)
+        y_quant(0, 1, 0, 2)
         c_out(0, 1, 2)
         c_out(0, 1, 3)
-        y_quant(0, 1, 0, 4)
+        x_perm(0)
+        cast(5, 0)
+        y_lay(1, 1, 0, 2, on_vector)
+        c_whole(0, 0)
+        y_lay(1, 1, 2, 2, on_pool, "yi_010")
+        c_whole(0, 1)
+        zy_half(1, 0, (0, 1, 2, 3), 0)
+        turn(0)
+        c_whole(0, 2)
+        zy_half(1, 1, (0, 1), 0)
         y_quant(1, 1, 0, 2)
         y_quant(1, 1, 2, 2)
         x_out(0)
-        x_out(1)
-        zy(1, 0, (0, 1))
-        scale_pool(3, 0)
-        scale_pool(3, 1)
-        c_whole(0, 0)
-        c_whole(0, 1)
-        zy(1, 0, (2, 3))
-        widen(2)
-        x_quant(0)
-        c_whole(0, 2)
-        c_whole(0, 3)
+        widen(1)
+        zy_half(1, 0, (0, 1, 2, 3), 1)
         c_out(1, 0, 0)
+        turn(1)
+        zy_half(1, 1, (0, 1), 1)
+        x_quant(0, 0, 1)
+        widen(2)
+        widen(3)
         c_out(1, 0, 1)
-        x_perm(2)
         c_out(1, 0, 2)
         c_out(1, 0, 3)
-        widen(4)
-        c_quant(0, 1)
-        v_mm(0, 0)
-        v_out(0, 0)
-        zy(1, 1, (0, 1))
+        v_mm(0, 0, (0,))
+        v_mm(0, 1, (0,))
+        x_out(1)
+        x_perm(2)
+        c_whole(0, 3)
+        scale_pool(5, 0)
         turn(2)
         turn(3)
-        cast(6)
-        x_out(2)
-        x_out(3)
-        widen(5)
-        c_quant(0, 0)
-        scale_pool(6, 0)
-        scale_pool(6, 1)
         c_whole(1, 0)
         c_whole(1, 1)
+        x_quant(0, 1, 1)
+        v_out(0, 0, (0,))
+        v_out(0, 1, (0,))
+        zy(1, 1, (2,))
+        v_mm(0, 0, (1,))
+        v_mm(0, 1, (1,))
+        x_out(2)
+        x_out(3)
+        zy(1, 1, (3,))
+        widen(4)
         x_quant(1)
-        v_mm(0, 1)
-        zy(1, 1, (2, 3))
+        v_out(0, 0, (1,))
+        cast(5, 1)
+        v_out(0, 1, (1,))
         x_perm(4)
-        x_perm(5)
-        v_out(0, 1)
-        c_quant(1, 0)
+        c_quant(0, 1)
+        c_quant(0, 0)
         c_whole(1, 2)
+        scale_pool(5, 1)
         c_whole(1, 3)
         v_quant(0)
+        c_quant(1, 0)
         c_quant(1, 1)
-        for pair in range(1, PAIRS - 2):
+
+        for pair in range(1, PAIRS - 1):
+            a, b, prev = 2 * pair + 2, 2 * pair + 3, 2 * pair - 2
             v_mm(pair, 0)
-            v_out(pair, 0)
-            turn(2 * pair + 2)
-            turn(2 * pair + 3)
-            x_out(2 * pair + 2)
-            x_out(2 * pair + 3)
-            if pair > 1: widen(2 * pair + 4)
-            x_quant(pair + 1)
-            widen(2 * pair + 5)
+            v_out(pair, 0, (0,))
+            x_perm(b)
+            if pair > 1:
+                o_out(prev - 1, 0)
+                o_out(prev - 2, 512)
+                o_pool_store(prev - 2, 0)
+                o_out(prev - 1, 512)
             v_mm(pair, 1)
+            v_out(pair, 0, (1,))
             v_out(pair, 1, (0,))
-            o_pool(2 * pair - 2, 0)
+            if pair > 1:
+                v_quant(pair - 1)
+            turn(a)
+            turn(b)
+            x_out(a)
+            x_out(b)
             v_out(pair, 1, (1,))
-            x_perm(2 * pair + 4)
-            x_perm(2 * pair + 5)
-            o_part(2 * pair - 1, 0, 512)
-            o_part(2 * pair - 2, 512, 512)
-            o_pool_store(2 * pair - 2, 0)
-            o_part(2 * pair - 1, 512, 512)
-            v_quant(pair)
-        last = PAIRS - 1
-        v_mm(4, 0)
-        v_out(4, 0)
-        turn(10)
-        turn(11)
-        x_out(10)
-        x_out(11)
-        x_quant(5)
-        v_mm(4, 1)
-        v_out(4, 1)
-        o_part(6, 0, 512)
-        o_part(7, 0, 512)
+            widen(a + 2)
+            x_quant(pair + 1)
+            widen(b + 2)
+            o_mm(prev, 0)
+            o_mm(prev + 1, 0)
+            o_mm(prev, 512)
+            o_mm(prev + 1, 512)
+            if pair < PAIRS - 2:
+                o_pool(prev, 0)
+            x_perm(a + 2)
+        o_out(6, 0)
+        o_out(7, 0)
         v_quant(4)
-        o_part(6, 512, 512)
-        o_part(7, 512, 512)
-        v_mm(last, 0, (0,))
-        v_mm(last, 1, (0,))
-        v_out(last, 0, (0,))
-        v_out(last, 1, (0,))
-        o_part(8, 0, 512)
-        o_part(8, 512, 512)
-        v_quant(last, 0, 2)
-        o_part(9, 0, 512)
-        v_mm(last, 0, (1,))
-        v_mm(last, 1, (1,))
-        v_out(last, 0, (1,))
-        v_out(last, 1, (1,))
-        v_quant(last, 2, 1)
-        o_part(9, 512, 512)
-        v_quant(last, 3, 1)
-        o_part(10, 0, 512)
-        o_part(10, 512, 512)
-        o_part(11, 0, 512)
+        v_mm(5, 0, (0,))
+        v_mm(5, 1, (0,))
+        v_out(5, 0, (0,))
+        v_out(5, 1, (0,))
+        o_out(6, 512)
+        o_out(7, 512)
+        o_part(8, 0)
+        o_part(8, 512)
+        v_quant(5, 0, 2)
+        o_part(9, 0)
+        v_mm(5, 0, (1,))
+        v_mm(5, 1, (1,))
+        v_out(5, 0, (1,))
+        v_out(5, 1, (1,))
+        v_quant(5, 2, 1)
+        o_part(9, 512)
+        v_quant(5, 3, 1)
+        o_part(10, 0)
+        o_part(10, 512)
+        o_part(11, 0)
         o_part(11, 512, 256)
         o_part(11, 768, 256)

@@ -21,7 +21,6 @@ COPY = mybir.ActivationFunctionType.Copy
 P = 128
 TILES = M // P
 PAIRS = TILES // 2
-XW = 4
 
 
 def tile_coupled_newton_colouring_step_s11_kernel(tc, x_bytes, x_scale, y, z_words, z_scales, gain, out):
@@ -31,7 +30,7 @@ def tile_coupled_newton_colouring_step_s11_kernel(tc, x_bytes, x_scale, y, z_wor
         work = ctx.enter_context(tc.tile_pool(name="work", bufs=3))
         psum = ctx.enter_context(tc.psum_pool(name="psum", bufs=1))
         ctx.enter_context(tc.manual_schedule())
-        on_vector, on_scalar = nc.vector.tensor_copy, nc.scalar.copy
+        on_vector, on_scalar, on_gpsimd = nc.vector.tensor_copy, nc.scalar.copy, nc.gpsimd.tensor_copy
 
         def on_pool(out, in_):
             nc.gpsimd.tensor_scalar(out=out, in0=in_, scalar1=1.0, scalar2=0.0, op0=MULT, op1=ADD)
@@ -46,16 +45,15 @@ def tile_coupled_newton_colouring_step_s11_kernel(tc, x_bytes, x_scale, y, z_wor
         def give_back(key):
             free_banks.append(taken[key])
 
-        xs_col = keep.tile([P, 8], F32, name="xs_col")
+        xs4 = keep.tile([P, 2, 4], F32, name="xs4")
         zs_raw = [keep.tile([P, N], U8, name=f"zs_raw_{kp}", align_bytes=64) for kp in range(2)]
         gain_bc = keep.tile([P, N], BF16, name="gain_bc", align_bytes=64)
         y_view = y.rearrange("(g p j) n -> g p j n", p=P, j=4)
-        x_view = x_bytes.rearrange("(i p) k -> i p k", p=P)
         x_view2 = x_bytes.rearrange("(i s p) k -> i p s k", s=2, p=P)
         y_raw, zw_raw, xb = {}, {}, {}
 
         def load_xs():
-            nc.sync.dma_start(out=xs_col[:], in_=x_scale.rearrange("o (p j) -> p (o j)", j=8))
+            nc.sync.dma_start(out=xs4[:], in_=x_scale.rearrange("o (g p t) -> p (o g) t", p=P, t=4))
 
         def load_zs(kp):
             for q in range(4):
@@ -74,44 +72,21 @@ def tile_coupled_newton_colouring_step_s11_kernel(tc, x_bytes, x_scale, y, z_wor
             nc.sync.dma_start(out=t[:].rearrange("p g n -> p (g n)").bitcast(I32), in_=z_words[kp].bitcast(I32))
             zw_raw[kp, 0], zw_raw[kp, 1] = t[:, 0], t[:, 1]
 
-        def load_x(i):
-            t = keep.tile([P, N], U8, name=f"xb_{i}", align_bytes=64)
-            nc.sync.dma_start(out=t[:], in_=x_view[i])
-            xb[i] = t[:]
-
         def load_x_pair(pair):
             t = keep.tile([P, 2, N], U8, name=f"xb2_{pair}", align_bytes=64)
             nc.sync.dma_start(out=t[:], in_=x_view2[pair])
-            xb[2 * pair], xb[2 * pair + 1] = t[:, 0, :], t[:, 1, :]
+            xb[pair] = t
 
         def load_gain():
             nc.sync.dma_start(out=gain_bc[:], in_=gain.partition_broadcast(P))
 
         ident = keep.tile([P, P], F32, name="ident", align_bytes=64)
         eye15 = keep.tile([P, P, 8], BF16, name="eye15", align_bytes=64)
-        xsb = keep.tile([P, N], F32, name="xsb", align_bytes=64)
-        xs_ps = {}
 
         def constants():
             make_identity(nc, ident[:])
             nc.gpsimd.memset(eye15[:].rearrange("p n c -> p (n c)").bitcast(I32), 0)
             nc.vector.tensor_scalar(out=eye15[:, :, 3], in0=ident[:], scalar1=1.5, scalar2=None, op0=MULT)
-
-        def xs_turn(half, plain=0):
-            xs_ps[half] = bank(("xs", half))
-            for j in range(4):
-                col = xs_col[:, 4 * half + j : 4 * half + j + 1].to_broadcast([P, P])
-                if j < plain:
-                    nc.tensor.matmul(xs_ps[half][:, j, :], lhsT=col, rhs=ident[:], start=True, stop=True)
-                else:
-                    nc.tensor.transpose(xs_ps[half][:, j, :], col, ident[:])
-
-        def xs_out(half, copy):
-            copy(
-                out=xsb[:].rearrange("p (c j) -> p c j", j=8)[:, :, 4 * half : 4 * half + 4],
-                in_=xs_ps[half][:].rearrange("p j c -> p c j"),
-            )
-            give_back(("xs", half))
 
         yq = keep.tile([P, 2, N], U32, name="yq", align_bytes=64)
         ys = keep.tile([P, 2, N], U8, name="ys", align_bytes=64)
@@ -151,34 +126,22 @@ def tile_coupled_newton_colouring_step_s11_kernel(tc, x_bytes, x_scale, y, z_wor
                 in_=zs_raw[kp][:].bitcast(I32).rearrange("p (g q t r) -> p g t q r", g=2, t=4, r=2),
             )
 
-        xw, xp, xt, xi, xq, xqs = {}, {}, {}, {}, {}, {}
+        xc, xp, xt, xi, xq, xqs = {}, {}, {}, {}, {}, {}
 
-        def widen(i):
-            if i < TILES:
-                if i == 1:
-                    xw[i] = keep.tile([P, N], BF16, name="xw_1", tag="xw_1", align_bytes=64)
-                else:
-                    xw[i] = work.tile([P, N], BF16, name="xw", tag="xw", bufs=XW, align_bytes=64)
-                nc.vector.tensor_tensor(out=xw[i][:], in0=xb[i].bitcast(FP8), in1=xsb[:], op=MULT)
+        def cast(pair, copy, s0=0, ns=2, after=None):
+            if pair < PAIRS:
+                if pair not in xc:
+                    tag = after or f"xc{pair}"
+                    xc[pair] = keep.tile([P, 2, N], BF16, name=tag, tag=tag, align_bytes=64)
+                copy(
+                    out=xc[pair][:, s0 : s0 + ns].rearrange("p s k -> p (s k)"),
+                    in_=xb[pair][:, s0 : s0 + ns].rearrange("p s k -> p (s k)").bitcast(FP8),
+                )
 
-        plain = {}
-
-        def cast(i, g):
-            if g == 0:
-                plain[i] = keep.tile([P, N], BF16, name=f"plain_{i}", align_bytes=64)
-            c = slice(512 * g, 512 * g + 512)
-            nc.scalar.copy(out=plain[i][:, c], in_=xb[i][:, c].bitcast(FP8))
-
-        def scale_pool(i, g):
-            if g == 0:
-                xw[i] = keep.tile([P, N], BF16, name="xw_1", tag="xw_1", align_bytes=64)
-            c = slice(512 * g, 512 * g + 512)
-            nc.gpsimd.tensor_tensor(out=xw[i][:, c], in0=plain[i][:, c], in1=xsb[:, c], op=MULT)
-
-        def x_perm(i):
+        def x_perm(i, copy=on_scalar):
             if i < TILES:
                 xp[i] = work.tile([P, 2, 2, P], F32, name="xp", tag="xp", bufs=4, align_bytes=64)
-                nc.scalar.copy(out=xp[i][:], in_=xw[i][:].bitcast(F32).rearrange("p (g n u) -> p g u n", g=2, u=2))
+                copy(out=xp[i][:], in_=xc[i // 2][:, i % 2].bitcast(F32).rearrange("p (g n u) -> p g u n", g=2, u=2))
 
         def turn(i):
             if i < TILES:
@@ -188,16 +151,19 @@ def tile_coupled_newton_colouring_step_s11_kernel(tc, x_bytes, x_scale, y, z_wor
                         if i in xp:
                             words = xp[i][:, g, u, :]
                         else:
-                            words = xw[i][:].bitcast(F32)[:, 256 * g + u : 256 * (g + 1) : 2]
-                        nc.tensor.transpose(xt[i][:, 2 * g + u, :], words, ident[:])
+                            words = xc[i // 2][:, i % 2].bitcast(F32)[:, 256 * g + u : 256 * (g + 1) : 2]
+                        nc.tensor.transpose(xt[i][:, 2 * u + g, :], words, ident[:])
 
         def x_out(i):
             if i < TILES:
                 if i // 2 not in xi:
-                    xi[i // 2] = work.tile([P, 2, 2, P, 4], BF16, name="xi", tag="xi", bufs=2, align_bytes=64)
-                nc.scalar.copy(
-                    out=xi[i // 2][:, i % 2].rearrange("p g m t -> p (g m t)").bitcast(F32).rearrange("p (g m u) -> p g m u", g=2, u=2),
-                    in_=xt[i][:].rearrange("p (g u) m -> p g m u", u=2),
+                    tag = f"xo{i // 2 % 2}"
+                    xi[i // 2] = keep.tile([P, 2, 2, P, 4], BF16, name=tag, tag=tag, align_bytes=64)
+                nc.vector.tensor_tensor(
+                    out=xi[i // 2][:, i % 2].rearrange("p g m (u e) -> p g m u e", u=2),
+                    in0=xt[i][:].rearrange("p a m -> p (a m)").bitcast(BF16).rearrange("p (u g m e) -> p g m u e", u=2, g=2, e=2),
+                    in1=xs4[:].rearrange("p g (u e) -> p g u e", u=2).unsqueeze(2).to_broadcast([P, 2, P, 2, 2]),
+                    op=MULT,
                 )
                 give_back(("x", i))
 
@@ -244,7 +210,7 @@ def tile_coupled_newton_colouring_step_s11_kernel(tc, x_bytes, x_scale, y, z_wor
 
         def c_dst(h, g, t1):
             if (g, h) not in ci:
-                ci[g, h] = keep.tile([P, 512, 4], BF16, name=f"ci_{g}{h}", align_bytes=64)
+                ci[g, h] = keep.tile([P, 512, 4], BF16, name=f"ci_{g}{h}", tag=f"ci_{g}{h}", align_bytes=64)
             return ci[g, h][:].rearrange("p (q t r) f -> p t q r f", t=4, r=8)[:, t1]
 
         def c_out(h, g, t1, vector=False):
@@ -289,7 +255,7 @@ def tile_coupled_newton_colouring_step_s11_kernel(tc, x_bytes, x_scale, y, z_wor
 
         def v_out(pair, g, tiles=(0, 1)):
             if pair not in vi:
-                vi[pair] = work.tile([P, 2, 2, P, 4], BF16, name="vi", tag="vi", bufs=2, align_bytes=64)
+                vi[pair] = keep.tile([P, 2, 2, P, 4], BF16, name=f"vx{pair % 2}", tag=f"vx{pair % 2}", align_bytes=64)
             for s in tiles:
                 nc.scalar.copy(out=vi[pair][:, s, g], in_=vps[pair, g, s][:].rearrange("p t m -> p m t"))
                 give_back(("v", pair, g, s))
@@ -334,19 +300,22 @@ def tile_coupled_newton_colouring_step_s11_kernel(tc, x_bytes, x_scale, y, z_wor
             o_mm(i, c0, width)
             o_out(i, c0, width)
 
-        def o_pool(i, c0):
-            stage = work.tile([P, 512], F32, name="stage", tag="stage", bufs=2, align_bytes=64)
-            nc.scalar.copy(out=stage[:], in_=accs[i, c0])
+        stage = {}
+
+        def o_stage(i, c0):
+            stage[i] = work.tile([P, 512], F32, name="stage", tag="stage", bufs=2, align_bytes=64)
+            nc.scalar.copy(out=stage[i][:], in_=accs[i, c0])
             give_back(("o", i, c0))
-            held[i] = work.tile([P, 512], F32, name="og", tag="og", bufs=2, align_bytes=64)
-            nc.gpsimd.tensor_tensor(out=held[i][:], in0=stage[:], in1=gain_bc[:, c0 : c0 + 512], op=MULT)
+
+        def o_pool(i, c0, tag):
+            held[i] = keep.tile([P, 512], F32, name=tag, tag=tag, align_bytes=64)
+            nc.gpsimd.tensor_tensor(out=held[i][:], in0=stage[i][:], in1=gain_bc[:, c0 : c0 + 512], op=MULT)
 
         def o_pool_store(i, c0):
             nc.sync.dma_start(out=out_view[i][:, c0 : c0 + 512], in_=held[i][:])
 
         for kp in range(2):
             nc.vector.memset(zs_raw[kp][:].bitcast(I32), 0)
-        load_xs()
         load_y(0, 0)
         load_z(0, 1)
         load_zs(0)
@@ -354,8 +323,9 @@ def tile_coupled_newton_colouring_step_s11_kernel(tc, x_bytes, x_scale, y, z_wor
         load_y(1, 0)
         load_zs(1)
         load_z_whole(1)
-        load_y(0, 1)
         load_x_pair(0)
+        load_y(0, 1)
+        load_xs()
         load_y(1, 1)
         load_x_pair(1)
         load_x_pair(2)
@@ -365,9 +335,6 @@ def tile_coupled_newton_colouring_step_s11_kernel(tc, x_bytes, x_scale, y, z_wor
         load_x_pair(5)
         constants()
 
-        xs_turn(0)
-        xs_turn(1, 3)
-        xs_out(0, on_scalar)
         y_lay(0, 0, 0, 1, on_vector)
         y_lay(0, 0, 2, 2, on_scalar)
         z_lay_words(0, 1)
@@ -381,128 +348,126 @@ def tile_coupled_newton_colouring_step_s11_kernel(tc, x_bytes, x_scale, y, z_wor
         zy_half(0, 1, (1,), 0)
         zy_half(0, 0, (1,), 0)
         y_quant(0, 0, 2, 2)
-        zy_half(0, 1, (2,), 0)
-        zy_half(0, 0, (2,), 0)
-        zy_half(0, 1, (3,), 0)
-        xs_out(1, on_scalar)
-        zy_half(0, 0, (3,), 0)
+        for t1 in (2, 3):
+            zy_half(0, 1, (t1,), 0)
+            zy_half(0, 0, (t1,), 0)
         y_lay(1, 0, 0, 2, on_vector)
         y_lay(1, 0, 2, 2, on_scalar)
         z_lay_scales(1)
         y_quant(1, 0, 0, 2)
-        z_lay_words(1, 1)
-        zy_half(0, 1, (0, 1), 1)
         z_lay_words(1, 0)
-        y_quant(1, 0, 2, 2)
         zy_half(0, 0, (0, 1), 1)
-        zy_half(0, 1, (2, 3), 1)
+        z_lay_words(1, 1)
+        y_quant(1, 0, 2, 2)
+        zy_half(0, 1, (0, 1), 1)
         zy_half(0, 0, (2, 3), 1)
-        y_lay(0, 1, 0, 2, on_scalar)
+        zy_half(0, 1, (2, 3), 1)
+        cast(0, on_vector, 0, 1)
+        cast(0, on_scalar, 1, 1)
         y_lay(0, 1, 2, 2, on_vector)
-        widen(0)
+        y_lay(0, 1, 0, 2, on_scalar)
+        x_perm(0, on_vector)
+        x_perm(1, on_vector)
+        c_whole(0, 0)
+        c_whole(0, 1)
+        y_quant(0, 1, 2, 2)
+        turn(0)
+        turn(1)
+        y_quant(0, 1, 0, 2)
         c_out(0, 1, 0)
         c_out(0, 1, 1)
-        y_quant(0, 1, 2, 2)
-        y_quant(0, 1, 0, 2)
+        y_lay(1, 1, 2, 2, on_pool, "yi_010")
+        c_whole(0, 2)
+        c_whole(0, 3)
+        zy_half(1, 0, (0, 1, 2, 3), 0)
+        y_lay(1, 1, 0, 2, on_scalar)
+        x_out(0)
+        y_quant(1, 1, 2, 2)
         c_out(0, 1, 2)
         c_out(0, 1, 3)
-        x_perm(0)
-        cast(5, 0)
-        y_lay(1, 1, 0, 2, on_vector)
-        c_whole(0, 0)
-        y_lay(1, 1, 2, 2, on_pool, "yi_010")
-        c_whole(0, 1)
-        zy_half(1, 0, (0, 1, 2, 3), 0)
-        turn(0)
-        c_whole(0, 2)
-        zy_half(1, 1, (0, 1), 0)
         y_quant(1, 1, 0, 2)
-        y_quant(1, 1, 2, 2)
-        x_out(0)
-        widen(1)
-        zy_half(1, 0, (0, 1, 2, 3), 1)
-        c_out(1, 0, 0)
-        turn(1)
+        cast(1, on_scalar)
+        zy_half(1, 1, (0, 1), 0)
+        zy_half(1, 0, (2, 3, 0, 1), 1)
+        x_out(1)
         zy_half(1, 1, (0, 1), 1)
-        x_quant(0, 0, 1)
-        widen(2)
-        widen(3)
-        c_out(1, 0, 1)
+        x_quant(0)
         c_out(1, 0, 2)
         c_out(1, 0, 3)
-        v_mm(0, 0, (0,))
-        v_mm(0, 1, (0,))
-        x_out(1)
-        x_perm(2)
-        c_whole(0, 3)
-        scale_pool(5, 0)
-        turn(2)
-        turn(3)
-        c_whole(1, 0)
-        c_whole(1, 1)
-        x_quant(0, 1, 1)
-        v_out(0, 0, (0,))
-        v_out(0, 1, (0,))
-        zy(1, 1, (2,))
-        v_mm(0, 0, (1,))
-        v_mm(0, 1, (1,))
-        x_out(2)
-        x_out(3)
-        zy(1, 1, (3,))
-        widen(4)
-        x_quant(1)
-        v_out(0, 0, (1,))
-        cast(5, 1)
-        v_out(0, 1, (1,))
-        x_perm(4)
         c_quant(0, 1)
         c_quant(0, 0)
-        c_whole(1, 2)
-        scale_pool(5, 1)
-        c_whole(1, 3)
-        v_quant(0)
+        cast(2, on_gpsimd, after="ci_00")
+        cast(3, on_gpsimd, 0, 1)
+        c_whole(1, 0)
+        c_whole(1, 1)
+        v_mm(0, 0)
+        turn(2)
+        turn(3)
+        c_out(1, 0, 0)
+        c_out(1, 0, 1)
+        x_out(2)
+        x_out(3)
+        v_mm(0, 1)
+        v_out(0, 0)
+        zy(1, 1, (2, 3))
+        x_quant(1)
+        x_perm(4)
+        x_perm(5)
+        v_out(0, 1)
+        cast(3, on_scalar, 1, 1)
         c_quant(1, 0)
-        c_quant(1, 1)
+        c_whole(1, 2)
+        c_whole(1, 3)
 
         for pair in range(1, PAIRS - 1):
             a, b, prev = 2 * pair + 2, 2 * pair + 3, 2 * pair - 2
-            v_mm(pair, 0)
-            v_out(pair, 0, (0,))
-            x_perm(b)
-            if pair > 1:
-                o_out(prev - 1, 0)
-                o_out(prev - 2, 512)
-                o_pool_store(prev - 2, 0)
-                o_out(prev - 1, 512)
-            v_mm(pair, 1)
-            v_out(pair, 0, (1,))
-            v_out(pair, 1, (0,))
-            if pair > 1:
-                v_quant(pair - 1)
             turn(a)
             turn(b)
+            if pair > 1:
+                o_stage(prev - 1, 512)
+            v_quant(pair - 1)
+            if pair == 1:
+                c_quant(1, 1)
+            else:
+                cast(pair + 2, on_gpsimd, after=f"vx{(pair + 1) % 2}")
+                o_pool(prev - 1, 512, "og")
+            if pair == 1:
+                v_mm(pair, 0)
+                v_mm(pair, 1)
+                v_out(pair, 0)
+                v_out(pair, 1)
             x_out(a)
             x_out(b)
-            v_out(pair, 1, (1,))
-            widen(a + 2)
-            x_quant(pair + 1)
-            widen(b + 2)
-            o_mm(prev, 0)
-            o_mm(prev + 1, 0)
+            if pair == 2:
+                o_out(prev - 1, 0)
+            if pair > 1:
+                o_out(prev - 2, 512)
+            if pair > 1:
+                v_mm(pair, 0)
+                v_mm(pair, 1)
+                v_out(pair, 0)
+                v_out(pair, 1)
+            if pair == PAIRS - 2:
+                x_quant(pair + 1)
+            o_part(prev, 0)
+            if pair > 1:
+                o_pool_store(prev - 1, 512)
+                o_part(prev + 1, 0)
+            else:
+                o_mm(prev + 1, 0)
+            if pair < PAIRS - 2:
+                x_quant(pair + 1)
             o_mm(prev, 512)
             o_mm(prev + 1, 512)
-            if pair < PAIRS - 2:
-                o_pool(prev, 0)
             x_perm(a + 2)
-        o_out(6, 0)
-        o_out(7, 0)
+            x_perm(b + 2)
         v_quant(4)
+        o_out(6, 512)
+        o_out(7, 512)
         v_mm(5, 0, (0,))
         v_mm(5, 1, (0,))
         v_out(5, 0, (0,))
         v_out(5, 1, (0,))
-        o_out(6, 512)
-        o_out(7, 512)
         o_part(8, 0)
         o_part(8, 512)
         v_quant(5, 0, 2)

@@ -21,6 +21,7 @@ COPY = mybir.ActivationFunctionType.Copy
 P = 128
 TILES = M // P
 PAIRS = TILES // 2
+KEPT = 256
 
 
 def tile_coupled_newton_colouring_step_s11_kernel(tc, x_bytes, x_scale, y, z_words, z_scales, gain, out):
@@ -88,6 +89,12 @@ def tile_coupled_newton_colouring_step_s11_kernel(tc, x_bytes, x_scale, y, z_wor
             nc.gpsimd.memset(eye15[:].rearrange("p n c -> p (n c)").bitcast(I32), 0)
             nc.vector.tensor_scalar(out=eye15[:, :, 3], in0=ident[:], scalar1=1.5, scalar2=None, op0=MULT)
 
+        def warm(n):
+            b = bank("warm")
+            for j in range(n):
+                nc.tensor.matmul(b[:, j % 4, :], lhsT=ident[:], rhs=ident[:], start=True, stop=True)
+            give_back("warm")
+
         yq = keep.tile([P, 2, N], U32, name="yq", align_bytes=64)
         ys = keep.tile([P, 2, N], U8, name="ys", align_bytes=64)
         zq = keep.tile([P, 2, 2 * N], U8, name="zq", align_bytes=64)
@@ -130,18 +137,16 @@ def tile_coupled_newton_colouring_step_s11_kernel(tc, x_bytes, x_scale, y, z_wor
 
         def cast(pair, copy, s0=0, ns=2, after=None):
             if pair < PAIRS:
-                if pair not in xc:
-                    tag = after or f"xc{pair}"
-                    xc[pair] = keep.tile([P, 2, N], BF16, name=tag, tag=tag, align_bytes=64)
-                copy(
-                    out=xc[pair][:, s0 : s0 + ns].rearrange("p s k -> p (s k)"),
-                    in_=xb[pair][:, s0 : s0 + ns].rearrange("p s k -> p (s k)").bitcast(FP8),
-                )
+                tag = after or f"xc{pair}{s0}"
+                t = keep.tile([P, ns, N], BF16, name=tag, tag=tag, align_bytes=64)
+                copy(out=t[:].rearrange("p s k -> p (s k)"), in_=xb[pair][:, s0 : s0 + ns].rearrange("p s k -> p (s k)").bitcast(FP8))
+                for s in range(ns):
+                    xc[2 * pair + s0 + s] = t[:, s]
 
         def x_perm(i, copy=on_scalar):
             if i < TILES:
                 xp[i] = work.tile([P, 2, 2, P], F32, name="xp", tag="xp", bufs=4, align_bytes=64)
-                copy(out=xp[i][:], in_=xc[i // 2][:, i % 2].bitcast(F32).rearrange("p (g n u) -> p g u n", g=2, u=2))
+                copy(out=xp[i][:], in_=xc[i].bitcast(F32).rearrange("p (g n u) -> p g u n", g=2, u=2))
 
         def turn(i):
             if i < TILES:
@@ -151,7 +156,7 @@ def tile_coupled_newton_colouring_step_s11_kernel(tc, x_bytes, x_scale, y, z_wor
                         if i in xp:
                             words = xp[i][:, g, u, :]
                         else:
-                            words = xc[i // 2][:, i % 2].bitcast(F32)[:, 256 * g + u : 256 * (g + 1) : 2]
+                            words = xc[i].bitcast(F32)[:, 256 * g + u : 256 * (g + 1) : 2]
                         nc.tensor.transpose(xt[i][:, 2 * u + g, :], words, ident[:])
 
         def x_out(i):
@@ -255,7 +260,7 @@ def tile_coupled_newton_colouring_step_s11_kernel(tc, x_bytes, x_scale, y, z_wor
 
         def v_out(pair, g, tiles=(0, 1)):
             if pair not in vi:
-                vi[pair] = keep.tile([P, 2, 2, P, 4], BF16, name=f"vx{pair % 2}", tag=f"vx{pair % 2}", align_bytes=64)
+                vi[pair] = keep.tile([P, 2, 2, P, 4], BF16, name=f"vx{pair % 4}", tag=f"vx{pair % 4}", align_bytes=64)
             for s in tiles:
                 nc.scalar.copy(out=vi[pair][:, s, g], in_=vps[pair, g, s][:].rearrange("p t m -> p m t"))
                 give_back(("v", pair, g, s))
@@ -292,7 +297,7 @@ def tile_coupled_newton_colouring_step_s11_kernel(tc, x_bytes, x_scale, y, z_wor
 
         def o_out(i, c0, width=512):
             ot = work.tile([P, 512], F32, name="ot", tag="ot", bufs=8, align_bytes=64)
-            nc.vector.tensor_tensor(out=ot[:, 0:width], in0=accs[i, c0], in1=gain_bc[:, c0 : c0 + width], op=MULT)
+            nc.vector.tensor_tensor(out=ot[:, 0:width], in0=accs[i, c0][:, 0:width], in1=gain_bc[:, c0 : c0 + width], op=MULT)
             give_back(("o", i, c0))
             nc.sync.dma_start(out=out_view[i][:, c0 : c0 + width], in_=ot[:, 0:width])
 
@@ -311,35 +316,48 @@ def tile_coupled_newton_colouring_step_s11_kernel(tc, x_bytes, x_scale, y, z_wor
             held[i] = keep.tile([P, 512], F32, name=tag, tag=tag, align_bytes=64)
             nc.gpsimd.tensor_tensor(out=held[i][:], in0=stage[i][:], in1=gain_bc[:, c0 : c0 + 512], op=MULT)
 
+        def o_stage2(i):
+            stage[i] = work.tile([P, N - KEPT], F32, name="stage2", tag="stage2", bufs=2, align_bytes=64)
+            nc.scalar.copy(out=stage[i][:, 0 : 512 - KEPT], in_=accs[i, 0][:, KEPT:512])
+            nc.scalar.copy(out=stage[i][:, 512 - KEPT :], in_=accs[i, 512])
+            give_back(("o", i, 512))
+
+        def o_pool2(i, tag):
+            held[i] = keep.tile([P, N - KEPT], F32, name=tag, tag=tag, align_bytes=64)
+            nc.gpsimd.tensor_tensor(out=held[i][:], in0=stage[i][:], in1=gain_bc[:, KEPT:], op=MULT)
+
+        def o_pool_store2(i):
+            nc.sync.dma_start(out=out_view[i][:, KEPT:], in_=held[i][:])
+
         def o_pool_store(i, c0):
             nc.sync.dma_start(out=out_view[i][:, c0 : c0 + 512], in_=held[i][:])
 
         for kp in range(2):
             nc.vector.memset(zs_raw[kp][:].bitcast(I32), 0)
         load_y(0, 0)
-        load_z(0, 1)
         load_zs(0)
-        load_z(0, 0)
+        load_z_whole(0)
+        load_xs()
+        load_x_pair(0)
         load_y(1, 0)
         load_zs(1)
         load_z_whole(1)
-        load_x_pair(0)
         load_y(0, 1)
-        load_xs()
         load_y(1, 1)
         load_x_pair(1)
         load_x_pair(2)
-        load_gain()
         load_x_pair(3)
+        load_gain()
         load_x_pair(4)
         load_x_pair(5)
         constants()
+        warm(5)
 
         y_lay(0, 0, 0, 1, on_vector)
         y_lay(0, 0, 2, 2, on_scalar)
-        z_lay_words(0, 1)
-        y_quant(0, 0, 0, 1)
         z_lay_scales(0)
+        y_quant(0, 0, 0, 1)
+        z_lay_words(0, 1)
         zy_half(0, 1, (0,), 0)
         y_lay(0, 0, 1, 1, on_vector)
         z_lay_words(0, 0)
@@ -348,9 +366,11 @@ def tile_coupled_newton_colouring_step_s11_kernel(tc, x_bytes, x_scale, y, z_wor
         zy_half(0, 1, (1,), 0)
         zy_half(0, 0, (1,), 0)
         y_quant(0, 0, 2, 2)
-        for t1 in (2, 3):
-            zy_half(0, 1, (t1,), 0)
-            zy_half(0, 0, (t1,), 0)
+        zy_half(0, 1, (2, 3), 0)
+        cast(0, on_scalar, 0, 1)
+        cast(0, on_vector, 1, 1)
+        turn(0)
+        turn(1)
         y_lay(1, 0, 0, 2, on_vector)
         y_lay(1, 0, 2, 2, on_scalar)
         z_lay_scales(1)
@@ -359,110 +379,100 @@ def tile_coupled_newton_colouring_step_s11_kernel(tc, x_bytes, x_scale, y, z_wor
         zy_half(0, 0, (0, 1), 1)
         z_lay_words(1, 1)
         y_quant(1, 0, 2, 2)
-        zy_half(0, 1, (0, 1), 1)
-        zy_half(0, 0, (2, 3), 1)
-        zy_half(0, 1, (2, 3), 1)
-        cast(0, on_vector, 0, 1)
-        cast(0, on_scalar, 1, 1)
-        y_lay(0, 1, 2, 2, on_vector)
+        zy_half(0, 1, (0, 1, 2, 3), 1)
+        x_out(0)
+        y_lay(0, 1, 2, 2, on_pool, "yi_101")
         y_lay(0, 1, 0, 2, on_scalar)
-        x_perm(0, on_vector)
-        x_perm(1, on_vector)
+        x_out(1)
+        zy(0, 0, (2,))
+        y_quant(0, 1, 0, 2)
+        y_quant(0, 1, 2, 2)
+        c_out(0, 1, 0)
+        zy(0, 0, (3,))
+        c_out(0, 1, 1)
+        y_lay(1, 1, 2, 2, on_pool, "yi_101")
+        x_quant(0)
+        zy_half(1, 0, (2, 3), 0)
+        cast(1, on_scalar)
         c_whole(0, 0)
         c_whole(0, 1)
-        y_quant(0, 1, 2, 2)
-        turn(0)
-        turn(1)
-        y_quant(0, 1, 0, 2)
-        c_out(0, 1, 0)
-        c_out(0, 1, 1)
-        y_lay(1, 1, 2, 2, on_pool, "yi_010")
+        v_mm(0, 0)
         c_whole(0, 2)
-        c_whole(0, 3)
-        zy_half(1, 0, (0, 1, 2, 3), 0)
         y_lay(1, 1, 0, 2, on_scalar)
-        x_out(0)
         y_quant(1, 1, 2, 2)
-        c_out(0, 1, 2)
-        c_out(0, 1, 3)
         y_quant(1, 1, 0, 2)
-        cast(1, on_scalar)
-        zy_half(1, 1, (0, 1), 0)
-        zy_half(1, 0, (2, 3, 0, 1), 1)
-        x_out(1)
-        zy_half(1, 1, (0, 1), 1)
-        x_quant(0)
+        cast(2, on_gpsimd, after="yi_110")
+        turn(2)
+        zy_half(1, 0, (2, 3), 1)
+        c_out(0, 1, 2)
+        turn(3)
+        c_whole(0, 3)
+        c_out(0, 1, 3)
+        zy(1, 0, (0, 1))
+        v_out(0, 0)
+        x_out(2)
+        zy(1, 1, (0, 1))
+        x_out(3)
+        c_quant(0, 0)
+        x_quant(1)
+        c_quant(0, 1)
         c_out(1, 0, 2)
         c_out(1, 0, 3)
-        c_quant(0, 1)
-        c_quant(0, 0)
-        cast(2, on_gpsimd, after="ci_00")
-        cast(3, on_gpsimd, 0, 1)
-        c_whole(1, 0)
-        c_whole(1, 1)
-        v_mm(0, 0)
-        turn(2)
-        turn(3)
+        v_mm(0, 1)
         c_out(1, 0, 0)
         c_out(1, 0, 1)
-        x_out(2)
-        x_out(3)
-        v_mm(0, 1)
-        v_out(0, 0)
+        c_whole(1, 0)
+        c_whole(1, 1)
         zy(1, 1, (2, 3))
-        x_quant(1)
         x_perm(4)
         x_perm(5)
         v_out(0, 1)
-        cast(3, on_scalar, 1, 1)
+        cast(3, on_scalar)
         c_quant(1, 0)
         c_whole(1, 2)
         c_whole(1, 3)
+        v_quant(0)
+        c_quant(1, 1)
+        cast(4, on_gpsimd, after="ci_11")
 
         for pair in range(1, PAIRS - 1):
             a, b, prev = 2 * pair + 2, 2 * pair + 3, 2 * pair - 2
             turn(a)
             turn(b)
             if pair > 1:
-                o_stage(prev - 1, 512)
-            v_quant(pair - 1)
-            if pair == 1:
-                c_quant(1, 1)
-            else:
-                cast(pair + 2, on_gpsimd, after=f"vx{(pair + 1) % 2}")
-                o_pool(prev - 1, 512, "og")
-            if pair == 1:
-                v_mm(pair, 0)
-                v_mm(pair, 1)
-                v_out(pair, 0)
-                v_out(pair, 1)
+                o_stage2(prev - 1)
+                v_quant(pair - 1)
+                if pair < PAIRS - 2:
+                    cast(PAIRS - 1, on_gpsimd, pair - 2, 1, after=f"vx{(pair - 1) % 4}")
+                    o_pool2(prev - 1, f"og{pair % 2}")
+                else:
+                    o_pool2(prev - 1, f"vx{(pair - 1) % 4}")
             x_out(a)
             x_out(b)
-            if pair == 2:
-                o_out(prev - 1, 0)
             if pair > 1:
-                o_out(prev - 2, 512)
-            if pair > 1:
-                v_mm(pair, 0)
-                v_mm(pair, 1)
-                v_out(pair, 0)
-                v_out(pair, 1)
+                o_out(prev - 1, 0, KEPT)
+            v_mm(pair, 0)
+            v_mm(pair, 1)
+            v_out(pair, 0)
+            v_out(pair, 1)
             if pair == PAIRS - 2:
                 x_quant(pair + 1)
             o_part(prev, 0)
             if pair > 1:
-                o_pool_store(prev - 1, 512)
-                o_part(prev + 1, 0)
-            else:
-                o_mm(prev + 1, 0)
+                o_part(prev, 512)
+                o_pool_store2(prev - 1)
             if pair < PAIRS - 2:
                 x_quant(pair + 1)
-            o_mm(prev, 512)
+            if pair == 1:
+                o_mm(prev + 1, 0)
+                o_part(prev, 512)
+            else:
+                o_mm(prev + 1, 0)
             o_mm(prev + 1, 512)
             x_perm(a + 2)
             x_perm(b + 2)
         v_quant(4)
-        o_out(6, 512)
+        o_out(7, 0)
         o_out(7, 512)
         v_mm(5, 0, (0,))
         v_mm(5, 1, (0,))

@@ -336,10 +336,11 @@ def tile_coupled_newton_colouring_step_s11_kernel(tc, x_bytes, x_scale, y, z_wor
             nc.vector.memset(zs_raw[kp][:].bitcast(I32), 0)
         load_y(0, 0)
         load_zs(0)
-        load_z_whole(0)
-        load_xs()
+        load_z(0, 1)
+        load_z(0, 0)
         load_x_pair(0)
         load_y(1, 0)
+        load_xs()
         load_zs(1)
         load_z_whole(1)
         load_y(0, 1)
@@ -385,34 +386,37 @@ def tile_coupled_newton_colouring_step_s11_kernel(tc, x_bytes, x_scale, y, z_wor
         y_lay(0, 1, 0, 2, on_scalar)
         x_out(1)
         zy(0, 0, (2,))
-        y_quant(0, 1, 0, 2)
+        x_quant(0, 0, 1)
+        x_quant(0, 1, 1)
         y_quant(0, 1, 2, 2)
         c_out(0, 1, 0)
         zy(0, 0, (3,))
         c_out(0, 1, 1)
         y_lay(1, 1, 2, 2, on_pool, "yi_101")
-        x_quant(0)
-        zy_half(1, 0, (2, 3), 0)
-        cast(1, on_scalar)
+        y_quant(0, 1, 0, 2)
+        v_mm(0, 0)
+        c_out(0, 1, 2)
+        cast(1, on_scalar, 0, 1)
+        cast(1, on_scalar, 1, 1)
+        turn(2)
         c_whole(0, 0)
         c_whole(0, 1)
-        v_mm(0, 0)
+        zy_half(1, 0, (2, 3), 0)
         c_whole(0, 2)
         y_lay(1, 1, 0, 2, on_scalar)
+        turn(3)
         y_quant(1, 1, 2, 2)
+        zy_half(1, 0, (2, 3), 1)
+        c_whole(0, 3)
         y_quant(1, 1, 0, 2)
         cast(2, on_gpsimd, after="yi_110")
-        turn(2)
-        zy_half(1, 0, (2, 3), 1)
-        c_out(0, 1, 2)
-        turn(3)
-        c_whole(0, 3)
         c_out(0, 1, 3)
         zy(1, 0, (0, 1))
         v_out(0, 0)
         x_out(2)
         zy(1, 1, (0, 1))
         x_out(3)
+        c_whole(1, 0)
         c_quant(0, 0)
         x_quant(1)
         c_quant(0, 1)
@@ -421,19 +425,19 @@ def tile_coupled_newton_colouring_step_s11_kernel(tc, x_bytes, x_scale, y, z_wor
         v_mm(0, 1)
         c_out(1, 0, 0)
         c_out(1, 0, 1)
-        c_whole(1, 0)
-        c_whole(1, 1)
         zy(1, 1, (2, 3))
         x_perm(4)
         x_perm(5)
         v_out(0, 1)
-        cast(3, on_scalar)
         c_quant(1, 0)
+        cast(3, on_gpsimd, 0, 1, after="ci_01")
+        cast(3, on_scalar, 1, 1)
+        c_whole(1, 1)
         c_whole(1, 2)
         c_whole(1, 3)
         v_quant(0)
         c_quant(1, 1)
-        cast(4, on_gpsimd, after="ci_11")
+        cast(4, on_gpsimd, 0, 1, after="ci_11")
 
         for pair in range(1, PAIRS - 1):
             a, b, prev = 2 * pair + 2, 2 * pair + 3, 2 * pair - 2
@@ -441,36 +445,48 @@ def tile_coupled_newton_colouring_step_s11_kernel(tc, x_bytes, x_scale, y, z_wor
             turn(b)
             if pair > 1:
                 o_stage2(prev - 1)
-                v_quant(pair - 1)
-                if pair < PAIRS - 2:
-                    cast(PAIRS - 1, on_gpsimd, pair - 2, 1, after=f"vx{(pair - 1) % 4}")
-                    o_pool2(prev - 1, f"og{pair % 2}")
-                else:
-                    o_pool2(prev - 1, f"vx{(pair - 1) % 4}")
-            x_out(a)
-            x_out(b)
-            if pair > 1:
+                if pair > 2:
+                    v_quant(pair - 1)
+                if pair == 3:
+                    cast(PAIRS - 1, on_gpsimd, 1, 1, after=f"vx{(pair - 1) % 4}")
+                o_pool2(prev - 1, f"vx{(pair - 1) % 4}" if pair == 4 else f"og{pair % 2}")
+                x_out(a)
+                x_out(b)
+                if pair == 2:
+                    o_pool_store(0, 512)
                 o_out(prev - 1, 0, KEPT)
             v_mm(pair, 0)
             v_mm(pair, 1)
             v_out(pair, 0)
             v_out(pair, 1)
+            if pair == 1:
+                x_out(a)
+                x_out(b)
+            if pair == 1:
+                x_quant(pair + 1, 0, 1)
+                x_quant(pair + 1, 1, 1)
             if pair == PAIRS - 2:
                 x_quant(pair + 1)
+            if pair == 1:
+                v_quant(pair)
             o_part(prev, 0)
             if pair > 1:
                 o_part(prev, 512)
                 o_pool_store2(prev - 1)
-            if pair < PAIRS - 2:
+            if 1 < pair < PAIRS - 2:
                 x_quant(pair + 1)
+            o_mm(prev + 1, 0)
             if pair == 1:
-                o_mm(prev + 1, 0)
-                o_part(prev, 512)
-            else:
-                o_mm(prev + 1, 0)
+                o_mm(prev, 512)
             o_mm(prev + 1, 512)
             x_perm(a + 2)
             x_perm(b + 2)
+            if pair == 1:
+                o_stage(prev, 512)
+                o_pool(prev, 512, "vx1")
+                cast(4, on_scalar, 1, 1)
+            if pair == 2:
+                cast(5, on_scalar, 0, 1)
         v_quant(4)
         o_out(7, 0)
         o_out(7, 512)

@@ -95,12 +95,12 @@ def tile_coupled_newton_colouring_step_s11_kernel(tc, x_bytes, x_scale, y, z_wor
                 nc.tensor.matmul(b[:, j % 4, :], lhsT=ident[:], rhs=ident[:], start=True, stop=True)
             give_back("warm")
 
-        yq = keep.tile([P, 2, N], U32, name="yq", align_bytes=64)
-        ys = keep.tile([P, 2, N], U8, name="ys", align_bytes=64)
-        zq = keep.tile([P, 2, 2 * N], U8, name="zq", align_bytes=64)
-        zs = keep.tile([P, 2, N], U8, name="zs", align_bytes=64)
-        cq = keep.tile([P, 2, N], U32, name="cq", align_bytes=64)
-        cs = keep.tile([P, 2, N], U8, name="cs", align_bytes=64)
+        yq = keep.tile([P, 2, N], U32, name="yq", align_bytes=256)
+        ys = keep.tile([P, 2, N], U8, name="ys", align_bytes=256)
+        zq = keep.tile([P, 2, 2 * N], U8, name="zq", align_bytes=256)
+        zs = keep.tile([P, 2, N], U8, name="zs", align_bytes=256)
+        cq = keep.tile([P, 2, N], U32, name="cq", align_bytes=256)
+        cs = keep.tile([P, 2, N], U8, name="cs", align_bytes=256)
         yi = {}
         ci = {}
 
@@ -175,8 +175,8 @@ def tile_coupled_newton_colouring_step_s11_kernel(tc, x_bytes, x_scale, y, z_wor
         def x_quant(pair, s0=0, ns=2):
             if pair < PAIRS:
                 if pair not in xq:
-                    xq[pair] = work.tile([P, 4 * P], U32, name="xq", tag="xq", bufs=3, align_bytes=64)
-                    xqs[pair] = work.tile([P, 4 * P], U8, name="xqs", tag="xqs", bufs=3, align_bytes=64)
+                    xq[pair] = work.tile([P, 4 * P], U32, name="xq", tag="xq", bufs=3, align_bytes=256)
+                    xqs[pair] = work.tile([P, 4 * P], U8, name="xqs", tag="xqs", bufs=3, align_bytes=256)
                 c = slice(2 * P * s0, 2 * P * (s0 + ns))
                 nc.vector.quantize_mx(
                     out=xq[pair][:, c].bitcast(FP8X4), scales=xqs[pair][:, c], in_=xi[pair][:, s0 : s0 + ns].rearrange("p s g m t -> p (s g m t)")
@@ -267,8 +267,8 @@ def tile_coupled_newton_colouring_step_s11_kernel(tc, x_bytes, x_scale, y, z_wor
 
         def v_quant(pair, j0=0, nj=4):
             if pair not in vq:
-                vq[pair] = work.tile([P, 4 * P], U32, name="vq", tag="vq", bufs=3, align_bytes=64)
-                vqs[pair] = work.tile([P, 4 * P], U8, name="vqs", tag="vqs", bufs=3, align_bytes=64)
+                vq[pair] = work.tile([P, 4 * P], U32, name="vq", tag="vq", bufs=3, align_bytes=256)
+                vqs[pair] = work.tile([P, 4 * P], U8, name="vqs", tag="vqs", bufs=3, align_bytes=256)
             c = slice(P * j0, P * (j0 + nj))
             nc.vector.quantize_mx(
                 out=vq[pair][:, c].bitcast(FP8X4),

@@ -22,6 +22,7 @@ P = 128
 TILES = M // P
 PAIRS = TILES // 2
 KEPT = 256
+WIDE = (4,)
 
 
 def tile_coupled_newton_colouring_step_s11_kernel(tc, x_bytes, x_scale, y, z_words, z_scales, gain, out):
@@ -110,7 +111,14 @@ def tile_coupled_newton_colouring_step_s11_kernel(tc, x_bytes, x_scale, y, z_wor
                 yi[kp, h, t0 // 2] = keep.tile([P, 256, 4], BF16, name=name, tag=name, align_bytes=64)
             dst = yi[kp, h, t0 // 2][:].rearrange("p (t q r) j -> p q t r j", t=2, r=8)
             raw = y_raw[kp, h][:].rearrange("p j (q t r) -> p q t r j", t=4, r=8)
-            copy(out=dst[:, :, t0 % 2 : t0 % 2 + nt], in_=raw[:, :, t0 : t0 + nt])
+            if copy is on_pool:
+                copy(out=dst[:, :, t0 % 2 : t0 % 2 + nt], in_=raw[:, :, t0 : t0 + nt])
+            else:
+                for t in range(t0, t0 + nt):
+                    copy(
+                        out=dst[:, :, t % 2].rearrange("p q (a i) j -> p q a j i", i=4),
+                        in_=raw[:, :, t].rearrange("p q (a i) j -> p q a j i", i=4),
+                    )
 
         def y_quant(kp, h, t0, nt):
             lo = 128 * (t0 % 2)
@@ -165,7 +173,7 @@ def tile_coupled_newton_colouring_step_s11_kernel(tc, x_bytes, x_scale, y, z_wor
                     tag = f"xo{i // 2 % 2}"
                     xi[i // 2] = keep.tile([P, 2, 2, P, 4], BF16, name=tag, tag=tag, align_bytes=64)
                 nc.vector.tensor_tensor(
-                    out=xi[i // 2][:, i % 2].rearrange("p g m (u e) -> p g m u e", u=2),
+                    out=(xi[i // 2][:, :, i % 2] if i // 2 in WIDE else xi[i // 2][:, i % 2]).rearrange("p g m (u e) -> p g m u e", u=2),
                     in0=xt[i][:].rearrange("p a m -> p (a m)").bitcast(BF16).rearrange("p (u g m e) -> p g m u e", u=2, g=2, e=2),
                     in1=xs4[:].rearrange("p g (u e) -> p g u e", u=2).unsqueeze(2).to_broadcast([P, 2, P, 2, 2]),
                     op=MULT,
@@ -241,7 +249,27 @@ def tile_coupled_newton_colouring_step_s11_kernel(tc, x_bytes, x_scale, y, z_wor
 
         vps, vi, vq, vqs = {}, {}, {}, {}
 
+        def v_mm_wide(pair, g):
+            for tp in range(2):
+                vps[pair, g, tp] = bank(("v", pair, g, tp))
+                acc = vps[pair, g, tp][:].rearrange("p (t a) m -> p t (a m)", t=2)
+                for tt in range(2):
+                    for kp in range(2):
+                        c0 = 512 * g + 128 * (2 * tp + tt)
+                        c = slice(2 * P * kp, 2 * P * (kp + 1))
+                        nc.tensor.matmul_mx(
+                            out=acc[:, tt, :],
+                            lhsT=yq[:, kp, c0 : c0 + 128].bitcast(FP8X4),
+                            lhsT_scale=ys[:, kp, c0 : c0 + 128],
+                            rhs=xq[pair][:, c].bitcast(FP8X4),
+                            rhs_scale=xqs[pair][:, c],
+                            start=(kp == 0),
+                            stop=(kp == 1),
+                        )
+
         def v_mm(pair, g, tiles=(0, 1)):
+            if pair in WIDE:
+                return v_mm_wide(pair, g)
             for s in tiles:
                 vps[pair, g, s] = bank(("v", pair, g, s))
                 for t in range(4):
@@ -262,7 +290,10 @@ def tile_coupled_newton_colouring_step_s11_kernel(tc, x_bytes, x_scale, y, z_wor
             if pair not in vi:
                 vi[pair] = keep.tile([P, 2, 2, P, 4], BF16, name=f"vx{pair % 4}", tag=f"vx{pair % 4}", align_bytes=64)
             for s in tiles:
-                nc.scalar.copy(out=vi[pair][:, s, g], in_=vps[pair, g, s][:].rearrange("p t m -> p m t"))
+                if pair in WIDE:
+                    nc.scalar.copy(out=vi[pair][:, :, g, :, 2 * s : 2 * s + 2], in_=vps[pair, g, s][:].rearrange("p (t a) m -> p a m t", t=2))
+                else:
+                    nc.scalar.copy(out=vi[pair][:, s, g], in_=vps[pair, g, s][:].rearrange("p t m -> p m t"))
                 give_back(("v", pair, g, s))
 
         def v_quant(pair, j0=0, nj=4):

@@ -22,7 +22,7 @@ P = 128
 TILES = M // P
 PAIRS = TILES // 2
 KEPT = 256
-WIDE = (4,)
+WIDE = (3, 4)
 
 
 def tile_coupled_newton_colouring_step_s11_kernel(tc, x_bytes, x_scale, y, z_words, z_scales, gain, out):
@@ -51,7 +51,7 @@ def tile_coupled_newton_colouring_step_s11_kernel(tc, x_bytes, x_scale, y, z_wor
         zs_raw = [keep.tile([P, N], U8, name=f"zs_raw_{kp}", align_bytes=64) for kp in range(2)]
         gain_bc = keep.tile([P, N], BF16, name="gain_bc", align_bytes=64)
         y_view = y.rearrange("(g p j) n -> g p j n", p=P, j=4)
-        x_view2 = x_bytes.rearrange("(i s p) k -> i p s k", s=2, p=P)
+        x_view2 = x_bytes.rearrange("(i p s) k -> i p s k", s=2, p=P)
         y_raw, zw_raw, xb = {}, {}, {}
 
         def load_xs():
@@ -307,7 +307,8 @@ def tile_coupled_newton_colouring_step_s11_kernel(tc, x_bytes, x_scale, y, z_wor
                 in_=vi[pair][:].rearrange("p g s m t -> p (g s m t)")[:, 4 * P * j0 : 4 * P * (j0 + nj)],
             )
 
-        out_view = out.rearrange("(i p) n -> i p n", p=P)
+        out_pairs = out.rearrange("(i p s) n -> i s p n", s=2, p=P)
+        out_view = [out_pairs[i // 2][i % 2] for i in range(TILES)]
 
         accs, held = {}, {}
 
@@ -367,13 +368,13 @@ def tile_coupled_newton_colouring_step_s11_kernel(tc, x_bytes, x_scale, y, z_wor
             nc.vector.memset(zs_raw[kp][:].bitcast(I32), 0)
         load_y(0, 0)
         load_zs(0)
-        load_z(0, 1)
-        load_z(0, 0)
+        load_z_whole(0)
+        load_xs()
         load_x_pair(0)
         load_y(1, 0)
-        load_xs()
         load_zs(1)
-        load_z_whole(1)
+        load_z(1, 1)
+        load_z(1, 0)
         load_y(0, 1)
         load_y(1, 1)
         load_x_pair(1)
@@ -406,32 +407,32 @@ def tile_coupled_newton_colouring_step_s11_kernel(tc, x_bytes, x_scale, y, z_wor
         y_lay(1, 0, 0, 2, on_vector)
         y_lay(1, 0, 2, 2, on_scalar)
         z_lay_scales(1)
+        z_lay_words(1, 1)
         y_quant(1, 0, 0, 2)
+        zy_half(0, 1, (0, 1), 1)
         z_lay_words(1, 0)
         zy_half(0, 0, (0, 1), 1)
-        z_lay_words(1, 1)
         y_quant(1, 0, 2, 2)
-        zy_half(0, 1, (0, 1, 2, 3), 1)
+        zy_half(0, 1, (2, 3), 1)
         x_out(0)
         y_lay(0, 1, 2, 2, on_pool, "yi_101")
+        c_out(0, 1, 0)
         y_lay(0, 1, 0, 2, on_scalar)
+        zy(0, 0, (2, 3))
         x_out(1)
-        zy(0, 0, (2,))
         x_quant(0, 0, 1)
         x_quant(0, 1, 1)
         y_quant(0, 1, 2, 2)
-        c_out(0, 1, 0)
-        zy(0, 0, (3,))
         c_out(0, 1, 1)
         y_lay(1, 1, 2, 2, on_pool, "yi_101")
         y_quant(0, 1, 0, 2)
         v_mm(0, 0)
-        c_out(0, 1, 2)
         cast(1, on_scalar, 0, 1)
         cast(1, on_scalar, 1, 1)
-        turn(2)
         c_whole(0, 0)
+        turn(2)
         c_whole(0, 1)
+        c_out(0, 1, 2)
         zy_half(1, 0, (2, 3), 0)
         c_whole(0, 2)
         y_lay(1, 1, 0, 2, on_scalar)
@@ -476,12 +477,19 @@ def tile_coupled_newton_colouring_step_s11_kernel(tc, x_bytes, x_scale, y, z_wor
             turn(b)
             if pair > 1:
                 o_stage2(prev - 1)
+                if pair == 3:
+                    x_perm(a + 2)
+                if pair == 4:
+                    x_out(a)
                 if pair > 2:
                     v_quant(pair - 1)
+                if pair == 4:
+                    x_quant(pair + 1, 0, 1)
                 if pair == 3:
                     cast(PAIRS - 1, on_gpsimd, 1, 1, after=f"vx{(pair - 1) % 4}")
                 o_pool2(prev - 1, f"vx{(pair - 1) % 4}" if pair == 4 else f"og{pair % 2}")
-                x_out(a)
+                if pair < 4:
+                    x_out(a)
                 x_out(b)
                 if pair == 2:
                     o_pool_store(0, 512)
@@ -489,6 +497,8 @@ def tile_coupled_newton_colouring_step_s11_kernel(tc, x_bytes, x_scale, y, z_wor
             v_mm(pair, 0)
             v_mm(pair, 1)
             v_out(pair, 0)
+            if pair == 3:
+                x_perm(b + 2)
             v_out(pair, 1)
             if pair == 1:
                 x_out(a)
@@ -496,8 +506,6 @@ def tile_coupled_newton_colouring_step_s11_kernel(tc, x_bytes, x_scale, y, z_wor
             if pair == 1:
                 x_quant(pair + 1, 0, 1)
                 x_quant(pair + 1, 1, 1)
-            if pair == PAIRS - 2:
-                x_quant(pair + 1)
             if pair == 1:
                 v_quant(pair)
             o_part(prev, 0)
@@ -510,14 +518,16 @@ def tile_coupled_newton_colouring_step_s11_kernel(tc, x_bytes, x_scale, y, z_wor
             if pair == 1:
                 o_mm(prev, 512)
             o_mm(prev + 1, 512)
-            x_perm(a + 2)
-            x_perm(b + 2)
+            if pair < 3:
+                x_perm(a + 2)
+                x_perm(b + 2)
             if pair == 1:
                 o_stage(prev, 512)
                 o_pool(prev, 512, "vx1")
                 cast(4, on_scalar, 1, 1)
             if pair == 2:
                 cast(5, on_scalar, 0, 1)
+        x_quant(5, 1, 1)
         v_quant(4)
         o_out(7, 0)
         o_out(7, 512)

@@ -19,10 +19,11 @@ ADD = mybir.AluOpType.add
 COPY = mybir.ActivationFunctionType.Copy
 
 P = 128
-TILES = M // P
-PAIRS = TILES // 2
+HALF = 512
+BANKS = 8
 KEPT = 256
 WIDE = (3, 4)
+WARM_UPS = 5
 
 
 def tile_coupled_newton_colouring_step_s11_kernel(tc, x_bytes, x_scale, y, z_words, z_scales, gain, out):
@@ -34,10 +35,7 @@ def tile_coupled_newton_colouring_step_s11_kernel(tc, x_bytes, x_scale, y, z_wor
         ctx.enter_context(tc.manual_schedule())
         on_vector, on_scalar, on_gpsimd = nc.vector.tensor_copy, nc.scalar.copy, nc.gpsimd.tensor_copy
 
-        def on_pool(out, in_):
-            nc.gpsimd.tensor_scalar(out=out, in0=in_, scalar1=1.0, scalar2=0.0, op0=MULT, op1=ADD)
-
-        free_banks = list(range(8))
+        free_banks = list(range(BANKS))
         taken = {}
 
         def bank(key):
@@ -47,40 +45,36 @@ def tile_coupled_newton_colouring_step_s11_kernel(tc, x_bytes, x_scale, y, z_wor
         def give_back(key):
             free_banks.append(taken[key])
 
-        xs4 = keep.tile([P, 2, 4], F32, name="xs4")
+        scale_cols = keep.tile([P, 2, 4], F32, name="xs4")
         zs_raw = [keep.tile([P, N], U8, name=f"zs_raw_{kp}", align_bytes=64) for kp in range(2)]
-        gain_bc = keep.tile([P, N], BF16, name="gain_bc", align_bytes=64)
+        gain_rows = keep.tile([P, N], BF16, name="gain_bc", align_bytes=64)
         y_view = y.rearrange("(g p j) n -> g p j n", p=P, j=4)
-        x_view2 = x_bytes.rearrange("(i p s) k -> i p s k", s=2, p=P)
-        y_raw, zw_raw, xb = {}, {}, {}
+        x_view = x_bytes.rearrange("(i p s) k -> i p s k", s=2, p=P)
+        out_view = out.rearrange("(i p s) n -> i s p n", s=2, p=P)
+        y_raw, zw_raw, x_raw = {}, {}, {}
 
-        def load_xs():
-            nc.sync.dma_start(out=xs4[:], in_=x_scale.rearrange("o (g p t) -> p (o g) t", p=P, t=4))
+        def load_scale():
+            nc.sync.dma_start(out=scale_cols[:], in_=x_scale.rearrange("o (g p t) -> p (o g) t", p=P, t=4))
 
-        def load_zs(kp):
-            for q in range(4):
-                nc.sync.dma_start(out=zs_raw[kp][32 * q : 32 * q + 4, :].bitcast(I32), in_=z_scales[kp, 4 * q : 4 * q + 4, :].bitcast(I32))
+        def load_z_scales(kp):
+            for quad in range(4):
+                nc.sync.dma_start(out=zs_raw[kp][32 * quad : 32 * quad + 4, :].bitcast(I32), in_=z_scales[kp, 4 * quad : 4 * quad + 4, :].bitcast(I32))
 
         def load_y(kp, h):
-            y_raw[kp, h] = keep.tile([P, 4, 512], BF16, name=f"y_raw_{kp}{h}", align_bytes=64)
-            nc.sync.dma_start(out=y_raw[kp, h][:], in_=y_view[kp][:, :, 512 * h : 512 * h + 512])
+            y_raw[kp, h] = keep.tile([P, 4, HALF], BF16, name=f"y_raw_{kp}{h}", align_bytes=64)
+            nc.sync.dma_start(out=y_raw[kp, h][:], in_=y_view[kp][:, :, HALF * h : HALF * (h + 1)])
 
-        def load_z(kp, g):
-            zw_raw[kp, g] = keep.tile([P, N], U8, name=f"zw_raw_{kp}{g}", align_bytes=64)
-            nc.sync.dma_start(out=zw_raw[kp, g][:].bitcast(I32), in_=z_words[kp][:, N * g : N * (g + 1)].bitcast(I32))
+        def load_z_words(kp):
+            both = keep.tile([P, 2, N], U8, name=f"zw_raw_{kp}", align_bytes=64)
+            nc.sync.dma_start(out=both[:].rearrange("p g n -> p (g n)").bitcast(I32), in_=z_words[kp].bitcast(I32))
+            zw_raw[kp, 0], zw_raw[kp, 1] = both[:, 0], both[:, 1]
 
-        def load_z_whole(kp):
-            t = keep.tile([P, 2, N], U8, name=f"zw_raw_{kp}", align_bytes=64)
-            nc.sync.dma_start(out=t[:].rearrange("p g n -> p (g n)").bitcast(I32), in_=z_words[kp].bitcast(I32))
-            zw_raw[kp, 0], zw_raw[kp, 1] = t[:, 0], t[:, 1]
-
-        def load_x_pair(pair):
-            t = keep.tile([P, 2, N], U8, name=f"xb2_{pair}", align_bytes=64)
-            nc.sync.dma_start(out=t[:], in_=x_view2[pair])
-            xb[pair] = t
+        def load_x(pair):
+            x_raw[pair] = keep.tile([P, 2, N], U8, name=f"xb2_{pair}", align_bytes=64)
+            nc.sync.dma_start(out=x_raw[pair][:], in_=x_view[pair])
 
         def load_gain():
-            nc.sync.dma_start(out=gain_bc[:], in_=gain.partition_broadcast(P))
+            nc.sync.dma_start(out=gain_rows[:], in_=gain.partition_broadcast(P))
 
         ident = keep.tile([P, P], F32, name="ident", align_bytes=64)
         eye15 = keep.tile([P, P, 8], BF16, name="eye15", align_bytes=64)
@@ -90,10 +84,10 @@ def tile_coupled_newton_colouring_step_s11_kernel(tc, x_bytes, x_scale, y, z_wor
             nc.gpsimd.memset(eye15[:].rearrange("p n c -> p (n c)").bitcast(I32), 0)
             nc.vector.tensor_scalar(out=eye15[:, :, 3], in0=ident[:], scalar1=1.5, scalar2=None, op0=MULT)
 
-        def warm(n):
-            b = bank("warm")
-            for j in range(n):
-                nc.tensor.matmul(b[:, j % 4, :], lhsT=ident[:], rhs=ident[:], start=True, stop=True)
+        def warm_up():
+            unread = bank("warm")
+            for j in range(WARM_UPS):
+                nc.tensor.matmul(unread[:, j % 4, :], lhsT=ident[:], rhs=ident[:], start=True, stop=True)
             give_back("warm")
 
         yq = keep.tile([P, 2, N], U32, name="yq", align_bytes=256)
@@ -102,31 +96,33 @@ def tile_coupled_newton_colouring_step_s11_kernel(tc, x_bytes, x_scale, y, z_wor
         zs = keep.tile([P, 2, N], U8, name="zs", align_bytes=256)
         cq = keep.tile([P, 2, N], U32, name="cq", align_bytes=256)
         cs = keep.tile([P, 2, N], U8, name="cs", align_bytes=256)
-        yi = {}
-        ci = {}
+        y_laid, c_laid = {}, {}
 
-        def y_lay(kp, h, t0, nt, copy, tag=None):
-            if (kp, h, t0 // 2) not in yi:
-                name = tag or f"yi_{kp}{h}{t0 // 2}"
-                yi[kp, h, t0 // 2] = keep.tile([P, 256, 4], BF16, name=name, tag=name, align_bytes=64)
-            dst = yi[kp, h, t0 // 2][:].rearrange("p (t q r) j -> p q t r j", t=2, r=8)
-            raw = y_raw[kp, h][:].rearrange("p j (q t r) -> p q t r j", t=4, r=8)
-            if copy is on_pool:
-                copy(out=dst[:, :, t0 % 2 : t0 % 2 + nt], in_=raw[:, :, t0 : t0 + nt])
-            else:
-                for t in range(t0, t0 + nt):
-                    copy(
-                        out=dst[:, :, t % 2].rearrange("p q (a i) j -> p q a j i", i=4),
-                        in_=raw[:, :, t].rearrange("p q (a i) j -> p q a j i", i=4),
-                    )
+        def y_views(kp, h, t0, buffer):
+            if (kp, h, t0 // 2) not in y_laid:
+                y_laid[kp, h, t0 // 2] = keep.tile([P, 2 * P, 4], BF16, name=buffer, tag=buffer, align_bytes=64)
+            laid = y_laid[kp, h, t0 // 2][:].rearrange("p (t q r) j -> p q t r j", t=2, r=8)
+            return laid, y_raw[kp, h][:].rearrange("p j (q t r) -> p q t r j", t=4, r=8)
+
+        def y_lay(kp, h, t0, nt, copy):
+            laid, raw = y_views(kp, h, t0, f"yi_{kp}{h}{t0 // 2}")
+            for t in range(t0, t0 + nt):
+                copy(
+                    out=laid[:, :, t % 2].rearrange("p q (a i) j -> p q a j i", i=4),
+                    in_=raw[:, :, t].rearrange("p q (a i) j -> p q a j i", i=4),
+                )
+
+        def y_lay_gpsimd(kp, h, buffer):
+            laid, raw = y_views(kp, h, 2, buffer)
+            nc.gpsimd.tensor_scalar(out=laid[:, :, 0:2], in0=raw[:, :, 2:4], scalar1=1.0, scalar2=0.0, op0=MULT, op1=ADD)
 
         def y_quant(kp, h, t0, nt):
-            lo = 128 * (t0 % 2)
-            c = slice(512 * h + 128 * t0, 512 * h + 128 * (t0 + nt))
+            lo = P * (t0 % 2)
+            cols = slice(HALF * h + P * t0, HALF * h + P * (t0 + nt))
             nc.vector.quantize_mx(
-                out=yq[:, kp, c].bitcast(FP8X4),
-                scales=ys[:, kp, c],
-                in_=yi[kp, h, t0 // 2][:, lo : lo + 128 * nt].rearrange("p n j -> p (n j)"),
+                out=yq[:, kp, cols].bitcast(FP8X4),
+                scales=ys[:, kp, cols],
+                in_=y_laid[kp, h, t0 // 2][:, lo : lo + P * nt].rearrange("p n j -> p (n j)"),
             )
 
         def z_lay_words(kp, g):
@@ -141,64 +137,60 @@ def tile_coupled_newton_colouring_step_s11_kernel(tc, x_bytes, x_scale, y, z_wor
                 in_=zs_raw[kp][:].bitcast(I32).rearrange("p (g q t r) -> p g t q r", g=2, t=4, r=2),
             )
 
-        xc, xp, xt, xi, xq, xqs = {}, {}, {}, {}, {}, {}
+        x_cast, x_split, x_turned, x_laid, xq, xs = {}, {}, {}, {}, {}, {}
 
-        def cast(pair, copy, s0=0, ns=2, after=None):
-            if pair < PAIRS:
-                tag = after or f"xc{pair}{s0}"
-                t = keep.tile([P, ns, N], BF16, name=tag, tag=tag, align_bytes=64)
-                copy(out=t[:].rearrange("p s k -> p (s k)"), in_=xb[pair][:, s0 : s0 + ns].rearrange("p s k -> p (s k)").bitcast(FP8))
-                for s in range(ns):
-                    xc[2 * pair + s0 + s] = t[:, s]
+        def cast(pair, s0, ns, copy, buffer=None):
+            buffer = buffer or f"xc{pair}{s0}"
+            wide = keep.tile([P, ns, N], BF16, name=buffer, tag=buffer, align_bytes=64)
+            copy(out=wide[:].rearrange("p s k -> p (s k)"), in_=x_raw[pair][:, s0 : s0 + ns].rearrange("p s k -> p (s k)").bitcast(FP8))
+            for s in range(ns):
+                x_cast[2 * pair + s0 + s] = wide[:, s]
 
-        def x_perm(i, copy=on_scalar):
-            if i < TILES:
-                xp[i] = work.tile([P, 2, 2, P], F32, name="xp", tag="xp", bufs=4, align_bytes=64)
-                copy(out=xp[i][:], in_=xc[i].bitcast(F32).rearrange("p (g n u) -> p g u n", g=2, u=2))
+        def split(i, copy=on_scalar):
+            x_split[i] = work.tile([P, 2, 2, P], F32, name="xp", tag="xp", bufs=4, align_bytes=64)
+            copy(out=x_split[i][:], in_=x_cast[i].bitcast(F32).rearrange("p (g n u) -> p g u n", g=2, u=2))
 
         def turn(i):
-            if i < TILES:
-                xt[i] = bank(("x", i))
-                for g in range(2):
-                    for u in range(2):
-                        if i in xp:
-                            words = xp[i][:, g, u, :]
-                        else:
-                            words = xc[i].bitcast(F32)[:, 256 * g + u : 256 * (g + 1) : 2]
-                        nc.tensor.transpose(xt[i][:, 2 * u + g, :], words, ident[:])
+            x_turned[i] = bank(("x", i))
+            for kp in range(2):
+                for u in range(2):
+                    if i in x_split:
+                        words = x_split[i][:, kp, u, :]
+                    else:
+                        words = x_cast[i].bitcast(F32)[:, 2 * P * kp + u : 2 * P * (kp + 1) : 2]
+                    nc.tensor.transpose(x_turned[i][:, 2 * u + kp, :], words, ident[:])
 
         def x_out(i):
-            if i < TILES:
-                if i // 2 not in xi:
-                    tag = f"xo{i // 2 % 2}"
-                    xi[i // 2] = keep.tile([P, 2, 2, P, 4], BF16, name=tag, tag=tag, align_bytes=64)
-                nc.vector.tensor_tensor(
-                    out=(xi[i // 2][:, :, i % 2] if i // 2 in WIDE else xi[i // 2][:, i % 2]).rearrange("p g m (u e) -> p g m u e", u=2),
-                    in0=xt[i][:].rearrange("p a m -> p (a m)").bitcast(BF16).rearrange("p (u g m e) -> p g m u e", u=2, g=2, e=2),
-                    in1=xs4[:].rearrange("p g (u e) -> p g u e", u=2).unsqueeze(2).to_broadcast([P, 2, P, 2, 2]),
-                    op=MULT,
-                )
-                give_back(("x", i))
+            pair, s = divmod(i, 2)
+            if pair not in x_laid:
+                x_laid[pair] = keep.tile([P, 2, 2, P, 4], BF16, name=f"xo{pair % 2}", tag=f"xo{pair % 2}", align_bytes=64)
+            dst = x_laid[pair][:, :, s] if pair in WIDE else x_laid[pair][:, s]
+            nc.vector.tensor_tensor(
+                out=dst.rearrange("p g m (u e) -> p g m u e", u=2),
+                in0=x_turned[i][:].rearrange("p a m -> p (a m)").bitcast(BF16).rearrange("p (u g m e) -> p g m u e", u=2, g=2, e=2),
+                in1=scale_cols[:].rearrange("p g (u e) -> p g u e", u=2).unsqueeze(2).to_broadcast([P, 2, P, 2, 2]),
+                op=MULT,
+            )
+            give_back(("x", i))
 
         def x_quant(pair, s0=0, ns=2):
-            if pair < PAIRS:
-                if pair not in xq:
-                    xq[pair] = work.tile([P, 4 * P], U32, name="xq", tag="xq", bufs=3, align_bytes=256)
-                    xqs[pair] = work.tile([P, 4 * P], U8, name="xqs", tag="xqs", bufs=3, align_bytes=256)
-                c = slice(2 * P * s0, 2 * P * (s0 + ns))
-                nc.vector.quantize_mx(
-                    out=xq[pair][:, c].bitcast(FP8X4), scales=xqs[pair][:, c], in_=xi[pair][:, s0 : s0 + ns].rearrange("p s g m t -> p (s g m t)")
-                )
+            if pair not in xq:
+                xq[pair] = work.tile([P, 4 * P], U32, name="xq", tag="xq", bufs=3, align_bytes=256)
+                xs[pair] = work.tile([P, 4 * P], U8, name="xqs", tag="xqs", bufs=3, align_bytes=256)
+            cols = slice(2 * P * s0, 2 * P * (s0 + ns))
+            nc.vector.quantize_mx(
+                out=xq[pair][:, cols].bitcast(FP8X4), scales=xs[pair][:, cols], in_=x_laid[pair][:, s0 : s0 + ns].rearrange("p s g m t -> p (s g m t)")
+            )
 
-        zps = {}
+        zy_banks = {}
 
-        def zy_pass(h, t1, g, t, kp, start, stop):
-            cols = slice(512 * h + 128 * t1, 512 * h + 128 * t1 + 128)
-            c0 = 512 * g + 128 * t
+        def zy_pass(h, g, t1, t, kp, start, stop):
+            cols = slice(HALF * h + P * t1, HALF * h + P * (t1 + 1))
+            c0 = HALF * g + P * t
             nc.tensor.matmul_mx(
-                out=zps[h, t1, g][:, t, :],
-                lhsT=zq[:, kp, 2 * c0 : 2 * c0 + 256].bitcast(FP4X4),
-                lhsT_scale=zs[:, kp, c0 : c0 + 128],
+                out=zy_banks[h, g, t1][:, t, :],
+                lhsT=zq[:, kp, 2 * c0 : 2 * (c0 + P)].bitcast(FP4X4),
+                lhsT_scale=zs[:, kp, c0 : c0 + P],
                 rhs=yq[:, kp, cols].bitcast(FP8X4),
                 rhs_scale=ys[:, kp, cols],
                 start=start,
@@ -207,347 +199,340 @@ def tile_coupled_newton_colouring_step_s11_kernel(tc, x_bytes, x_scale, y, z_wor
 
         def zy(h, g, t1s):
             for t1 in t1s:
-                zps[h, t1, g] = bank(("c", h, t1, g))
+                zy_banks[h, g, t1] = bank(("c", h, g, t1))
             for t1 in t1s:
                 for t in range(4):
                     for kp in range(2):
-                        zy_pass(h, t1, g, t, kp, kp == 0, kp == 1)
+                        zy_pass(h, g, t1, t, kp, kp == 0, kp == 1)
 
-        def zy_half(h, g, t1s, kp):
-            for t1 in t1s:
-                if kp == 0:
-                    zps[h, t1, g] = bank(("c", h, t1, g))
+        def zy_by_pass(h, g, t1s, kp):
+            if kp == 0:
+                for t1 in t1s:
+                    zy_banks[h, g, t1] = bank(("c", h, g, t1))
             for t1 in t1s:
                 for t in range(4):
-                    zy_pass(h, t1, g, t, kp, kp == 0 and t == 0, kp == 1 and t == 3)
+                    zy_pass(h, g, t1, t, kp, kp == 0 and t == 0, kp == 1 and t == 3)
 
-        def c_dst(h, g, t1):
-            if (g, h) not in ci:
-                ci[g, h] = keep.tile([P, 512, 4], BF16, name=f"ci_{g}{h}", tag=f"ci_{g}{h}", align_bytes=64)
-            return ci[g, h][:].rearrange("p (q t r) f -> p t q r f", t=4, r=8)[:, t1]
+        def c_views(h, g, t1):
+            if (g, h) not in c_laid:
+                c_laid[g, h] = keep.tile([P, HALF, 4], BF16, name=f"ci_{g}{h}", tag=f"ci_{g}{h}", align_bytes=64)
+            dst = c_laid[g, h][:].rearrange("p (q t r) f -> p t q r f", t=4, r=8)[:, t1]
+            return dst, zy_banks[h, g, t1][:].rearrange("p f (q r) -> p q r f", r=8)
 
-        def c_out(h, g, t1, vector=False):
-            src = zps[h, t1, g][:].rearrange("p f (q r) -> p q r f", r=8)
-            if vector:
-                nc.vector.tensor_scalar(out=c_dst(h, g, t1), in0=src, scalar1=-0.5, scalar2=None, op0=MULT)
-            else:
-                nc.scalar.activation(out=c_dst(h, g, t1), in_=src, func=COPY, scale=-0.5)
-            give_back(("c", h, t1, g))
+        def c_out(h, t1):
+            dst, src = c_views(h, 1 - h, t1)
+            nc.scalar.activation(out=dst, in_=src, func=COPY, scale=-0.5)
+            give_back(("c", h, 1 - h, t1))
 
-        def c_whole(h, t1):
-            src = zps[h, t1, h][:].rearrange("p f (q r) -> p q r f", r=8)
+        def c_out_diagonal(h, t1):
+            dst, src = c_views(h, h, t1)
             eye = eye15[:, :, 3 - t1 : 7 - t1].rearrange("p (q r) f -> p q r f", r=8)
-            nc.vector.scalar_tensor_tensor(out=c_dst(h, h, t1), in0=src, scalar=-0.5, in1=eye, op0=MULT, op1=ADD)
-            give_back(("c", h, t1, h))
+            nc.vector.scalar_tensor_tensor(out=dst, in0=src, scalar=-0.5, in1=eye, op0=MULT, op1=ADD)
+            give_back(("c", h, h, t1))
 
         def c_quant(h, g):
-            nc.vector.quantize_mx(
-                out=cq[:, g, 512 * h : 512 * h + 512].bitcast(FP8X4),
-                scales=cs[:, g, 512 * h : 512 * h + 512],
-                in_=ci[g, h][:].rearrange("p n f -> p (n f)"),
-            )
+            cols = slice(HALF * h, HALF * (h + 1))
+            nc.vector.quantize_mx(out=cq[:, g, cols].bitcast(FP8X4), scales=cs[:, g, cols], in_=c_laid[g, h][:].rearrange("p n f -> p (n f)"))
 
-        vps, vi, vq, vqs = {}, {}, {}, {}
+        v_banks, v_laid, vq, vs = {}, {}, {}, {}
 
-        def v_mm_wide(pair, g):
-            for tp in range(2):
-                vps[pair, g, tp] = bank(("v", pair, g, tp))
-                acc = vps[pair, g, tp][:].rearrange("p (t a) m -> p t (a m)", t=2)
-                for tt in range(2):
-                    for kp in range(2):
-                        c0 = 512 * g + 128 * (2 * tp + tt)
-                        c = slice(2 * P * kp, 2 * P * (kp + 1))
-                        nc.tensor.matmul_mx(
-                            out=acc[:, tt, :],
-                            lhsT=yq[:, kp, c0 : c0 + 128].bitcast(FP8X4),
-                            lhsT_scale=ys[:, kp, c0 : c0 + 128],
-                            rhs=xq[pair][:, c].bitcast(FP8X4),
-                            rhs_scale=xqs[pair][:, c],
-                            start=(kp == 0),
-                            stop=(kp == 1),
-                        )
+        def v_sum(acc, pair, g, t, first_col, width):
+            c0 = HALF * g + P * t
+            for kp in range(2):
+                cols = slice(first_col + width * kp, first_col + width * (kp + 1))
+                nc.tensor.matmul_mx(
+                    out=acc,
+                    lhsT=yq[:, kp, c0 : c0 + P].bitcast(FP8X4),
+                    lhsT_scale=ys[:, kp, c0 : c0 + P],
+                    rhs=xq[pair][:, cols].bitcast(FP8X4),
+                    rhs_scale=xs[pair][:, cols],
+                    start=(kp == 0),
+                    stop=(kp == 1),
+                )
 
-        def v_mm(pair, g, tiles=(0, 1)):
-            if pair in WIDE:
-                return v_mm_wide(pair, g)
-            for s in tiles:
-                vps[pair, g, s] = bank(("v", pair, g, s))
-                for t in range(4):
-                    for kp in range(2):
-                        c0 = 512 * g + 128 * t
-                        c = slice(P * (2 * s + kp), P * (2 * s + kp + 1))
-                        nc.tensor.matmul_mx(
-                            out=vps[pair, g, s][:, t, :],
-                            lhsT=yq[:, kp, c0 : c0 + 128].bitcast(FP8X4),
-                            lhsT_scale=ys[:, kp, c0 : c0 + 128],
-                            rhs=xq[pair][:, c].bitcast(FP8X4),
-                            rhs_scale=xqs[pair][:, c],
-                            start=(kp == 0),
-                            stop=(kp == 1),
-                        )
-
-        def v_out(pair, g, tiles=(0, 1)):
-            if pair not in vi:
-                vi[pair] = keep.tile([P, 2, 2, P, 4], BF16, name=f"vx{pair % 4}", tag=f"vx{pair % 4}", align_bytes=64)
-            for s in tiles:
+        def v_mm(pair, g, banks=(0, 1)):
+            for b in banks:
+                v_banks[pair, g, b] = bank(("v", pair, g, b))
                 if pair in WIDE:
-                    nc.scalar.copy(out=vi[pair][:, :, g, :, 2 * s : 2 * s + 2], in_=vps[pair, g, s][:].rearrange("p (t a) m -> p a m t", t=2))
+                    acc = v_banks[pair, g, b][:].rearrange("p (t a) m -> p t (a m)", t=2)
+                    for t in range(2):
+                        v_sum(acc[:, t, :], pair, g, 2 * b + t, 0, 2 * P)
                 else:
-                    nc.scalar.copy(out=vi[pair][:, s, g], in_=vps[pair, g, s][:].rearrange("p t m -> p m t"))
-                give_back(("v", pair, g, s))
+                    for t in range(4):
+                        v_sum(v_banks[pair, g, b][:, t, :], pair, g, t, 2 * P * b, P)
+
+        def v_out(pair, g, banks=(0, 1)):
+            if pair not in v_laid:
+                v_laid[pair] = keep.tile([P, 2, 2, P, 4], BF16, name=f"vx{pair % 4}", tag=f"vx{pair % 4}", align_bytes=64)
+            for b in banks:
+                if pair in WIDE:
+                    nc.scalar.copy(out=v_laid[pair][:, :, g, :, 2 * b : 2 * b + 2], in_=v_banks[pair, g, b][:].rearrange("p (t a) m -> p a m t", t=2))
+                else:
+                    nc.scalar.copy(out=v_laid[pair][:, b, g], in_=v_banks[pair, g, b][:].rearrange("p t m -> p m t"))
+                give_back(("v", pair, g, b))
 
         def v_quant(pair, j0=0, nj=4):
             if pair not in vq:
                 vq[pair] = work.tile([P, 4 * P], U32, name="vq", tag="vq", bufs=3, align_bytes=256)
-                vqs[pair] = work.tile([P, 4 * P], U8, name="vqs", tag="vqs", bufs=3, align_bytes=256)
-            c = slice(P * j0, P * (j0 + nj))
+                vs[pair] = work.tile([P, 4 * P], U8, name="vqs", tag="vqs", bufs=3, align_bytes=256)
+            cols = slice(P * j0, P * (j0 + nj))
             nc.vector.quantize_mx(
-                out=vq[pair][:, c].bitcast(FP8X4),
-                scales=vqs[pair][:, c],
-                in_=vi[pair][:].rearrange("p g s m t -> p (g s m t)")[:, 4 * P * j0 : 4 * P * (j0 + nj)],
+                out=vq[pair][:, cols].bitcast(FP8X4),
+                scales=vs[pair][:, cols],
+                in_=v_laid[pair][:].rearrange("p s g m t -> p (s g m t)")[:, 4 * P * j0 : 4 * P * (j0 + nj)],
             )
 
-        out_pairs = out.rearrange("(i p s) n -> i s p n", s=2, p=P)
-        out_view = [out_pairs[i // 2][i % 2] for i in range(TILES)]
+        o_banks, staged, scaled = {}, {}, {}
 
-        accs, held = {}, {}
-
-        def o_mm(i, c0, width=512):
-            accs[i, c0] = bank(("o", i, c0))[:].rearrange("p a b -> p (a b)")[:, 0:width]
-            c = slice(c0, c0 + width)
+        def o_mm(i, c0, width=HALF):
+            o_banks[i, c0] = bank(("o", i, c0))[:].rearrange("p a b -> p (a b)")[:, 0:width]
+            cols = slice(c0, c0 + width)
             for g in range(2):
-                m = slice(P * (2 * (i % 2) + g), P * (2 * (i % 2) + g + 1))
+                rows = slice(P * (2 * (i % 2) + g), P * (2 * (i % 2) + g + 1))
                 nc.tensor.matmul_mx(
-                    out=accs[i, c0],
-                    lhsT=vq[i // 2][:, m].bitcast(FP8X4),
-                    lhsT_scale=vqs[i // 2][:, m],
-                    rhs=cq[:, g, c].bitcast(FP8X4),
-                    rhs_scale=cs[:, g, c],
+                    out=o_banks[i, c0],
+                    lhsT=vq[i // 2][:, rows].bitcast(FP8X4),
+                    lhsT_scale=vs[i // 2][:, rows],
+                    rhs=cq[:, g, cols].bitcast(FP8X4),
+                    rhs_scale=cs[:, g, cols],
                     start=(g == 0),
                     stop=(g == 1),
                 )
 
-        def o_out(i, c0, width=512):
-            ot = work.tile([P, 512], F32, name="ot", tag="ot", bufs=8, align_bytes=64)
-            nc.vector.tensor_tensor(out=ot[:, 0:width], in0=accs[i, c0][:, 0:width], in1=gain_bc[:, c0 : c0 + width], op=MULT)
+        def o_out(i, c0, width=HALF):
+            result = work.tile([P, HALF], F32, name="ot", tag="ot", bufs=8, align_bytes=64)
+            nc.vector.tensor_tensor(out=result[:, 0:width], in0=o_banks[i, c0][:, 0:width], in1=gain_rows[:, c0 : c0 + width], op=MULT)
             give_back(("o", i, c0))
-            nc.sync.dma_start(out=out_view[i][:, c0 : c0 + width], in_=ot[:, 0:width])
+            nc.sync.dma_start(out=out_view[i // 2][i % 2][:, c0 : c0 + width], in_=result[:, 0:width])
 
-        def o_part(i, c0, width=512):
+        def o_part(i, c0, width=HALF):
             o_mm(i, c0, width)
             o_out(i, c0, width)
 
-        stage = {}
-
         def o_stage(i, c0):
-            stage[i] = work.tile([P, 512], F32, name="stage", tag="stage", bufs=2, align_bytes=64)
-            nc.scalar.copy(out=stage[i][:], in_=accs[i, c0])
-            give_back(("o", i, c0))
+            if c0 == HALF:
+                staged[i] = work.tile([P, HALF], F32, name="stage", tag="stage", bufs=2, align_bytes=64)
+            else:
+                staged[i] = work.tile([P, N - c0], F32, name="stage2", tag="stage2", bufs=2, align_bytes=64)
+                nc.scalar.copy(out=staged[i][:, 0 : HALF - c0], in_=o_banks[i, 0][:, c0:HALF])
+            nc.scalar.copy(out=staged[i][:, HALF - c0 :], in_=o_banks[i, HALF])
+            give_back(("o", i, HALF))
 
-        def o_pool(i, c0, tag):
-            held[i] = keep.tile([P, 512], F32, name=tag, tag=tag, align_bytes=64)
-            nc.gpsimd.tensor_tensor(out=held[i][:], in0=stage[i][:], in1=gain_bc[:, c0 : c0 + 512], op=MULT)
+        def o_gain_gpsimd(i, c0, buffer):
+            scaled[i] = keep.tile([P, N - c0], F32, name=buffer, tag=buffer, align_bytes=64)
+            nc.gpsimd.tensor_tensor(out=scaled[i][:], in0=staged[i][:], in1=gain_rows[:, c0:], op=MULT)
 
-        def o_stage2(i):
-            stage[i] = work.tile([P, N - KEPT], F32, name="stage2", tag="stage2", bufs=2, align_bytes=64)
-            nc.scalar.copy(out=stage[i][:, 0 : 512 - KEPT], in_=accs[i, 0][:, KEPT:512])
-            nc.scalar.copy(out=stage[i][:, 512 - KEPT :], in_=accs[i, 512])
-            give_back(("o", i, 512))
-
-        def o_pool2(i, tag):
-            held[i] = keep.tile([P, N - KEPT], F32, name=tag, tag=tag, align_bytes=64)
-            nc.gpsimd.tensor_tensor(out=held[i][:], in0=stage[i][:], in1=gain_bc[:, KEPT:], op=MULT)
-
-        def o_pool_store2(i):
-            nc.sync.dma_start(out=out_view[i][:, KEPT:], in_=held[i][:])
-
-        def o_pool_store(i, c0):
-            nc.sync.dma_start(out=out_view[i][:, c0 : c0 + 512], in_=held[i][:])
+        def o_store_gpsimd(i, c0):
+            nc.sync.dma_start(out=out_view[i // 2][i % 2][:, c0:], in_=scaled[i][:])
 
         for kp in range(2):
             nc.vector.memset(zs_raw[kp][:].bitcast(I32), 0)
         load_y(0, 0)
-        load_zs(0)
-        load_z_whole(0)
-        load_xs()
-        load_x_pair(0)
+        load_z_scales(0)
+        load_z_words(0)
+        load_x(0)
         load_y(1, 0)
-        load_zs(1)
-        load_z(1, 1)
-        load_z(1, 0)
+        load_z_scales(1)
+        load_z_words(1)
+        load_scale()
         load_y(0, 1)
         load_y(1, 1)
-        load_x_pair(1)
-        load_x_pair(2)
-        load_x_pair(3)
+        for pair in (1, 2, 3):
+            load_x(pair)
         load_gain()
-        load_x_pair(4)
-        load_x_pair(5)
+        for pair in (4, 5):
+            load_x(pair)
         constants()
-        warm(5)
+        warm_up()
 
         y_lay(0, 0, 0, 1, on_vector)
         y_lay(0, 0, 2, 2, on_scalar)
         z_lay_scales(0)
         y_quant(0, 0, 0, 1)
         z_lay_words(0, 1)
-        zy_half(0, 1, (0,), 0)
+        zy_by_pass(0, 1, (0,), 0)
         y_lay(0, 0, 1, 1, on_vector)
         z_lay_words(0, 0)
-        zy_half(0, 0, (0,), 0)
+        zy_by_pass(0, 0, (0,), 0)
         y_quant(0, 0, 1, 1)
-        zy_half(0, 1, (1,), 0)
-        zy_half(0, 0, (1,), 0)
+        zy_by_pass(0, 1, (1,), 0)
+        zy_by_pass(0, 0, (1,), 0)
         y_quant(0, 0, 2, 2)
-        zy_half(0, 1, (2, 3), 0)
-        cast(0, on_scalar, 0, 1)
-        cast(0, on_vector, 1, 1)
+        zy_by_pass(0, 1, (2, 3), 0)
+        cast(0, 0, 1, on_scalar)
+        cast(0, 1, 1, on_vector)
+        split(0, on_vector)
         turn(0)
         turn(1)
+
         y_lay(1, 0, 0, 2, on_vector)
         y_lay(1, 0, 2, 2, on_scalar)
         z_lay_scales(1)
         z_lay_words(1, 1)
         y_quant(1, 0, 0, 2)
-        zy_half(0, 1, (0, 1), 1)
+        zy_by_pass(0, 1, (0, 1), 1)
         z_lay_words(1, 0)
-        zy_half(0, 0, (0, 1), 1)
+        zy_by_pass(0, 0, (0, 1), 1)
         y_quant(1, 0, 2, 2)
-        zy_half(0, 1, (2, 3), 1)
+        zy_by_pass(0, 1, (2, 3), 1)
+
         x_out(0)
-        y_lay(0, 1, 2, 2, on_pool, "yi_101")
-        c_out(0, 1, 0)
+        y_lay_gpsimd(0, 1, buffer="yi_101")
+        c_out(0, 0)
         y_lay(0, 1, 0, 2, on_scalar)
         zy(0, 0, (2, 3))
         x_out(1)
         x_quant(0, 0, 1)
-        x_quant(0, 1, 1)
         y_quant(0, 1, 2, 2)
-        c_out(0, 1, 1)
-        y_lay(1, 1, 2, 2, on_pool, "yi_101")
-        y_quant(0, 1, 0, 2)
+        x_quant(0, 1, 1)
+        c_out(0, 1)
+        y_lay_gpsimd(1, 1, buffer="yi_101")
         v_mm(0, 0)
-        cast(1, on_scalar, 0, 1)
-        cast(1, on_scalar, 1, 1)
-        c_whole(0, 0)
+        c_out(0, 2)
+        cast(1, 0, 1, on_scalar)
+        cast(1, 1, 1, on_scalar)
+        c_out_diagonal(0, 0)
+        zy_by_pass(1, 0, (2, 3), 0)
+        c_out_diagonal(0, 1)
         turn(2)
-        c_whole(0, 1)
-        c_out(0, 1, 2)
-        zy_half(1, 0, (2, 3), 0)
-        c_whole(0, 2)
+        c_out_diagonal(0, 2)
         y_lay(1, 1, 0, 2, on_scalar)
         turn(3)
         y_quant(1, 1, 2, 2)
-        zy_half(1, 0, (2, 3), 1)
-        c_whole(0, 3)
+        y_quant(0, 1, 0, 2)
+        zy_by_pass(1, 0, (2, 3), 1)
+        c_out_diagonal(0, 3)
         y_quant(1, 1, 0, 2)
-        cast(2, on_gpsimd, after="yi_110")
-        c_out(0, 1, 3)
+
+        cast(2, 0, 2, on_gpsimd, buffer="yi_110")
+        c_out(0, 3)
         zy(1, 0, (0, 1))
         v_out(0, 0)
         x_out(2)
         zy(1, 1, (0, 1))
         x_out(3)
-        c_whole(1, 0)
+        c_out_diagonal(1, 0)
         c_quant(0, 0)
         x_quant(1)
         c_quant(0, 1)
-        c_out(1, 0, 2)
-        c_out(1, 0, 3)
+        c_out(1, 2)
+        c_out(1, 3)
         v_mm(0, 1)
-        c_out(1, 0, 0)
-        c_out(1, 0, 1)
+        c_out(1, 0)
+        c_out(1, 1)
         zy(1, 1, (2, 3))
-        x_perm(4)
-        x_perm(5)
+        split(4)
+        split(5)
         v_out(0, 1)
         c_quant(1, 0)
-        cast(3, on_gpsimd, 0, 1, after="ci_01")
-        cast(3, on_scalar, 1, 1)
-        c_whole(1, 1)
-        c_whole(1, 2)
-        c_whole(1, 3)
+        cast(3, 0, 1, on_gpsimd, buffer="ci_01")
+        cast(3, 1, 1, on_scalar)
+        for t1 in (1, 2, 3):
+            c_out_diagonal(1, t1)
         v_quant(0)
         c_quant(1, 1)
-        cast(4, on_gpsimd, 0, 1, after="ci_11")
+        cast(4, 0, 1, on_gpsimd, buffer="ci_11")
 
-        for pair in range(1, PAIRS - 1):
-            a, b, prev = 2 * pair + 2, 2 * pair + 3, 2 * pair - 2
-            turn(a)
-            turn(b)
-            if pair > 1:
-                o_stage2(prev - 1)
-                if pair == 3:
-                    x_perm(a + 2)
-                if pair == 4:
-                    x_out(a)
-                if pair > 2:
-                    v_quant(pair - 1)
-                if pair == 4:
-                    x_quant(pair + 1, 0, 1)
-                if pair == 3:
-                    cast(PAIRS - 1, on_gpsimd, 1, 1, after=f"vx{(pair - 1) % 4}")
-                o_pool2(prev - 1, f"vx{(pair - 1) % 4}" if pair == 4 else f"og{pair % 2}")
-                if pair < 4:
-                    x_out(a)
-                x_out(b)
-                if pair == 2:
-                    o_pool_store(0, 512)
-                o_out(prev - 1, 0, KEPT)
+        def v_both(pair, split_between=None):
             v_mm(pair, 0)
             v_mm(pair, 1)
             v_out(pair, 0)
-            if pair == 3:
-                x_perm(b + 2)
+            if split_between is not None:
+                split(split_between)
             v_out(pair, 1)
-            if pair == 1:
-                x_out(a)
-                x_out(b)
-            if pair == 1:
-                x_quant(pair + 1, 0, 1)
-                x_quant(pair + 1, 1, 1)
-            if pair == 1:
-                v_quant(pair)
-            o_part(prev, 0)
-            if pair > 1:
-                o_part(prev, 512)
-                o_pool_store2(prev - 1)
-            if 1 < pair < PAIRS - 2:
-                x_quant(pair + 1)
-            o_mm(prev + 1, 0)
-            if pair == 1:
-                o_mm(prev, 512)
-            o_mm(prev + 1, 512)
-            if pair < 3:
-                x_perm(a + 2)
-                x_perm(b + 2)
-            if pair == 1:
-                o_stage(prev, 512)
-                o_pool(prev, 512, "vx1")
-                cast(4, on_scalar, 1, 1)
-            if pair == 2:
-                cast(5, on_scalar, 0, 1)
+
+        def even_tile_then_store(pair):
+            o_part(2 * pair, 0)
+            o_part(2 * pair, HALF)
+            o_store_gpsimd(2 * pair - 1, KEPT)
+
+        def odd_tile_mm(pair):
+            o_mm(2 * pair + 1, 0)
+            o_mm(2 * pair + 1, HALF)
+
+        turn(4)
+        turn(5)
+        v_both(1)
+        x_out(4)
+        x_out(5)
+        x_quant(2, 0, 1)
+        x_quant(2, 1, 1)
+        v_quant(1)
+        o_part(0, 0)
+        o_mm(1, 0)
+        o_mm(0, HALF)
+        o_mm(1, HALF)
+        split(6)
+        split(7)
+        o_stage(0, HALF)
+        o_gain_gpsimd(0, HALF, buffer="vx1")
+        cast(4, 1, 1, on_scalar)
+
+        turn(6)
+        turn(7)
+        o_stage(1, KEPT)
+        o_gain_gpsimd(1, KEPT, buffer="og0")
+        x_out(6)
+        x_out(7)
+        o_store_gpsimd(0, HALF)
+        o_out(1, 0, KEPT)
+        v_both(2)
+        even_tile_then_store(1)
+        x_quant(3)
+        odd_tile_mm(1)
+        split(8)
+        split(9)
+        cast(5, 0, 1, on_scalar)
+
+        turn(8)
+        turn(9)
+        o_stage(3, KEPT)
+        split(10)
+        v_quant(2)
+        cast(5, 1, 1, on_gpsimd, buffer="vx2")
+        o_gain_gpsimd(3, KEPT, buffer="og1")
+        x_out(8)
+        x_out(9)
+        o_out(3, 0, KEPT)
+        v_both(3, split_between=11)
+        even_tile_then_store(2)
+        x_quant(4)
+        odd_tile_mm(2)
+
+        turn(10)
+        turn(11)
+        o_stage(5, KEPT)
+        x_out(10)
+        v_quant(3)
+        x_quant(5, 0, 1)
+        o_gain_gpsimd(5, KEPT, buffer="vx3")
+        x_out(11)
+        o_out(5, 0, KEPT)
+        v_both(4)
+        even_tile_then_store(3)
+        odd_tile_mm(3)
+
         x_quant(5, 1, 1)
         v_quant(4)
         o_out(7, 0)
-        o_out(7, 512)
-        v_mm(5, 0, (0,))
-        v_mm(5, 1, (0,))
-        v_out(5, 0, (0,))
-        v_out(5, 1, (0,))
+        o_out(7, HALF)
+        for g in range(2):
+            v_mm(5, g, (0,))
+        for g in range(2):
+            v_out(5, g, (0,))
         o_part(8, 0)
-        o_part(8, 512)
+        o_part(8, HALF)
         v_quant(5, 0, 2)
         o_part(9, 0)
-        v_mm(5, 0, (1,))
-        v_mm(5, 1, (1,))
-        v_out(5, 0, (1,))
-        v_out(5, 1, (1,))
+        for g in range(2):
+            v_mm(5, g, (1,))
+        for g in range(2):
+            v_out(5, g, (1,))
         v_quant(5, 2, 1)
-        o_part(9, 512)
+        o_part(9, HALF)
         v_quant(5, 3, 1)
         o_part(10, 0)
-        o_part(10, 512)
+        o_part(10, HALF)
         o_part(11, 0)
-        o_part(11, 512, 256)
-        o_part(11, 768, 256)
+        o_part(11, HALF, HALF // 2)
+        o_part(11, HALF + HALF // 2, HALF // 2)

@@ -23,7 +23,7 @@ HALF = 512
 BANKS = 8
 KEPT = 256
 WIDE = (3, 4)
-WARM_UPS = 5
+WARM_UPS = 0
 
 
 def tile_coupled_newton_colouring_step_s11_kernel(tc, x_bytes, x_scale, y, z_words, z_scales, gain, out):
@@ -47,6 +47,7 @@ def tile_coupled_newton_colouring_step_s11_kernel(tc, x_bytes, x_scale, y, z_wor
 
         scale_cols = keep.tile([P, 2, 4], F32, name="xs4")
         zs_raw = [keep.tile([P, N], U8, name=f"zs_raw_{kp}", align_bytes=64) for kp in range(2)]
+        scale_rows = keep.tile([P, N], F32, name="xs_bc", align_bytes=64)
         gain_rows = keep.tile([P, N], BF16, name="gain_bc", align_bytes=64)
         y_view = y.rearrange("(g p j) n -> g p j n", p=P, j=4)
         x_view = x_bytes.rearrange("(i p s) k -> i p s k", s=2, p=P)
@@ -56,9 +57,12 @@ def tile_coupled_newton_colouring_step_s11_kernel(tc, x_bytes, x_scale, y, z_wor
         def load_scale():
             nc.sync.dma_start(out=scale_cols[:], in_=x_scale.rearrange("o (g p t) -> p (o g) t", p=P, t=4))
 
+        def load_scale_rows():
+            nc.sync.dma_start(out=scale_rows[:], in_=x_scale.rearrange("o k -> (o k)").partition_broadcast(P))
+
         def load_z_scales(kp):
             for quad in range(4):
-                nc.sync.dma_start(out=zs_raw[kp][32 * quad : 32 * quad + 4, :].bitcast(I32), in_=z_scales[kp, 4 * quad : 4 * quad + 4, :].bitcast(I32))
+                nc.sync.dma_start(out=zs_raw[kp][quad:P:32, :].bitcast(I32), in_=z_scales[kp, quad:16:4, :].bitcast(I32))
 
         def load_y(kp, h):
             y_raw[kp, h] = keep.tile([P, 4, HALF], BF16, name=f"y_raw_{kp}{h}", align_bytes=64)
@@ -68,6 +72,10 @@ def tile_coupled_newton_colouring_step_s11_kernel(tc, x_bytes, x_scale, y, z_wor
             both = keep.tile([P, 2, N], U8, name=f"zw_raw_{kp}", align_bytes=64)
             nc.sync.dma_start(out=both[:].rearrange("p g n -> p (g n)").bitcast(I32), in_=z_words[kp].bitcast(I32))
             zw_raw[kp, 0], zw_raw[kp, 1] = both[:, 0], both[:, 1]
+
+        def load_z_half(kp, g):
+            zw_raw[kp, g] = keep.tile([P, N], U8, name=f"zw_raw_{kp}{g}", align_bytes=64)
+            nc.sync.dma_start(out=zw_raw[kp, g][:].bitcast(I32), in_=z_words[kp][:, N * g : N * (g + 1)].bitcast(I32))
 
         def load_x(pair):
             x_raw[pair] = keep.tile([P, 2, N], U8, name=f"xb2_{pair}", align_bytes=64)
@@ -79,10 +87,16 @@ def tile_coupled_newton_colouring_step_s11_kernel(tc, x_bytes, x_scale, y, z_wor
         ident = keep.tile([P, P], F32, name="ident", align_bytes=64)
         eye15 = keep.tile([P, P, 8], BF16, name="eye15", align_bytes=64)
 
+        ident16 = keep.tile([P, P], BF16, name="ident16", align_bytes=64)
+        ones = keep.tile([P, 1], F32, name="ones", align_bytes=64)
+
         def constants():
-            make_identity(nc, ident[:])
-            nc.gpsimd.memset(eye15[:].rearrange("p n c -> p (n c)").bitcast(I32), 0)
-            nc.vector.tensor_scalar(out=eye15[:, :, 3], in0=ident[:], scalar1=1.5, scalar2=None, op0=MULT)
+            make_identity(nc, ident16[:])
+            nc.vector.memset(ones[:], 1.0)
+
+        def make_eye():
+            nc.vector.tensor_scalar(out=eye15[:, :, 3], in0=ident16[:], scalar1=1.5, scalar2=None, op0=MULT)
+            nc.vector.tensor_copy(out=ident[:], in_=ident16[:])
 
         def warm_up():
             unread = bank("warm")
@@ -138,6 +152,7 @@ def tile_coupled_newton_colouring_step_s11_kernel(tc, x_bytes, x_scale, y, z_wor
             )
 
         x_cast, x_split, x_turned, x_laid, xq, xs = {}, {}, {}, {}, {}, {}
+        plain = set()
 
         def cast(pair, s0, ns, copy, buffer=None):
             buffer = buffer or f"xc{pair}{s0}"
@@ -147,24 +162,68 @@ def tile_coupled_newton_colouring_step_s11_kernel(tc, x_bytes, x_scale, y, z_wor
                 x_cast[2 * pair + s0 + s] = wide[:, s]
 
         def split(i, copy=on_scalar):
-            x_split[i] = work.tile([P, 2, 2, P], F32, name="xp", tag="xp", bufs=4, align_bytes=64)
-            copy(out=x_split[i][:], in_=x_cast[i].bitcast(F32).rearrange("p (g n u) -> p g u n", g=2, u=2))
+            x_split[i] = work.tile([P, 2, 2 * P], F32, name="xp", tag="xp", bufs=4, align_bytes=64)
+            copy(out=x_split[i][:], in_=x_cast[i].bitcast(F32).rearrange("p (n u) -> p u n", u=2))
+
+        def cast_split(i):
+            x_split[i] = work.tile([P, 2, 2 * P], F32, name="xp", tag="xp", bufs=4, align_bytes=64)
+            nc.vector.tensor_scalar(
+                out=x_split[i][:].bitcast(BF16).rearrange("p u (n e) -> p n u e", e=2),
+                in0=x_raw[i // 2][:, i % 2].bitcast(FP8).rearrange("p (n u e) -> p n u e", u=2, e=2),
+                scalar1=ones[:],
+                scalar2=None,
+                op0=MULT,
+            )
+
+        def scale_split(i, buffer):
+            x_split[i] = keep.tile([P, 2, 2 * P], F32, name=buffer, tag=buffer, align_bytes=64)
+            nc.gpsimd.tensor_tensor(
+                out=x_split[i][:].bitcast(BF16).rearrange("p u (n e) -> p u n e", e=2),
+                in0=x_cast[i].rearrange("p (n u e) -> p u n e", u=2, e=2),
+                in1=scale_rows[:].rearrange("p (n u e) -> p u n e", u=2, e=2),
+                op=MULT,
+            )
+
+        def turn_plain(i, kps=(0, 1)):
+            if 0 in kps:
+                x_turned[i] = bank(("x", i))
+                plain.add(i)
+            planes = x_turned[i][:].rearrange("p a m -> p (a m)").bitcast(BF16).rearrange("p (g j m) -> p g j m", g=2, j=4)
+            for kp in kps:
+                for j in range(4):
+                    nc.tensor.matmul(planes[:, kp, j, :], lhsT=x_cast[i][:, HALF * kp + j : HALF * (kp + 1) : 4], rhs=ident16[:], start=True, stop=True)
 
         def turn(i):
             x_turned[i] = bank(("x", i))
             for kp in range(2):
                 for u in range(2):
                     if i in x_split:
-                        words = x_split[i][:, kp, u, :]
+                        words = x_split[i][:, u, P * kp : P * (kp + 1)]
                     else:
                         words = x_cast[i].bitcast(F32)[:, 2 * P * kp + u : 2 * P * (kp + 1) : 2]
                     nc.tensor.transpose(x_turned[i][:, 2 * u + kp, :], words, ident[:])
 
-        def x_out(i):
+        def x_dst(i):
             pair, s = divmod(i, 2)
             if pair not in x_laid:
                 x_laid[pair] = keep.tile([P, 2, 2, P, 4], BF16, name=f"xo{pair % 2}", tag=f"xo{pair % 2}", align_bytes=64)
-            dst = x_laid[pair][:, :, s] if pair in WIDE else x_laid[pair][:, s]
+            return x_laid[pair][:, :, s] if pair in WIDE else x_laid[pair][:, s]
+
+        def x_copy_out(i):
+            nc.scalar.copy(out=x_dst(i).bitcast(F32), in_=x_turned[i][:].rearrange("p (u g) m -> p g m u", u=2))
+            give_back(("x", i))
+
+        def x_out(i):
+            dst = x_dst(i)
+            if i in plain:
+                nc.vector.tensor_tensor(
+                    out=dst,
+                    in0=x_turned[i][:].rearrange("p a m -> p (a m)").bitcast(BF16).rearrange("p (g j m) -> p g m j", g=2, j=4),
+                    in1=scale_cols[:].unsqueeze(2).to_broadcast([P, 2, P, 4]),
+                    op=MULT,
+                )
+                give_back(("x", i))
+                return
             nc.vector.tensor_tensor(
                 out=dst.rearrange("p g m (u e) -> p g m u e", u=2),
                 in0=x_turned[i][:].rearrange("p a m -> p (a m)").bitcast(BF16).rearrange("p (u g m e) -> p g m u e", u=2, g=2, e=2),
@@ -327,192 +386,198 @@ def tile_coupled_newton_colouring_step_s11_kernel(tc, x_bytes, x_scale, y, z_wor
 
         for kp in range(2):
             nc.vector.memset(zs_raw[kp][:].bitcast(I32), 0)
+        nc.vector.memset(eye15[:].rearrange("p n c -> p (n c)").bitcast(I32), 0)
+        load_x(0)
         load_y(0, 0)
         load_z_scales(0)
-        load_z_words(0)
-        load_x(0)
+        load_z_half(0, 1)
+        load_z_half(0, 0)
+        load_scale()
+        load_x(1)
         load_y(1, 0)
         load_z_scales(1)
-        load_z_words(1)
-        load_scale()
+        load_z_half(1, 1)
+        load_z_half(1, 0)
         load_y(0, 1)
         load_y(1, 1)
-        for pair in (1, 2, 3):
-            load_x(pair)
+        load_x(2)
+        load_scale_rows()
+        load_x(3)
         load_gain()
         for pair in (4, 5):
             load_x(pair)
         constants()
-        warm_up()
 
+        cast(0, 0, 1, on_vector)
+        cast(0, 1, 1, on_scalar)
+        make_eye()
+        turn_plain(0)
+        turn_plain(1)
         y_lay(0, 0, 0, 1, on_vector)
+        y_lay(0, 0, 1, 1, on_scalar)
         y_lay(0, 0, 2, 2, on_scalar)
-        z_lay_scales(0)
         y_quant(0, 0, 0, 1)
+        z_lay_scales(0)
         z_lay_words(0, 1)
         zy_by_pass(0, 1, (0,), 0)
-        y_lay(0, 0, 1, 1, on_vector)
-        z_lay_words(0, 0)
-        zy_by_pass(0, 0, (0,), 0)
         y_quant(0, 0, 1, 1)
+        z_lay_words(0, 0)
         zy_by_pass(0, 1, (1,), 0)
-        zy_by_pass(0, 0, (1,), 0)
-        y_quant(0, 0, 2, 2)
-        zy_by_pass(0, 1, (2, 3), 0)
-        cast(0, 0, 1, on_scalar)
-        cast(0, 1, 1, on_vector)
-        split(0, on_vector)
-        turn(0)
-        turn(1)
+        zy_by_pass(0, 0, (0, 1), 0)
+        y_quant(0, 0, 2, 1)
+        x_out(0)
+        zy_by_pass(0, 1, (2,), 0)
+        y_quant(0, 0, 3, 1)
+        zy_by_pass(0, 1, (3,), 0)
+        cast(1, 0, 1, on_scalar)
+        x_out(1)
+        cast(1, 1, 1, on_scalar)
+        turn_plain(2)
+        turn_plain(3)
 
-        y_lay(1, 0, 0, 2, on_vector)
+        y_lay(1, 0, 0, 1, on_vector)
+        y_lay(1, 0, 1, 1, on_scalar)
         y_lay(1, 0, 2, 2, on_scalar)
         z_lay_scales(1)
+        y_quant(1, 0, 0, 1)
         z_lay_words(1, 1)
-        y_quant(1, 0, 0, 2)
-        zy_by_pass(0, 1, (0, 1), 1)
+        zy_by_pass(0, 1, (0,), 1)
+        y_quant(1, 0, 1, 1)
         z_lay_words(1, 0)
+        zy_by_pass(0, 1, (1,), 1)
         zy_by_pass(0, 0, (0, 1), 1)
+        x_quant(0)
         y_quant(1, 0, 2, 2)
         zy_by_pass(0, 1, (2, 3), 1)
 
-        x_out(0)
         y_lay_gpsimd(0, 1, buffer="yi_101")
         c_out(0, 0)
-        y_lay(0, 1, 0, 2, on_scalar)
-        zy(0, 0, (2, 3))
-        x_out(1)
-        x_quant(0, 0, 1)
-        y_quant(0, 1, 2, 2)
-        x_quant(0, 1, 1)
         c_out(0, 1)
-        y_lay_gpsimd(1, 1, buffer="yi_101")
+        zy(0, 0, (2, 3))
+        x_out(2)
+        y_lay(0, 1, 0, 2, on_scalar)
+        x_out(3)
         v_mm(0, 0)
         c_out(0, 2)
-        cast(1, 0, 1, on_scalar)
-        cast(1, 1, 1, on_scalar)
-        c_out_diagonal(0, 0)
-        zy_by_pass(1, 0, (2, 3), 0)
-        c_out_diagonal(0, 1)
-        turn(2)
-        c_out_diagonal(0, 2)
-        y_lay(1, 1, 0, 2, on_scalar)
-        turn(3)
-        y_quant(1, 1, 2, 2)
-        y_quant(0, 1, 0, 2)
-        zy_by_pass(1, 0, (2, 3), 1)
-        c_out_diagonal(0, 3)
-        y_quant(1, 1, 0, 2)
-
-        cast(2, 0, 2, on_gpsimd, buffer="yi_110")
-        c_out(0, 3)
-        zy(1, 0, (0, 1))
-        v_out(0, 0)
-        x_out(2)
-        zy(1, 1, (0, 1))
-        x_out(3)
-        c_out_diagonal(1, 0)
-        c_quant(0, 0)
+        y_quant(0, 1, 2, 2)
         x_quant(1)
+        y_quant(0, 1, 0, 2)
+        y_lay_gpsimd(1, 1, buffer="yi_010")
+        c_out(0, 3)
+        v_mm(1, 0)
+        c_out_diagonal(0, 0)
+        c_out_diagonal(0, 1)
+        y_lay(1, 1, 0, 2, on_scalar)
+        c_out_diagonal(0, 2)
+        v_out(0, 0)
+        zy_by_pass(1, 0, (0, 1, 2, 3), 0)
+        y_quant(1, 1, 2, 2)
+        y_quant(1, 1, 0, 2)
+        c_out_diagonal(0, 3)
+        zy_by_pass(1, 0, (2, 3, 0, 1), 1)
+        cast(3, 0, 1, on_scalar)
+        v_out(1, 0)
+        zy(1, 1, (0, 1))
         c_quant(0, 1)
+        c_quant(0, 0)
+        cast_split(4)
+        cast_split(5)
+        scale_split(6, "ci_00")
         c_out(1, 2)
         c_out(1, 3)
-        v_mm(0, 1)
+        zy(1, 1, (2, 3))
         c_out(1, 0)
         c_out(1, 1)
-        zy(1, 1, (2, 3))
-        split(4)
-        split(5)
-        v_out(0, 1)
-        c_quant(1, 0)
-        cast(3, 0, 1, on_gpsimd, buffer="ci_01")
         cast(3, 1, 1, on_scalar)
-        for t1 in (1, 2, 3):
-            c_out_diagonal(1, t1)
-        v_quant(0)
-        c_quant(1, 1)
-        cast(4, 0, 1, on_gpsimd, buffer="ci_11")
-
-        def v_both(pair, split_between=None):
-            v_mm(pair, 0)
-            v_mm(pair, 1)
-            v_out(pair, 0)
-            if split_between is not None:
-                split(split_between)
-            v_out(pair, 1)
-
-        def even_tile_then_store(pair):
-            o_part(2 * pair, 0)
-            o_part(2 * pair, HALF)
-            o_store_gpsimd(2 * pair - 1, KEPT)
-
-        def odd_tile_mm(pair):
-            o_mm(2 * pair + 1, 0)
-            o_mm(2 * pair + 1, HALF)
-
+        c_out_diagonal(1, 0)
+        c_out_diagonal(1, 1)
+        v_mm(0, 1)
+        c_out_diagonal(1, 2)
+        c_out_diagonal(1, 3)
         turn(4)
         turn(5)
-        v_both(1)
-        x_out(4)
-        x_out(5)
-        x_quant(2, 0, 1)
-        x_quant(2, 1, 1)
-        v_quant(1)
-        o_part(0, 0)
-        o_mm(1, 0)
-        o_mm(0, HALF)
-        o_mm(1, HALF)
-        split(6)
+        v_out(0, 1)
         split(7)
-        o_stage(0, HALF)
-        o_gain_gpsimd(0, HALF, buffer="vx1")
-        cast(4, 1, 1, on_scalar)
-
-        turn(6)
-        turn(7)
-        o_stage(1, KEPT)
-        o_gain_gpsimd(1, KEPT, buffer="og0")
-        x_out(6)
-        x_out(7)
-        o_store_gpsimd(0, HALF)
-        o_out(1, 0, KEPT)
-        v_both(2)
-        even_tile_then_store(1)
-        x_quant(3)
-        odd_tile_mm(1)
-        split(8)
-        split(9)
+        v_mm(1, 1)
+        c_quant(1, 0)
+        v_quant(0)
+        v_out(1, 1)
+        cast(4, 0, 1, on_scalar)
         cast(5, 0, 1, on_scalar)
 
-        turn(8)
-        turn(9)
-        o_stage(3, KEPT)
-        split(10)
+        def out_mm(pair):
+            for i in (2 * pair, 2 * pair + 1):
+                o_mm(i, 0)
+                o_mm(i, HALF)
+
+        def out_out(pair):
+            for i in (2 * pair, 2 * pair + 1):
+                o_out(i, 0)
+                o_out(i, HALF)
+
+        o_mm(0, 0)
+        o_mm(1, 0)
+        x_out(4)
+        c_quant(1, 1)
+        turn(6)
+        turn(7)
+        o_mm(0, HALF)
+        o_mm(1, HALF)
+        x_quant(2, 0, 1)
+        x_out(5)
+        x_copy_out(6)
+        cast(4, 1, 1, on_scalar)
+        v_quant(1)
+        x_quant(2, 1, 1)
+        scale_split(8, "xo0")
+        v_mm(2, 0, (0,))
+        o_out(0, 0)
+        v_mm(2, 1, (0,))
+        o_out(1, 0)
+        o_out(0, HALF)
+        o_out(1, HALF)
+        v_mm(2, 0, (1,))
+        v_mm(2, 1, (1,))
+        split(9)
+        v_out(2, 0, (0,))
+        v_out(2, 1, (0,))
+        v_out(2, 0, (1,))
+        v_out(2, 1, (1,))
+        x_out(7)
+        out_mm(1)
+        cast(5, 1, 1, on_scalar)
+        x_quant(3)
         v_quant(2)
-        cast(5, 1, 1, on_gpsimd, buffer="vx2")
-        o_gain_gpsimd(3, KEPT, buffer="og1")
-        x_out(8)
+        scale_split(10, "vx2")
+        turn(9)
+        turn(8)
+        out_out(1)
+        x_copy_out(8)
+        v_mm(3, 0)
         x_out(9)
-        o_out(3, 0, KEPT)
-        v_both(3, split_between=11)
-        even_tile_then_store(2)
+        split(11)
+        v_out(3, 0)
+        v_mm(3, 1)
+        v_out(3, 1)
+        out_mm(2)
+        o_out(4, 0)
         x_quant(4)
-        odd_tile_mm(2)
-
-        turn(10)
+        o_out(4, HALF)
+        o_out(5, 0)
+        o_out(5, HALF)
         turn(11)
-        o_stage(5, KEPT)
-        x_out(10)
+        turn(10)
+        v_mm(4, 0)
         v_quant(3)
-        x_quant(5, 0, 1)
-        o_gain_gpsimd(5, KEPT, buffer="vx3")
         x_out(11)
-        o_out(5, 0, KEPT)
-        v_both(4)
-        even_tile_then_store(3)
-        odd_tile_mm(3)
-
-        x_quant(5, 1, 1)
+        x_copy_out(10)
+        v_out(4, 0)
+        v_mm(4, 1)
+        v_out(4, 1)
+        out_mm(3)
+        x_quant(5)
+        o_out(6, 0)
+        o_out(6, HALF)
         v_quant(4)
         o_out(7, 0)
         o_out(7, HALF)

@@ -23,7 +23,7 @@ HALF = 512
 BANKS = 8
 KEPT = 256
 WIDE = (3, 4)
-WARM_UPS = 0
+WARM_UPS = 5
 
 
 def tile_coupled_newton_colouring_step_s11_kernel(tc, x_bytes, x_scale, y, z_words, z_scales, gain, out):
@@ -46,7 +46,7 @@ def tile_coupled_newton_colouring_step_s11_kernel(tc, x_bytes, x_scale, y, z_wor
             free_banks.append(taken[key])
 
         scale_cols = keep.tile([P, 2, 4], F32, name="xs4")
-        zs_raw = [keep.tile([P, N], U8, name=f"zs_raw_{kp}", align_bytes=64) for kp in range(2)]
+        zs_raw = keep.tile([P, 2, N], U8, name="zs_raw", align_bytes=64)
         scale_rows = keep.tile([P, N], F32, name="xs_bc", align_bytes=64)
         gain_rows = keep.tile([P, N], BF16, name="gain_bc", align_bytes=64)
         y_view = y.rearrange("(g p j) n -> g p j n", p=P, j=4)
@@ -60,9 +60,10 @@ def tile_coupled_newton_colouring_step_s11_kernel(tc, x_bytes, x_scale, y, z_wor
         def load_scale_rows():
             nc.sync.dma_start(out=scale_rows[:], in_=x_scale.rearrange("o k -> (o k)").partition_broadcast(P))
 
-        def load_z_scales(kp):
+        def load_z_scales():
+            rows = z_scales.bitcast(I32).rearrange("g q n -> q g n")
             for quad in range(4):
-                nc.sync.dma_start(out=zs_raw[kp][quad:P:32, :].bitcast(I32), in_=z_scales[kp, quad:16:4, :].bitcast(I32))
+                nc.sync.dma_start(out=zs_raw[quad:P:32].bitcast(I32), in_=rows[quad:16:4])
 
         def load_y(kp, h):
             y_raw[kp, h] = keep.tile([P, 4, HALF], BF16, name=f"y_raw_{kp}{h}", align_bytes=64)
@@ -87,20 +88,18 @@ def tile_coupled_newton_colouring_step_s11_kernel(tc, x_bytes, x_scale, y, z_wor
         ident = keep.tile([P, P], F32, name="ident", align_bytes=64)
         eye15 = keep.tile([P, P, 8], BF16, name="eye15", align_bytes=64)
 
-        ident16 = keep.tile([P, P], BF16, name="ident16", align_bytes=64)
         ones = keep.tile([P, 1], F32, name="ones", align_bytes=64)
 
         def constants():
-            make_identity(nc, ident16[:])
+            make_identity(nc, ident[:])
             nc.vector.memset(ones[:], 1.0)
 
         def make_eye():
-            nc.vector.tensor_scalar(out=eye15[:, :, 3], in0=ident16[:], scalar1=1.5, scalar2=None, op0=MULT)
-            nc.vector.tensor_copy(out=ident[:], in_=ident16[:])
+            nc.vector.tensor_scalar(out=eye15[:, :, 3], in0=ident[:], scalar1=1.5, scalar2=None, op0=MULT)
 
-        def warm_up():
+        def warm_up(count):
             unread = bank("warm")
-            for j in range(WARM_UPS):
+            for j in range(count):
                 nc.tensor.matmul(unread[:, j % 4, :], lhsT=ident[:], rhs=ident[:], start=True, stop=True)
             give_back("warm")
 
@@ -148,11 +147,11 @@ def tile_coupled_newton_colouring_step_s11_kernel(tc, x_bytes, x_scale, y, z_wor
         def z_lay_scales(kp):
             nc.vector.tensor_copy(
                 out=zs[:, kp].bitcast(I32).rearrange("p (g t q r) -> p g t q r", g=2, t=4, r=2),
-                in_=zs_raw[kp][:].bitcast(I32).rearrange("p (g q t r) -> p g t q r", g=2, t=4, r=2),
+                in_=zs_raw[:, kp].bitcast(I32).rearrange("p (g q t r) -> p g t q r", g=2, t=4, r=2),
             )
 
         x_cast, x_split, x_turned, x_laid, xq, xs = {}, {}, {}, {}, {}, {}
-        plain = set()
+
 
         def cast(pair, s0, ns, copy, buffer=None):
             buffer = buffer or f"xc{pair}{s0}"
@@ -184,15 +183,6 @@ def tile_coupled_newton_colouring_step_s11_kernel(tc, x_bytes, x_scale, y, z_wor
                 op=MULT,
             )
 
-        def turn_plain(i, kps=(0, 1)):
-            if 0 in kps:
-                x_turned[i] = bank(("x", i))
-                plain.add(i)
-            planes = x_turned[i][:].rearrange("p a m -> p (a m)").bitcast(BF16).rearrange("p (g j m) -> p g j m", g=2, j=4)
-            for kp in kps:
-                for j in range(4):
-                    nc.tensor.matmul(planes[:, kp, j, :], lhsT=x_cast[i][:, HALF * kp + j : HALF * (kp + 1) : 4], rhs=ident16[:], start=True, stop=True)
-
         def turn(i):
             x_turned[i] = bank(("x", i))
             for kp in range(2):
@@ -215,15 +205,6 @@ def tile_coupled_newton_colouring_step_s11_kernel(tc, x_bytes, x_scale, y, z_wor
 
         def x_out(i):
             dst = x_dst(i)
-            if i in plain:
-                nc.vector.tensor_tensor(
-                    out=dst,
-                    in0=x_turned[i][:].rearrange("p a m -> p (a m)").bitcast(BF16).rearrange("p (g j m) -> p g m j", g=2, j=4),
-                    in1=scale_cols[:].unsqueeze(2).to_broadcast([P, 2, P, 4]),
-                    op=MULT,
-                )
-                give_back(("x", i))
-                return
             nc.vector.tensor_tensor(
                 out=dst.rearrange("p g m (u e) -> p g m u e", u=2),
                 in0=x_turned[i][:].rearrange("p a m -> p (a m)").bitcast(BF16).rearrange("p (u g m e) -> p g m u e", u=2, g=2, e=2),
@@ -384,25 +365,23 @@ def tile_coupled_newton_colouring_step_s11_kernel(tc, x_bytes, x_scale, y, z_wor
         def o_store_gpsimd(i, c0):
             nc.sync.dma_start(out=out_view[i // 2][i % 2][:, c0:], in_=scaled[i][:])
 
-        for kp in range(2):
-            nc.vector.memset(zs_raw[kp][:].bitcast(I32), 0)
+        nc.vector.memset(zs_raw[:].rearrange("p g n -> p (g n)").bitcast(I32), 0)
         nc.vector.memset(eye15[:].rearrange("p n c -> p (n c)").bitcast(I32), 0)
         load_x(0)
         load_y(0, 0)
-        load_z_scales(0)
+        load_z_scales()
         load_z_half(0, 1)
         load_z_half(0, 0)
         load_scale()
         load_x(1)
         load_y(1, 0)
-        load_z_scales(1)
         load_z_half(1, 1)
         load_z_half(1, 0)
         load_y(0, 1)
         load_y(1, 1)
         load_x(2)
-        load_scale_rows()
         load_x(3)
+        load_scale_rows()
         load_gain()
         for pair in (4, 5):
             load_x(pair)
@@ -411,10 +390,11 @@ def tile_coupled_newton_colouring_step_s11_kernel(tc, x_bytes, x_scale, y, z_wor
         cast(0, 0, 1, on_vector)
         cast(0, 1, 1, on_scalar)
         make_eye()
-        turn_plain(0)
-        turn_plain(1)
-        y_lay(0, 0, 0, 1, on_vector)
-        y_lay(0, 0, 1, 1, on_scalar)
+        warm_up(2)
+        turn(0)
+        turn(1)
+        warm_up(2)
+        y_lay(0, 0, 0, 2, on_vector)
         y_lay(0, 0, 2, 2, on_scalar)
         y_quant(0, 0, 0, 1)
         z_lay_scales(0)
@@ -424,28 +404,27 @@ def tile_coupled_newton_colouring_step_s11_kernel(tc, x_bytes, x_scale, y, z_wor
         z_lay_words(0, 0)
         zy_by_pass(0, 1, (1,), 0)
         zy_by_pass(0, 0, (0, 1), 0)
-        y_quant(0, 0, 2, 1)
+        y_quant(0, 0, 2, 2)
+        cast(1, 1, 1, on_gpsimd, buffer="yi_001")
+        zy_by_pass(0, 1, (2, 3), 0)
         x_out(0)
-        zy_by_pass(0, 1, (2,), 0)
-        y_quant(0, 0, 3, 1)
-        zy_by_pass(0, 1, (3,), 0)
         cast(1, 0, 1, on_scalar)
         x_out(1)
-        cast(1, 1, 1, on_scalar)
-        turn_plain(2)
-        turn_plain(3)
+        turn(2)
+        turn(3)
 
-        y_lay(1, 0, 0, 1, on_vector)
-        y_lay(1, 0, 1, 1, on_scalar)
-        y_lay(1, 0, 2, 2, on_scalar)
+        y_lay(1, 0, 0, 2, on_scalar)
         z_lay_scales(1)
-        y_quant(1, 0, 0, 1)
         z_lay_words(1, 1)
+        y_quant(1, 0, 0, 1)
         zy_by_pass(0, 1, (0,), 1)
-        y_quant(1, 0, 1, 1)
         z_lay_words(1, 0)
+        zy_by_pass(0, 0, (0,), 1)
+        y_lay(1, 0, 2, 1, on_vector)
+        y_lay(1, 0, 3, 1, on_scalar)
+        y_quant(1, 0, 1, 1)
         zy_by_pass(0, 1, (1,), 1)
-        zy_by_pass(0, 0, (0, 1), 1)
+        zy_by_pass(0, 0, (1,), 1)
         x_quant(0)
         y_quant(1, 0, 2, 2)
         zy_by_pass(0, 1, (2, 3), 1)

@@ -138,18 +138,21 @@ def tile_coupled_newton_colouring_step_s11_kernel(tc, x_bytes, x_scale, y, z_wor
                 in_=y_laid[kp, h, t0 // 2][:, lo : lo + P * nt].rearrange("p n j -> p (n j)"),
             )
 
-        def z_lay_words(kp, g):
-            nc.vector.tensor_copy(
-                out=zq[:, kp, N * g : N * (g + 1)].bitcast(I32).rearrange("p (t q r) -> p t q r", t=4, r=4),
-                in_=zw_raw[kp, g][:].bitcast(I32).rearrange("p (q t r) -> p t q r", t=4, r=4),
+        def z_lay_words(kp, g, copy=on_vector):
+            word = U32 if copy is on_scalar else I32
+            copy(
+                out=zq[:, kp, N * g : N * (g + 1)].bitcast(word).rearrange("p (t q r) -> p t q r", t=4, r=4),
+                in_=zw_raw[kp, g][:].bitcast(word).rearrange("p (q t r) -> p t q r", t=4, r=4),
             )
 
-        def z_lay_scales(kp):
-            nc.vector.tensor_copy(
-                out=zs[:, kp].bitcast(I32).rearrange("p (g t q r) -> p g t q r", g=2, t=4, r=2),
-                in_=zs_raw[:, kp].bitcast(I32).rearrange("p (g q t r) -> p g t q r", g=2, t=4, r=2),
+        def z_lay_scales(kp, copy=on_vector):
+            word = U32 if copy is on_scalar else I32
+            copy(
+                out=zs[:, kp].bitcast(word).rearrange("p (g t q r) -> p g t q r", g=2, t=4, r=2),
+                in_=zs_raw[:, kp].bitcast(word).rearrange("p (g q t r) -> p g t q r", g=2, t=4, r=2),
             )
 
+        halves = {}
         x_cast, x_split, x_turned, x_laid, xq, xs = {}, {}, {}, {}, {}, {}
 
 
@@ -160,12 +163,21 @@ def tile_coupled_newton_colouring_step_s11_kernel(tc, x_bytes, x_scale, y, z_wor
             for s in range(ns):
                 x_cast[2 * pair + s0 + s] = wide[:, s]
 
+        def cast_half(i, kp, buffer):
+            halves[i, kp] = keep.tile([P, HALF], BF16, name=buffer, tag=buffer, align_bytes=64)
+            on_gpsimd(out=halves[i, kp][:], in_=x_raw[i // 2][:, i % 2, HALF * kp : HALF * (kp + 1)].bitcast(FP8))
+
+        def split_halves(i):
+            x_split[i] = work.tile([P, 2, 2 * P], F32, name="xp", tag="xp", bufs=6, align_bytes=64)
+            for kp in range(2):
+                on_scalar(out=x_split[i][:, :, P * kp : P * (kp + 1)], in_=halves[i, kp][:].bitcast(F32).rearrange("p (n u) -> p u n", u=2))
+
         def split(i, copy=on_scalar):
-            x_split[i] = work.tile([P, 2, 2 * P], F32, name="xp", tag="xp", bufs=4, align_bytes=64)
+            x_split[i] = work.tile([P, 2, 2 * P], F32, name="xp", tag="xp", bufs=6, align_bytes=64)
             copy(out=x_split[i][:], in_=x_cast[i].bitcast(F32).rearrange("p (n u) -> p u n", u=2))
 
         def cast_split(i):
-            x_split[i] = work.tile([P, 2, 2 * P], F32, name="xp", tag="xp", bufs=4, align_bytes=64)
+            x_split[i] = work.tile([P, 2, 2 * P], F32, name="xp", tag="xp", bufs=6, align_bytes=64)
             nc.vector.tensor_scalar(
                 out=x_split[i][:].bitcast(BF16).rearrange("p u (n e) -> p n u e", e=2),
                 in0=x_raw[i // 2][:, i % 2].bitcast(FP8).rearrange("p (n u e) -> p n u e", u=2, e=2),
@@ -401,7 +413,8 @@ def tile_coupled_newton_colouring_step_s11_kernel(tc, x_bytes, x_scale, y, z_wor
         z_lay_words(0, 1)
         zy_by_pass(0, 1, (0,), 0)
         y_quant(0, 0, 1, 1)
-        z_lay_words(0, 0)
+        z_lay_words(0, 0, on_scalar)
+        z_lay_scales(1, on_scalar)
         zy_by_pass(0, 1, (1,), 0)
         zy_by_pass(0, 0, (0, 1), 0)
         y_quant(0, 0, 2, 2)
@@ -414,7 +427,6 @@ def tile_coupled_newton_colouring_step_s11_kernel(tc, x_bytes, x_scale, y, z_wor
         turn(3)
 
         y_lay(1, 0, 0, 2, on_scalar)
-        z_lay_scales(1)
         z_lay_words(1, 1)
         y_quant(1, 0, 0, 1)
         zy_by_pass(0, 1, (0,), 1)
@@ -425,8 +437,8 @@ def tile_coupled_newton_colouring_step_s11_kernel(tc, x_bytes, x_scale, y, z_wor
         y_quant(1, 0, 1, 1)
         zy_by_pass(0, 1, (1,), 1)
         zy_by_pass(0, 0, (1,), 1)
-        x_quant(0)
         y_quant(1, 0, 2, 2)
+        x_quant(0)
         zy_by_pass(0, 1, (2, 3), 1)
 
         y_lay_gpsimd(0, 1, buffer="yi_101")
@@ -443,46 +455,51 @@ def tile_coupled_newton_colouring_step_s11_kernel(tc, x_bytes, x_scale, y, z_wor
         y_quant(0, 1, 0, 2)
         y_lay_gpsimd(1, 1, buffer="yi_010")
         c_out(0, 3)
-        v_mm(1, 0)
+        zy_by_pass(1, 0, (2, 3), 0)
+        v_out(0, 0, (0,))
         c_out_diagonal(0, 0)
+        v_out(0, 0, (1,))
+        v_mm(1, 0)
         c_out_diagonal(0, 1)
         y_lay(1, 1, 0, 2, on_scalar)
         c_out_diagonal(0, 2)
-        v_out(0, 0)
-        zy_by_pass(1, 0, (0, 1, 2, 3), 0)
+        zy_by_pass(1, 0, (0, 1), 0)
+        zy_by_pass(1, 1, (2,), 0)
         y_quant(1, 1, 2, 2)
         y_quant(1, 1, 0, 2)
         c_out_diagonal(0, 3)
-        zy_by_pass(1, 0, (2, 3, 0, 1), 1)
+        zy_by_pass(1, 0, (2, 3), 1)
+        zy_by_pass(1, 1, (2,), 1)
+        zy_by_pass(1, 0, (0, 1), 1)
         cast(3, 0, 1, on_scalar)
         v_out(1, 0)
-        zy(1, 1, (0, 1))
+        zy(1, 1, (3, 0))
         c_quant(0, 1)
         c_quant(0, 0)
         cast_split(4)
-        cast_split(5)
         scale_split(6, "ci_00")
         c_out(1, 2)
         c_out(1, 3)
-        zy(1, 1, (2, 3))
+        zy(1, 1, (1,))
         c_out(1, 0)
         c_out(1, 1)
-        cast(3, 1, 1, on_scalar)
-        c_out_diagonal(1, 0)
-        c_out_diagonal(1, 1)
-        v_mm(0, 1)
+        cast(2, 1, 1, on_scalar)
         c_out_diagonal(1, 2)
         c_out_diagonal(1, 3)
+        v_mm(0, 1)
+        c_out_diagonal(1, 0)
+        c_out_diagonal(1, 1)
         turn(4)
         turn(5)
         v_out(0, 1)
-        split(7)
+        cast(3, 1, 1, on_scalar)
         v_mm(1, 1)
         c_quant(1, 0)
         v_quant(0)
-        v_out(1, 1)
+        v_out(1, 1, (0,))
+        split(7)
+        v_out(1, 1, (1,))
         cast(4, 0, 1, on_scalar)
-        cast(5, 0, 1, on_scalar)
 
         def out_mm(pair):
             for i in (2 * pair, 2 * pair + 1):
@@ -505,10 +522,11 @@ def tile_coupled_newton_colouring_step_s11_kernel(tc, x_bytes, x_scale, y, z_wor
         x_quant(2, 0, 1)
         x_out(5)
         x_copy_out(6)
-        cast(4, 1, 1, on_scalar)
+        cast(5, 0, 1, on_scalar)
         v_quant(1)
         x_quant(2, 1, 1)
         scale_split(8, "xo0")
+        cast(4, 1, 1, on_scalar)
         v_mm(2, 0, (0,))
         o_out(0, 0)
         v_mm(2, 1, (0,))
@@ -517,8 +535,8 @@ def tile_coupled_newton_colouring_step_s11_kernel(tc, x_bytes, x_scale, y, z_wor
         o_out(1, HALF)
         v_mm(2, 0, (1,))
         v_mm(2, 1, (1,))
-        split(9)
         v_out(2, 0, (0,))
+        split(9)
         v_out(2, 1, (0,))
         v_out(2, 0, (1,))
         v_out(2, 1, (1,))
@@ -556,8 +574,8 @@ def tile_coupled_newton_colouring_step_s11_kernel(tc, x_bytes, x_scale, y, z_wor
         out_mm(3)
         x_quant(5)
         o_out(6, 0)
-        o_out(6, HALF)
         v_quant(4)
+        o_out(6, HALF)
         o_out(7, 0)
         o_out(7, HALF)
         for g in range(2):

@@ -55,7 +55,7 @@ def tile_coupled_newton_colouring_step_s11_kernel(tc, x_bytes, x_scale, y, z_wor
         y_raw, zw_raw, x_raw = {}, {}, {}
 
         def load_scale():
-            nc.sync.dma_start(out=scale_cols[:], in_=x_scale.rearrange("o (g p t) -> p (o g) t", p=P, t=4))
+            nc.gpsimd.dma_start(out=scale_cols[:], in_=x_scale.rearrange("o (g p t) -> p (o g) t", p=P, t=4))
 
         def load_scale_rows():
             nc.sync.dma_start(out=scale_rows[:], in_=x_scale.rearrange("o k -> (o k)").partition_broadcast(P))
@@ -384,7 +384,6 @@ def tile_coupled_newton_colouring_step_s11_kernel(tc, x_bytes, x_scale, y, z_wor
         load_z_scales()
         load_z_half(0, 1)
         load_z_half(0, 0)
-        load_scale()
         load_x(1)
         load_y(1, 0)
         load_z_half(1, 1)
@@ -398,12 +397,14 @@ def tile_coupled_newton_colouring_step_s11_kernel(tc, x_bytes, x_scale, y, z_wor
         for pair in (4, 5):
             load_x(pair)
         constants()
+        load_scale()
 
         cast(0, 0, 1, on_vector)
         cast(0, 1, 1, on_scalar)
         make_eye()
-        warm_up(2)
+        warm_up(3)
         turn(0)
+
         turn(1)
         warm_up(2)
         y_lay(0, 0, 0, 2, on_vector)

@@ -212,7 +212,10 @@ def tile_coupled_newton_colouring_step_s11_kernel(tc, x_bytes, x_scale, y, z_wor
             return x_laid[pair][:, :, s] if pair in WIDE else x_laid[pair][:, s]
 
         def x_copy_out(i):
-            nc.scalar.copy(out=x_dst(i).bitcast(F32), in_=x_turned[i][:].rearrange("p (u g) m -> p g m u", u=2))
+            nc.scalar.copy(
+                out=x_dst(i).bitcast(F32).rearrange("p g (m i) u -> p g m u i", i=2),
+                in_=x_turned[i][:].rearrange("p (u g) (m i) -> p g m u i", u=2, i=2),
+            )
             give_back(("x", i))
 
         def x_out(i):
@@ -268,18 +271,19 @@ def tile_coupled_newton_colouring_step_s11_kernel(tc, x_bytes, x_scale, y, z_wor
         def c_views(h, g, t1):
             if (g, h) not in c_laid:
                 c_laid[g, h] = keep.tile([P, HALF, 4], BF16, name=f"ci_{g}{h}", tag=f"ci_{g}{h}", align_bytes=64)
-            dst = c_laid[g, h][:].rearrange("p (q t r) f -> p t q r f", t=4, r=8)[:, t1]
-            return dst, zy_banks[h, g, t1][:].rearrange("p f (q r) -> p q r f", r=8)
+            return c_laid[g, h][:, P * t1 : P * (t1 + 1)], zy_banks[h, g, t1][:].rearrange("p f c -> p c f")
+
+        def in_pairs(view):
+            return view.rearrange("p (c i) f -> p c f i", i=2)
 
         def c_out(h, t1):
             dst, src = c_views(h, 1 - h, t1)
-            nc.scalar.activation(out=dst, in_=src, func=COPY, scale=-0.5)
+            nc.scalar.activation(out=in_pairs(dst), in_=in_pairs(src), func=COPY, scale=-0.5)
             give_back(("c", h, 1 - h, t1))
 
         def c_out_diagonal(h, t1):
             dst, src = c_views(h, h, t1)
-            eye = eye15[:, :, 3 - t1 : 7 - t1].rearrange("p (q r) f -> p q r f", r=8)
-            nc.vector.scalar_tensor_tensor(out=dst, in0=src, scalar=-0.5, in1=eye, op0=MULT, op1=ADD)
+            nc.vector.scalar_tensor_tensor(out=dst, in0=src, scalar=-0.5, in1=eye15[:, :, 3 - t1 : 7 - t1], op0=MULT, op1=ADD)
             give_back(("c", h, h, t1))
 
         def c_quant(h, g):
@@ -320,7 +324,7 @@ def tile_coupled_newton_colouring_step_s11_kernel(tc, x_bytes, x_scale, y, z_wor
                 if pair in WIDE:
                     nc.scalar.copy(out=v_laid[pair][:, :, g, :, 2 * b : 2 * b + 2], in_=v_banks[pair, g, b][:].rearrange("p (t a) m -> p a m t", t=2))
                 else:
-                    nc.scalar.copy(out=v_laid[pair][:, b, g], in_=v_banks[pair, g, b][:].rearrange("p t m -> p m t"))
+                    nc.scalar.copy(out=in_pairs(v_laid[pair][:, b, g]), in_=in_pairs(v_banks[pair, g, b][:].rearrange("p t m -> p m t")))
                 give_back(("v", pair, g, b))
 
         def v_quant(pair, j0=0, nj=4):
@@ -353,7 +357,12 @@ def tile_coupled_newton_colouring_step_s11_kernel(tc, x_bytes, x_scale, y, z_wor
 
         def o_out(i, c0, width=HALF):
             result = work.tile([P, HALF], F32, name="ot", tag="ot", bufs=8, align_bytes=64)
-            nc.vector.tensor_tensor(out=result[:, 0:width], in0=o_banks[i, c0][:, 0:width], in1=gain_rows[:, c0 : c0 + width], op=MULT)
+            nc.vector.tensor_tensor(
+                out=result[:].rearrange("p (q t r) -> p q t r", t=4, r=8),
+                in0=o_banks[i, c0].rearrange("p (t q r) -> p q t r", t=4, r=8),
+                in1=gain_rows[:, c0 : c0 + width].rearrange("p (q t r) -> p q t r", t=4, r=8),
+                op=MULT,
+            )
             give_back(("o", i, c0))
             nc.sync.dma_start(out=out_view[i // 2][i % 2][:, c0 : c0 + width], in_=result[:, 0:width])
 
@@ -404,7 +413,6 @@ def tile_coupled_newton_colouring_step_s11_kernel(tc, x_bytes, x_scale, y, z_wor
         make_eye()
         warm_up(3)
         turn(0)
-
         turn(1)
         warm_up(2)
         y_lay(0, 0, 0, 2, on_vector)
@@ -420,12 +428,13 @@ def tile_coupled_newton_colouring_step_s11_kernel(tc, x_bytes, x_scale, y, z_wor
         zy_by_pass(0, 0, (0, 1), 0)
         y_quant(0, 0, 2, 2)
         cast(1, 1, 1, on_gpsimd, buffer="yi_001")
-        zy_by_pass(0, 1, (2, 3), 0)
-        x_out(0)
+        zy_by_pass(0, 1, (2,), 0)
         cast(1, 0, 1, on_scalar)
-        x_out(1)
         turn(2)
+        x_out(0)
         turn(3)
+        x_out(1)
+        zy_by_pass(0, 1, (3,), 0)
 
         y_lay(1, 0, 0, 2, on_scalar)
         z_lay_words(1, 1)
@@ -597,5 +606,4 @@ def tile_coupled_newton_colouring_step_s11_kernel(tc, x_bytes, x_scale, y, z_wor
         o_part(10, 0)
         o_part(10, HALF)
         o_part(11, 0)
-        o_part(11, HALF, HALF // 2)
-        o_part(11, HALF + HALF // 2, HALF // 2)
+        o_part(11, HALF)

@@ -447,8 +447,9 @@ def tile_coupled_newton_colouring_step_s11_kernel(tc, x_bytes, x_scale, y, z_wor
         y_quant(1, 0, 1, 1)
         zy_by_pass(0, 1, (1,), 1)
         zy_by_pass(0, 0, (1,), 1)
+        x_quant(0, 0, 1)
         y_quant(1, 0, 2, 2)
-        x_quant(0)
+        x_quant(0, 1, 1)
         zy_by_pass(0, 1, (2, 3), 1)
 
         y_lay_gpsimd(0, 1, buffer="yi_101")
@@ -456,10 +457,11 @@ def tile_coupled_newton_colouring_step_s11_kernel(tc, x_bytes, x_scale, y, z_wor
         c_out(0, 1)
         zy(0, 0, (2, 3))
         x_out(2)
-        y_lay(0, 1, 0, 2, on_scalar)
-        x_out(3)
-        v_mm(0, 0)
+        y_lay(0, 1, 0, 1, on_scalar)
         c_out(0, 2)
+        v_mm(0, 0)
+        x_out(3)
+        y_lay(0, 1, 1, 1, on_scalar)
         y_quant(0, 1, 2, 2)
         x_quant(1)
         y_quant(0, 1, 0, 2)
@@ -475,25 +477,27 @@ def tile_coupled_newton_colouring_step_s11_kernel(tc, x_bytes, x_scale, y, z_wor
         c_out_diagonal(0, 2)
         zy_by_pass(1, 0, (0, 1), 0)
         zy_by_pass(1, 1, (2,), 0)
+        c_out_diagonal(0, 3)
+        zy_by_pass(1, 1, (3,), 0)
         y_quant(1, 1, 2, 2)
         y_quant(1, 1, 0, 2)
-        c_out_diagonal(0, 3)
         zy_by_pass(1, 0, (2, 3), 1)
-        zy_by_pass(1, 1, (2,), 1)
+        zy_by_pass(1, 1, (2, 3), 1)
         zy_by_pass(1, 0, (0, 1), 1)
+        cast(2, 1, 1, on_scalar)
         cast(3, 0, 1, on_scalar)
         v_out(1, 0)
-        zy(1, 1, (3, 0))
+        zy(1, 1, (0,))
         c_quant(0, 1)
         c_quant(0, 0)
         cast_split(4)
+        split(5, on_vector)
         scale_split(6, "ci_00")
         c_out(1, 2)
         c_out(1, 3)
         zy(1, 1, (1,))
         c_out(1, 0)
         c_out(1, 1)
-        cast(2, 1, 1, on_scalar)
         c_out_diagonal(1, 2)
         c_out_diagonal(1, 3)
         v_mm(0, 1)

from contextlib import ExitStack

import concourse.mybir as mybir
from concourse.masks import make_identity

M, N = 1536, 1024
FLOPS = 2 * N * N * (2 * M + N)

F32 = mybir.dt.float32
BF16 = mybir.dt.bfloat16
I32 = mybir.dt.int32
U32 = mybir.dt.uint32
U8 = mybir.dt.uint8
FP8 = mybir.dt.float8_e4m3fn
FP8X4 = mybir.dt.float8_e4m3fn_x4
FP4X4 = mybir.dt.float4_e2m1fn_x4
MULT = mybir.AluOpType.mult
ADD = mybir.AluOpType.add
COPY = mybir.ActivationFunctionType.Copy

P = 128
HALF = 512
BANKS = 8
KEPT = 256
WIDE = (3, 4)
WARM_UPS = 5


def tile_coupled_newton_colouring_step_s11_kernel(tc, x_bytes, x_scale, y, z_words, z_scales, gain, out):
    nc = tc.nc
    with ExitStack() as ctx:
        keep = ctx.enter_context(tc.tile_pool(name="keep", bufs=1))
        work = ctx.enter_context(tc.tile_pool(name="work", bufs=3))
        psum = ctx.enter_context(tc.psum_pool(name="psum", bufs=1))
        ctx.enter_context(tc.manual_schedule())
        on_vector, on_scalar, on_gpsimd = nc.vector.tensor_copy, nc.scalar.copy, nc.gpsimd.tensor_copy

        free_banks = list(range(BANKS))
        taken = {}

        def bank(key):
            taken[key] = free_banks.pop(0)
            return psum.tile([P, 4, P], F32, name=f"bank{taken[key]}", tag=f"bank{taken[key]}", bufs=1)

        def give_back(key):
            free_banks.append(taken[key])

        scale_cols = keep.tile([P, 2, 4], F32, name="xs4")
        zs_raw = keep.tile([P, 2, N], U8, name="zs_raw", align_bytes=64)
        scale_rows = keep.tile([P, N], F32, name="xs_bc", align_bytes=64)
        gain_rows = keep.tile([P, N], BF16, name="gain_bc", align_bytes=64)
        y_view = y.rearrange("(g p j) n -> g p j n", p=P, j=4)
        x_view = x_bytes.rearrange("(i p s) k -> i p s k", s=2, p=P)
        out_view = out.rearrange("(i p s) n -> i s p n", s=2, p=P)
        y_raw, zw_raw, x_raw = {}, {}, {}

        def load_scale():
            nc.gpsimd.dma_start(out=scale_cols[:], in_=x_scale.rearrange("o (g p t) -> p (o g) t", p=P, t=4))

        def load_scale_rows():
            nc.sync.dma_start(out=scale_rows[:], in_=x_scale.rearrange("o k -> (o k)").partition_broadcast(P))

        def load_z_scales():
            rows = z_scales.bitcast(I32).rearrange("g q n -> q g n")
            for quad in range(4):
                nc.sync.dma_start(out=zs_raw[quad:P:32].bitcast(I32), in_=rows[quad:16:4])

        def load_y(kp, h):
            y_raw[kp, h] = keep.tile([P, 4, HALF], BF16, name=f"y_raw_{kp}{h}", align_bytes=64)
            nc.sync.dma_start(out=y_raw[kp, h][:], in_=y_view[kp][:, :, HALF * h : HALF * (h + 1)])

        def load_z_words(kp):
            both = keep.tile([P, 2, N], U8, name=f"zw_raw_{kp}", align_bytes=64)
            nc.sync.dma_start(out=both[:].rearrange("p g n -> p (g n)").bitcast(I32), in_=z_words[kp].bitcast(I32))
            zw_raw[kp, 0], zw_raw[kp, 1] = both[:, 0], both[:, 1]

        def load_z_half(kp, g):
            zw_raw[kp, g] = keep.tile([P, N], U8, name=f"zw_raw_{kp}{g}", align_bytes=64)
            nc.sync.dma_start(out=zw_raw[kp, g][:].bitcast(I32), in_=z_words[kp][:, N * g : N * (g + 1)].bitcast(I32))

        def load_x(pair):
            x_raw[pair] = keep.tile([P, 2, N], U8, name=f"xb2_{pair}", align_bytes=64)
            nc.sync.dma_start(out=x_raw[pair][:], in_=x_view[pair])

        def load_gain():
            nc.sync.dma_start(out=gain_rows[:], in_=gain.partition_broadcast(P))

        ident = keep.tile([P, P], F32, name="ident", align_bytes=64)
        eye15 = keep.tile([P, P, 8], BF16, name="eye15", align_bytes=64)

        ones = keep.tile([P, 1], F32, name="ones", align_bytes=64)

        def constants():
            make_identity(nc, ident[:])
            nc.vector.memset(ones[:], 1.0)

        def make_eye():
            nc.vector.tensor_scalar(out=eye15[:, :, 3], in0=ident[:], scalar1=1.5, scalar2=None, op0=MULT)

        def warm_up(count):
            unread = bank("warm")
            for j in range(count):
                nc.tensor.matmul(unread[:, j % 4, :], lhsT=ident[:], rhs=ident[:], start=True, stop=True)
            give_back("warm")

        yq = keep.tile([P, 2, N], U32, name="yq", align_bytes=256)
        ys = keep.tile([P, 2, N], U8, name="ys", align_bytes=256)
        zq = keep.tile([P, 2, 2 * N], U8, name="zq", align_bytes=256)
        zs = keep.tile([P, 2, N], U8, name="zs", align_bytes=256)
        cq = keep.tile([P, 2, N], U32, name="cq", align_bytes=256)
        cs = keep.tile([P, 2, N], U8, name="cs", align_bytes=256)
        y_laid, c_laid = {}, {}

        def y_views(kp, h, t0, buffer):
            if (kp, h, t0 // 2) not in y_laid:
                y_laid[kp, h, t0 // 2] = keep.tile([P, 2 * P, 4], BF16, name=buffer, tag=buffer, align_bytes=64)
            laid = y_laid[kp, h, t0 // 2][:].rearrange("p (t q r) j -> p q t r j", t=2, r=8)
            return laid, y_raw[kp, h][:].rearrange("p j (q t r) -> p q t r j", t=4, r=8)

        def y_lay(kp, h, t0, nt, copy):
            laid, raw = y_views(kp, h, t0, f"yi_{kp}{h}{t0 // 2}")
            for t in range(t0, t0 + nt):
                copy(
                    out=laid[:, :, t % 2].rearrange("p q (a i) j -> p q a j i", i=4),
                    in_=raw[:, :, t].rearrange("p q (a i) j -> p q a j i", i=4),
                )

        def y_lay_gpsimd(kp, h, buffer):
            laid, raw = y_views(kp, h, 2, buffer)
            nc.gpsimd.tensor_scalar(out=laid[:, :, 0:2], in0=raw[:, :, 2:4], scalar1=1.0, scalar2=0.0, op0=MULT, op1=ADD)

        def y_quant(kp, h, t0, nt):
            lo = P * (t0 % 2)
            cols = slice(HALF * h + P * t0, HALF * h + P * (t0 + nt))
            nc.vector.quantize_mx(
                out=yq[:, kp, cols].bitcast(FP8X4),
                scales=ys[:, kp, cols],
                in_=y_laid[kp, h, t0 // 2][:, lo : lo + P * nt].rearrange("p n j -> p (n j)"),
            )

        def z_lay_words(kp, g, copy=on_vector):
            word = U32 if copy is on_scalar else I32
            copy(
                out=zq[:, kp, N * g : N * (g + 1)].bitcast(word).rearrange("p (t q r) -> p t q r", t=4, r=4),
                in_=zw_raw[kp, g][:].bitcast(word).rearrange("p (q t r) -> p t q r", t=4, r=4),
            )

        def z_lay_scales(kp, copy=on_vector):
            word = U32 if copy is on_scalar else I32
            copy(
                out=zs[:, kp].bitcast(word).rearrange("p (g t q r) -> p g t q r", g=2, t=4, r=2),
                in_=zs_raw[:, kp].bitcast(word).rearrange("p (g q t r) -> p g t q r", g=2, t=4, r=2),
            )

        halves = {}
        x_cast, x_split, x_turned, x_laid, xq, xs = {}, {}, {}, {}, {}, {}


        def cast(pair, s0, ns, copy, buffer=None):
            buffer = buffer or f"xc{pair}{s0}"
            wide = keep.tile([P, ns, N], BF16, name=buffer, tag=buffer, align_bytes=64)
            copy(out=wide[:].rearrange("p s k -> p (s k)"), in_=x_raw[pair][:, s0 : s0 + ns].rearrange("p s k -> p (s k)").bitcast(FP8))
            for s in range(ns):
                x_cast[2 * pair + s0 + s] = wide[:, s]

        def cast_half(i, kp, buffer):
            halves[i, kp] = keep.tile([P, HALF], BF16, name=buffer, tag=buffer, align_bytes=64)
            on_gpsimd(out=halves[i, kp][:], in_=x_raw[i // 2][:, i % 2, HALF * kp : HALF * (kp + 1)].bitcast(FP8))

        def split_halves(i):
            x_split[i] = work.tile([P, 2, 2 * P], F32, name="xp", tag="xp", bufs=6, align_bytes=64)
            for kp in range(2):
                on_scalar(out=x_split[i][:, :, P * kp : P * (kp + 1)], in_=halves[i, kp][:].bitcast(F32).rearrange("p (n u) -> p u n", u=2))

        def split(i, copy=on_scalar):
            x_split[i] = work.tile([P, 2, 2 * P], F32, name="xp", tag="xp", bufs=6, align_bytes=64)
            copy(out=x_split[i][:], in_=x_cast[i].bitcast(F32).rearrange("p (n u) -> p u n", u=2))

        def cast_split(i):
            x_split[i] = work.tile([P, 2, 2 * P], F32, name="xp", tag="xp", bufs=6, align_bytes=64)
            nc.vector.tensor_scalar(
                out=x_split[i][:].bitcast(BF16).rearrange("p u (n e) -> p n u e", e=2),
                in0=x_raw[i // 2][:, i % 2].bitcast(FP8).rearrange("p (n u e) -> p n u e", u=2, e=2),
                scalar1=ones[:],
                scalar2=None,
                op0=MULT,
            )

        def scale_split(i, buffer):
            x_split[i] = keep.tile([P, 2, 2 * P], F32, name=buffer, tag=buffer, align_bytes=64)
            nc.gpsimd.tensor_tensor(
                out=x_split[i][:].bitcast(BF16).rearrange("p u (n e) -> p u n e", e=2),
                in0=x_cast[i].rearrange("p (n u e) -> p u n e", u=2, e=2),
                in1=scale_rows[:].rearrange("p (n u e) -> p u n e", u=2, e=2),
                op=MULT,
            )

        def turn(i):
            x_turned[i] = bank(("x", i))
            for kp in range(2):
                for u in range(2):
                    if i in x_split:
                        words = x_split[i][:, u, P * kp : P * (kp + 1)]
                    else:
                        words = x_cast[i].bitcast(F32)[:, 2 * P * kp + u : 2 * P * (kp + 1) : 2]
                    nc.tensor.transpose(x_turned[i][:, 2 * u + kp, :], words, ident[:])

        def x_dst(i):
            pair, s = divmod(i, 2)
            if pair not in x_laid:
                x_laid[pair] = keep.tile([P, 2, 2, P, 4], BF16, name=f"xo{pair % 2}", tag=f"xo{pair % 2}", align_bytes=64)
            return x_laid[pair][:, :, s] if pair in WIDE else x_laid[pair][:, s]

        def x_copy_out(i):
            nc.scalar.copy(
                out=x_dst(i).bitcast(F32).rearrange("p g (m i) u -> p g m u i", i=2),
                in_=x_turned[i][:].rearrange("p (u g) (m i) -> p g m u i", u=2, i=2),
            )
            give_back(("x", i))

        def x_out(i):
            dst = x_dst(i)
            nc.vector.tensor_tensor(
                out=dst.rearrange("p g m (u e) -> p g m u e", u=2),
                in0=x_turned[i][:].rearrange("p a m -> p (a m)").bitcast(BF16).rearrange("p (u g m e) -> p g m u e", u=2, g=2, e=2),
                in1=scale_cols[:].rearrange("p g (u e) -> p g u e", u=2).unsqueeze(2).to_broadcast([P, 2, P, 2, 2]),
                op=MULT,
            )
            give_back(("x", i))

        def x_quant(pair, s0=0, ns=2):
            if pair not in xq:
                xq[pair] = work.tile([P, 4 * P], U32, name="xq", tag="xq", bufs=3, align_bytes=256)
                xs[pair] = work.tile([P, 4 * P], U8, name="xqs", tag="xqs", bufs=3, align_bytes=256)
            cols = slice(2 * P * s0, 2 * P * (s0 + ns))
            nc.vector.quantize_mx(
                out=xq[pair][:, cols].bitcast(FP8X4), scales=xs[pair][:, cols], in_=x_laid[pair][:, s0 : s0 + ns].rearrange("p s g m t -> p (s g m t)")
            )

        zy_banks = {}

        def zy_pass(h, g, t1, t, kp, start, stop):
            cols = slice(HALF * h + P * t1, HALF * h + P * (t1 + 1))
            c0 = HALF * g + P * t
            nc.tensor.matmul_mx(
                out=zy_banks[h, g, t1][:, t, :],
                lhsT=zq[:, kp, 2 * c0 : 2 * (c0 + P)].bitcast(FP4X4),
                lhsT_scale=zs[:, kp, c0 : c0 + P],
                rhs=yq[:, kp, cols].bitcast(FP8X4),
                rhs_scale=ys[:, kp, cols],
                start=start,
                stop=stop,
            )

        def zy(h, g, t1s):
            for t1 in t1s:
                zy_banks[h, g, t1] = bank(("c", h, g, t1))
            for t1 in t1s:
                for t in range(4):
                    for kp in range(2):
                        zy_pass(h, g, t1, t, kp, kp == 0, kp == 1)

        def zy_by_pass(h, g, t1s, kp):
            if kp == 0:
                for t1 in t1s:
                    zy_banks[h, g, t1] = bank(("c", h, g, t1))
            for t1 in t1s:
                for t in range(4):
                    zy_pass(h, g, t1, t, kp, kp == 0 and t == 0, kp == 1 and t == 3)

        def c_views(h, g, t1):
            if (g, h) not in c_laid:
                c_laid[g, h] = keep.tile([P, HALF, 4], BF16, name=f"ci_{g}{h}", tag=f"ci_{g}{h}", align_bytes=64)
            return c_laid[g, h][:, P * t1 : P * (t1 + 1)], zy_banks[h, g, t1][:].rearrange("p f c -> p c f")

        def in_pairs(view):
            return view.rearrange("p (c i) f -> p c f i", i=2)

        def c_out(h, t1):
            dst, src = c_views(h, 1 - h, t1)
            nc.scalar.activation(out=in_pairs(dst), in_=in_pairs(src), func=COPY, scale=-0.5)
            give_back(("c", h, 1 - h, t1))

        def c_out_diagonal(h, t1):
            dst, src = c_views(h, h, t1)
            nc.vector.scalar_tensor_tensor(out=dst, in0=src, scalar=-0.5, in1=eye15[:, :, 3 - t1 : 7 - t1], op0=MULT, op1=ADD)
            give_back(("c", h, h, t1))

        def c_quant(h, g):
            cols = slice(HALF * h, HALF * (h + 1))
            nc.vector.quantize_mx(out=cq[:, g, cols].bitcast(FP8X4), scales=cs[:, g, cols], in_=c_laid[g, h][:].rearrange("p n f -> p (n f)"))

        v_banks, v_laid, vq, vs = {}, {}, {}, {}

        def v_sum(acc, pair, g, t, first_col, width):
            c0 = HALF * g + P * t
            for kp in range(2):
                cols = slice(first_col + width * kp, first_col + width * (kp + 1))
                nc.tensor.matmul_mx(
                    out=acc,
                    lhsT=yq[:, kp, c0 : c0 + P].bitcast(FP8X4),
                    lhsT_scale=ys[:, kp, c0 : c0 + P],
                    rhs=xq[pair][:, cols].bitcast(FP8X4),
                    rhs_scale=xs[pair][:, cols],
                    start=(kp == 0),
                    stop=(kp == 1),
                )

        def v_mm(pair, g, banks=(0, 1)):
            for b in banks:
                v_banks[pair, g, b] = bank(("v", pair, g, b))
                if pair in WIDE:
                    acc = v_banks[pair, g, b][:].rearrange("p (t a) m -> p t (a m)", t=2)
                    for t in range(2):
                        v_sum(acc[:, t, :], pair, g, 2 * b + t, 0, 2 * P)
                else:
                    for t in range(4):
                        v_sum(v_banks[pair, g, b][:, t, :], pair, g, t, 2 * P * b, P)

        def v_out(pair, g, banks=(0, 1)):
            if pair not in v_laid:
                v_laid[pair] = keep.tile([P, 2, 2, P, 4], BF16, name=f"vx{pair % 4}", tag=f"vx{pair % 4}", align_bytes=64)
            for b in banks:
                if pair in WIDE:
                    nc.scalar.copy(out=v_laid[pair][:, :, g, :, 2 * b : 2 * b + 2], in_=v_banks[pair, g, b][:].rearrange("p (t a) m -> p a m t", t=2))
                else:
                    nc.scalar.copy(out=in_pairs(v_laid[pair][:, b, g]), in_=in_pairs(v_banks[pair, g, b][:].rearrange("p t m -> p m t")))
                give_back(("v", pair, g, b))

        def v_quant(pair, j0=0, nj=4):
            if pair not in vq:
                vq[pair] = work.tile([P, 4 * P], U32, name="vq", tag="vq", bufs=3, align_bytes=256)
                vs[pair] = work.tile([P, 4 * P], U8, name="vqs", tag="vqs", bufs=3, align_bytes=256)
            cols = slice(P * j0, P * (j0 + nj))
            nc.vector.quantize_mx(
                out=vq[pair][:, cols].bitcast(FP8X4),
                scales=vs[pair][:, cols],
                in_=v_laid[pair][:].rearrange("p s g m t -> p (s g m t)")[:, 4 * P * j0 : 4 * P * (j0 + nj)],
            )

        o_banks, staged, scaled = {}, {}, {}

        def o_mm(i, c0, width=HALF):
            o_banks[i, c0] = bank(("o", i, c0))[:].rearrange("p a b -> p (a b)")[:, 0:width]
            cols = slice(c0, c0 + width)
            for g in range(2):
                rows = slice(P * (2 * (i % 2) + g), P * (2 * (i % 2) + g + 1))
                nc.tensor.matmul_mx(
                    out=o_banks[i, c0],
                    lhsT=vq[i // 2][:, rows].bitcast(FP8X4),
                    lhsT_scale=vs[i // 2][:, rows],
                    rhs=cq[:, g, cols].bitcast(FP8X4),
                    rhs_scale=cs[:, g, cols],
                    start=(g == 0),
                    stop=(g == 1),
                )

        def o_out(i, c0, width=HALF):
            result = work.tile([P, HALF], F32, name="ot", tag="ot", bufs=8, align_bytes=64)
            nc.vector.tensor_tensor(
                out=result[:].rearrange("p (q t r) -> p q t r", t=4, r=8),
                in0=o_banks[i, c0].rearrange("p (t q r) -> p q t r", t=4, r=8),
                in1=gain_rows[:, c0 : c0 + width].rearrange("p (q t r) -> p q t r", t=4, r=8),
                op=MULT,
            )
            give_back(("o", i, c0))
            nc.sync.dma_start(out=out_view[i // 2][i % 2][:, c0 : c0 + width], in_=result[:, 0:width])

        def o_part(i, c0, width=HALF):
            o_mm(i, c0, width)
            o_out(i, c0, width)

        def o_stage(i, c0):
            if c0 == HALF:
                staged[i] = work.tile([P, HALF], F32, name="stage", tag="stage", bufs=2, align_bytes=64)
            else:
                staged[i] = work.tile([P, N - c0], F32, name="stage2", tag="stage2", bufs=2, align_bytes=64)
                nc.scalar.copy(out=staged[i][:, 0 : HALF - c0], in_=o_banks[i, 0][:, c0:HALF])
            nc.scalar.copy(out=staged[i][:, HALF - c0 :], in_=o_banks[i, HALF])
            give_back(("o", i, HALF))

        def o_gain_gpsimd(i, c0, buffer):
            scaled[i] = keep.tile([P, N - c0], F32, name=buffer, tag=buffer, align_bytes=64)
            nc.gpsimd.tensor_tensor(out=scaled[i][:], in0=staged[i][:], in1=gain_rows[:, c0:], op=MULT)

        def o_store_gpsimd(i, c0):
            nc.sync.dma_start(out=out_view[i // 2][i % 2][:, c0:], in_=scaled[i][:])

        nc.vector.memset(zs_raw[:].rearrange("p g n -> p (g n)").bitcast(I32), 0)
        nc.vector.memset(eye15[:].rearrange("p n c -> p (n c)").bitcast(I32), 0)
        load_x(0)
        load_y(0, 0)
        load_z_scales()
        load_z_half(0, 1)
        load_z_half(0, 0)
        load_x(1)
        load_y(1, 0)
        load_z_half(1, 1)
        load_z_half(1, 0)
        load_y(0, 1)
        load_y(1, 1)
        load_x(2)
        load_x(3)
        load_scale_rows()
        load_gain()
        for pair in (4, 5):
            load_x(pair)
        constants()
        load_scale()

        cast(0, 0, 1, on_vector)
        cast(0, 1, 1, on_scalar)
        make_eye()
        warm_up(3)
        turn(0)
        turn(1)
        warm_up(2)
        y_lay(0, 0, 0, 2, on_vector)
        y_lay(0, 0, 2, 2, on_scalar)
        y_quant(0, 0, 0, 1)
        z_lay_scales(0)
        z_lay_words(0, 1)
        zy_by_pass(0, 1, (0,), 0)
        y_quant(0, 0, 1, 1)
        z_lay_words(0, 0, on_scalar)
        z_lay_scales(1, on_scalar)
        zy_by_pass(0, 1, (1,), 0)
        zy_by_pass(0, 0, (0, 1), 0)
        y_quant(0, 0, 2, 2)
        cast(1, 1, 1, on_gpsimd, buffer="yi_001")
        zy_by_pass(0, 1, (2,), 0)
        cast(1, 0, 1, on_scalar)
        turn(2)
        x_out(0)
        turn(3)
        x_out(1)
        zy_by_pass(0, 1, (3,), 0)

        y_lay(1, 0, 0, 2, on_scalar)
        z_lay_words(1, 1)
        y_quant(1, 0, 0, 1)
        zy_by_pass(0, 1, (0,), 1)
        z_lay_words(1, 0)
        zy_by_pass(0, 0, (0,), 1)
        y_lay(1, 0, 2, 1, on_vector)
        y_lay(1, 0, 3, 1, on_scalar)
        y_quant(1, 0, 1, 1)
        zy_by_pass(0, 1, (1,), 1)
        zy_by_pass(0, 0, (1,), 1)
        x_quant(0, 0, 1)
        y_quant(1, 0, 2, 2)
        x_quant(0, 1, 1)
        zy_by_pass(0, 1, (2, 3), 1)

        y_lay_gpsimd(0, 1, buffer="yi_101")
        c_out(0, 0)
        c_out(0, 1)
        zy(0, 0, (2, 3))
        x_out(2)
        y_lay(0, 1, 0, 1, on_scalar)
        c_out(0, 2)
        v_mm(0, 0)
        x_out(3)
        y_lay(0, 1, 1, 1, on_scalar)
        y_quant(0, 1, 2, 2)
        x_quant(1)
        y_quant(0, 1, 0, 2)
        y_lay_gpsimd(1, 1, buffer="yi_010")
        c_out(0, 3)
        zy_by_pass(1, 0, (2, 3), 0)
        v_out(0, 0, (0,))
        c_out_diagonal(0, 0)
        v_out(0, 0, (1,))
        v_mm(1, 0)
        c_out_diagonal(0, 1)
        y_lay(1, 1, 0, 2, on_scalar)
        c_out_diagonal(0, 2)
        zy_by_pass(1, 0, (0, 1), 0)
        zy_by_pass(1, 1, (2,), 0)
        c_out_diagonal(0, 3)
        zy_by_pass(1, 1, (3,), 0)
        y_quant(1, 1, 2, 2)
        y_quant(1, 1, 0, 2)
        zy_by_pass(1, 0, (2, 3), 1)
        zy_by_pass(1, 1, (2, 3), 1)
        zy_by_pass(1, 0, (0, 1), 1)
        cast(2, 1, 1, on_scalar)
        cast(3, 0, 1, on_scalar)
        v_out(1, 0)
        zy(1, 1, (0,))
        c_quant(0, 1)
        c_quant(0, 0)
        cast_split(4)
        split(5, on_vector)
        scale_split(6, "ci_00")
        c_out(1, 2)
        c_out(1, 3)
        zy(1, 1, (1,))
        c_out(1, 0)
        c_out(1, 1)
        c_out_diagonal(1, 2)
        c_out_diagonal(1, 3)
        v_mm(0, 1)
        c_out_diagonal(1, 0)
        c_out_diagonal(1, 1)
        turn(4)
        turn(5)
        v_out(0, 1)
        cast(3, 1, 1, on_scalar)
        v_mm(1, 1)
        c_quant(1, 0)
        v_quant(0)
        v_out(1, 1, (0,))
        split(7)
        v_out(1, 1, (1,))
        cast(4, 0, 1, on_scalar)

        def out_mm(pair):
            for i in (2 * pair, 2 * pair + 1):
                o_mm(i, 0)
                o_mm(i, HALF)

        def out_out(pair):
            for i in (2 * pair, 2 * pair + 1):
                o_out(i, 0)
                o_out(i, HALF)

        o_mm(0, 0)
        o_mm(1, 0)
        x_out(4)
        c_quant(1, 1)
        turn(6)
        turn(7)
        o_mm(0, HALF)
        o_mm(1, HALF)
        x_quant(2, 0, 1)
        x_out(5)
        x_copy_out(6)
        cast(5, 0, 1, on_scalar)
        v_quant(1)
        x_quant(2, 1, 1)
        scale_split(8, "xo0")
        cast(4, 1, 1, on_scalar)
        v_mm(2, 0, (0,))
        o_out(0, 0)
        v_mm(2, 1, (0,))
        o_out(1, 0)
        o_out(0, HALF)
        o_out(1, HALF)
        v_mm(2, 0, (1,))
        v_mm(2, 1, (1,))
        v_out(2, 0, (0,))
        split(9)
        v_out(2, 1, (0,))
        v_out(2, 0, (1,))
        v_out(2, 1, (1,))
        x_out(7)
        out_mm(1)
        cast(5, 1, 1, on_scalar)
        x_quant(3)
        v_quant(2)
        scale_split(10, "vx2")
        turn(9)
        turn(8)
        out_out(1)
        x_copy_out(8)
        v_mm(3, 0)
        x_out(9)
        split(11)
        v_out(3, 0)
        v_mm(3, 1)
        v_out(3, 1)
        out_mm(2)
        o_out(4, 0)
        x_quant(4)
        o_out(4, HALF)
        o_out(5, 0)
        o_out(5, HALF)
        turn(11)
        turn(10)
        v_mm(4, 0)
        v_quant(3)
        x_out(11)
        x_copy_out(10)
        v_out(4, 0)
        v_mm(4, 1)
        v_out(4, 1)
        out_mm(3)
        x_quant(5)
        o_out(6, 0)
        v_quant(4)
        o_out(6, HALF)
        o_out(7, 0)
        o_out(7, HALF)
        for g in range(2):
            v_mm(5, g, (0,))
        for g in range(2):
            v_out(5, g, (0,))
        o_part(8, 0)
        o_part(8, HALF)
        v_quant(5, 0, 2)
        o_part(9, 0)
        for g in range(2):
            v_mm(5, g, (1,))
        for g in range(2):
            v_out(5, g, (1,))
        v_quant(5, 2, 1)
        o_part(9, HALF)
        v_quant(5, 3, 1)
        o_part(10, 0)
        o_part(10, HALF)
        o_part(11, 0)
        o_part(11, HALF)
